import numpy as np, ml_dtypes
CORES = [5,29,101,125,133,157,229,253]
N = 8
import mx_ref
BF = ml_dtypes.bfloat16
def gentries(a):
    return np.ascontiguousarray(a.reshape(8, 16, -1).transpose(0, 2, 1)).reshape(8, -1)
def gtable(e):
    e = np.asarray(e); return np.ascontiguousarray(e.reshape(8, -1, 16).transpose(0, 2, 1)).reshape(128, -1).astype(np.int32)
def gcols(t, e):
    v = np.concatenate([t.reshape(8, 16, -1, 4), np.zeros((8, 16, 1, 4), BF)], axis=2)
    return np.ascontiguousarray(np.stack([v[g][:, e[g]] for g in range(8)])).reshape(128, -1)
def tile(rs):
    return np.stack(rs, axis=2).reshape(128, -1).astype(BF)
def cut(t, i, w=512):
    return t[:, w * i:w * i + w]
def pick(q, e):
    c = np.concatenate([q[0].reshape(128, -1, 4), np.zeros((128, 1, 4), np.uint8)], axis=1); s = np.concatenate([q[1], np.ones((16, 1), np.uint8)], axis=1)
    return (np.ascontiguousarray(c[:, e].reshape(128, -1)), np.ascontiguousarray(s[:, e]))
def join(*qs):
    return (np.concatenate([q[0] for q in qs], axis=1), np.concatenate([q[1] for q in qs], axis=1))
def put(q, e, v):
    c, s = q[0].reshape(128, -1, 4).copy(), q[1].copy(); c[:, e] = v[0].reshape(128, -1, 4); s[:, e] = v[1]
    return (c.reshape(128, -1), s)
def pk(c, s):
    return (np.ascontiguousarray(c), mx_ref.live(s))
def emit(q):
    return q[0], q[1]
def packed(v, rng):
    q = [mx_ref.quantize(np.ascontiguousarray(v[r])) for r in range(N)]
    return np.stack([a for a, b in q]), np.stack([mx_ref.plane(b, rng) for a, b in q])
def values_of_codes():
    e, c = np.zeros((128, 128, 4), np.float32), np.zeros((128, 2, 4), np.uint8)
    e[np.arange(128), np.arange(128), 0] = 1
    c[:127, :, 0] = np.arange(256).reshape(2, 128).T[:127]
    return mx_ref.matmul(mx_ref.quantize(e.reshape(128, 512).astype(BF)), (c.reshape(128, 8), np.full((16, 2), 127, np.uint8))).T.reshape(-1).astype(np.float64)
CODE_VALUE, SCALE_VALUE = values_of_codes(), 2.0 ** (np.arange(256) - 127.0)
def decode(q):
    return (CODE_VALUE[q[0]].reshape(16, 8, -1, 4) * SCALE_VALUE[q[1]][:, None, :, None] + 0.0).reshape(128, -1).astype(np.float32)
def f(rng, *shape):
    return mx_ref.flush((rng.standard_normal(shape, dtype=np.float32) * np.exp2(rng.integers(-2, 3, shape[:-1] + (1,)))).astype(BF))
def wide(rng, *shape, cols=0):
    v = rng.standard_normal(shape, dtype=np.float32) * np.exp2(rng.integers(-12, 13, shape)).astype(np.float32)
    if cols: v *= np.repeat(np.exp2(rng.integers(-cols, cols + 1, shape[:-2] + (1, shape[-1] // 4))) * (rng.random(shape[:-2] + (1, shape[-1] // 4)) > 0.0625), 4, axis=-1).astype(np.float32)
    return mx_ref.flush(v.astype(BF))
C, A, R = 352, 64, 2
def at(v, e):
    return np.take_along_axis(v, e, axis=1)
def bottleneck(s, up):
    c = np.abs(s - at(s, up))
    for i in range(9):
        c, up = np.maximum(c, at(c, up)), at(up, up)
    return c
def big(v):
    v = v.astype(np.float32)
    v[np.abs(v) < np.float32(2.0 ** -16)] = 0
    return v.astype(BF)
def numbers_of(rng):
    return {"x": big(f(rng, N, 128, 4 * C)), "u": np.array(f(rng, N, 128, 512)), "v": np.array(f(rng, N, 128, 512))}
def packed_layer(rng, w):
    c, p = packed(np.ascontiguousarray(w).reshape(N, 128, 2048), rng)
    return {"wc": c, "ws": p}
def weights(rng, still=[]):
    w = big(f(rng, N, 128, 2048)).reshape(N, 8, 16, 4, 8, 16, 4)
    for i in still:
        w[:, :, i] = 0
        w[:, :, :, :, :, i] = 0
    return packed_layer(rng, w)
def trees(rng):
    return rng.integers(0, np.maximum(np.arange(C), 1), (N, 8, C))
def places(rng):
    return np.stack([rng.integers(0, C + A * t, (N, 8, A, 4)) for t in range(R)], axis=2)
def lists_of(up, near):
    return {"pa": np.stack([gtable(up[r]) for r in range(N)]), "nr": np.stack([gtable(near[r].reshape(8, -1)) for r in range(N)])}
def signs(rng):
    return np.stack([rng.permutation(8) % 2 * 2.0 - 1.0 for r in range(N)])
def lost():
    t = np.zeros((128, 32, 4), np.float32)
    t[11, :, 0] = 4080
    t[8, :, 0] = 2.0 ** (11.0 - np.arange(32))
    once = decode(mx_ref.quantize(t.reshape(128, 128).astype(BF)))
    twice = decode(mx_ref.quantize(once.astype(BF)))
    e = np.flatnonzero((once[8, ::4] > 0) & (twice[8, ::4] == 0))
    return t[8, e[0] if len(e) else 16, 0]
def setup_inputs(rng):
    return {**numbers_of(rng), **weights(rng), **lists_of(trees(rng), places(rng))}
def setup_inputs_ties(rng):
    d = numbers_of(rng)
    e = rng.permutation(N)
    x = d["x"].reshape(N, 8, 16, C, 4)
    for r in range(N):
        k = np.zeros(C, int) if r == e[0] else rng.permutation(C) % 3
        a = x[r][:, :8, :3].copy()
        a[:, :, 2] = 0
        x[r][:, :8] = a[:, :, k]
    x[e[1]] = 0
    u = d["u"].reshape(N, 8, 16, 128, 4)
    u[:, :, 8:, ::16] = 0
    return {"x": x.reshape(N, 128, 4 * C), "u": u.reshape(N, 128, 512), "v": d["v"], **weights(rng, range(8)), **lists_of(trees(rng), places(rng))}
def setup_inputs_near(rng):
    d = numbers_of(rng)
    up, near = trees(rng), places(rng)
    x = d["x"].astype(np.float32).reshape(N, 8, 16, C, 4)
    x[:, :, 0] = 0
    x[:, :, 8:] = 0
    u = d["u"].reshape(N, 128, 128, 4)
    u[:, :, ::16] = 0
    o, c, j, half = rng.permutation(N) % 4, signs(rng), np.arange(C), C // 2
    for r in range(N):
        if o[r] == 3:
            up[r] = 0
            s = (j + rng.integers(A // 2, half, (8, 1))) % half
            x[r, :, 10, :, 0] = np.where(j < half, 9, 8) * 2.0 ** -30
        else:
            up[r] *= rng.integers(0, 2, (8, C))
            s = ((j + rng.integers(0, C, (8, 1))) % C + 1) // 2
        if o[r] < 2:
            x[r, :, 0, :, 0] = c[r][:, None]
            for g in rng.permutation(8)[:4]: x[r, g, 0, rng.integers(1, C), 0] *= np.float32(2.0 ** 30)
        b = ((s[:, :, None] >> np.arange(8)) & 1) * np.exp2(np.arange(8) - (23.0 if o[r] < 2 else 27.0))
        x[r, :, 8] = b[:, :, :4]
        x[r, :, 9] = b[:, :, 4:]
        k = 1.0 if o[r] == 0 else 2.0 ** -30
        for h in range(0, 128, 16):
            u[r, h, h, 0] = k
            u[r, h + 8:h + 10, h] = k
            u[r, h + 10, h, 0] = k
    x[:, :, 0, 0] = 0
    x[:, :, 8:, 0] = 0
    return {"x": x.reshape(N, 128, 4 * C).astype(BF), "u": u.reshape(N, 128, 512), "v": d["v"], **weights(rng, [0, 8, 9, 10, 11, 12, 13, 14, 15]), **lists_of(up, near)}
def setup_inputs_chains(rng):
    d = numbers_of(rng)
    up, near = trees(rng), places(rng)
    x = d["x"].astype(np.float32).reshape(N, 8, 16, C, 4)
    x[:, :, 8:] = 0
    u = d["u"].reshape(N, 128, 128, 4)
    u[:, :, ::16] = 0
    j = np.arange(C)
    chain, zig, h = np.maximum(j - 1, 0), 1 - 2 * (j % 2), rng.permutation(8)
    k = np.where(rng.permutation(N) < N // 2, 2.0 ** -30, 1.0)
    small = lost()
    p = int(rng.integers(N))
    for r in range(N):
        o = (r - p) % N
        s = rng.integers(0, 1000, (8, C))
        s[h[0], 0] = 4095
        s[h[1]] = 2048 + zig * ((C - j) // 2)
        s[h[2]] = 2048 + zig * ((j + 1) // 2)
        if o < 2:
            s[h[3]] = np.where(j <= A // 2, 1600 + zig * (599 + j), 1600)
            s[h[3], 0] = 0
        s[h[4]] = np.where(j < C // 2, 7, 3000)
        s[h[6]] = rng.integers(0, 8, C)
        s[h[7]] = 0
        up[r, h[:5]] = chain
        up[r, h[5]] = 0
        up[r, h[6]] = np.minimum(chain, C // 2)
        b = ((s[:, :, None] >> np.arange(12)) & 1) * np.exp2(np.arange(12.0))
        for i in range(3): x[r, :, 8 + i] = b[:, :, 4 * i:4 * i + 4]
        x[r, h[7], 8, 1:, 0] = small
        x[r, h[7], 11, :, 0] = 4080
        near[r, h[7], :, :, 0] = rng.integers(1, C, (R, A))
        near[r, h[7], :, :, 1] = 0
        near[r, h[7], 0, A // 2:] = rng.integers(1, C, (A - A // 2, 4))
        own = h[3] if o == 1 else h[5] if o == 3 else h[7]
        m = rng.permutation(h[:7][h[:7] != own])
        near[r, m[0]] = near[r, m[0], :, :1].copy()
        near[r, m[1]] = near[r, m[1], :, :, :1].copy()
        near[r, m[2]] = 0
        near[r, m[3]] = C - 1
        for t in range(R): near[r, m[4], t] = np.resize(rng.permutation(C + A * t), 4 * A).reshape(A, 4)
        near[r, m[5], 1] = C + rng.integers(0, A, (A, 4))
        for i in range(0, 128, 16): u[r, i + 8:i + 11, i] = k[r]
        if o == 1:
            near[r, h[3], 0] = 0
            near[r, h[3], 0, A // 2 + 1:] = np.arange(2, A // 2 + 1)[:, None] - np.array([1, 0, 1, 0])
        if o == 2:
            x[r, h[5], 8:] = 0
            x[r, h[5], 9, 1:, 0] = 10 * 2.0 ** -32
        if o == 3:
            x[r, h[5], 8:] = 0
            x[r, h[5], 8, 1:, 0] = 9 * 2.0 ** -32
            i = 16 * int(h[5])
            u[r, i + 8, i] = 9 * 2.0 ** -33
            u[r, i + 9:i + 11, i] = 2.0 ** -30
            near[r, h[5], 0, :, 0] = 0
    return {"x": x.reshape(N, 128, 4 * C).astype(BF), "u": u.reshape(N, 128, 512), "v": d["v"], **weights(rng, range(8, 16)), **lists_of(up, near)}
def setup_inputs_huge(rng):
    d = numbers_of(rng)
    up = trees(rng)
    c = np.stack([rng.permutation(C) % 2 * 2.0 - 1.0 for r in range(N)])
    c[rng.permutation(N) < N // 2] = -1
    for r in range(N):
        if (c[r] > 0).any():
            c[r, 1:3] = 1, -1
            e = np.where(c[r] > 0, 2, 1)
            e[:3] = 0, 0, 1
            up[r, rng.permutation(8)[:4]] = e
    x = (0.8 + 0.2 * rng.random((N, 128, C, 4))) * np.where(c < 0, -2.0 ** 30, 0.4 * 2.0 ** 30)[:, None, :, None]
    x[:, :, 0] = 0
    u = d["u"].reshape(N, 128, 128, 4)
    a = 2.0 ** 30 * (1 - 0.125 * rng.random((N, 128, 8, 4))) * signs(rng)[:, None, :, None]
    u[:, :, ::16] = a.astype(np.float32).astype(BF)
    w = np.zeros((N, 128, 4, 128, 4), np.float32)
    i = np.arange(128)
    for b in range(4): w[:, i, b, i, b] = 16
    return {"x": x.astype(np.float32).reshape(N, 128, 4 * C).astype(BF), "u": u.reshape(N, 128, 512), "v": d["v"], **packed_layer(rng, w.astype(BF)), **lists_of(up, places(rng))}
def setup_inputs_spread(rng):
    d = setup_inputs(rng)
    d["x"] = big(wide(rng, N, 128, 4 * C, cols=6))
    return d
def check_inputs(d):
    b = []
    for k in ("x", "u", "v"):
        a = np.abs(d[k].astype(np.float32))
        if not (np.isfinite(a).all() and ((a == 0) | (a >= 2.0 ** -30) & (a <= 2.0 ** 30)).all()): b.append("a value of " + k)
    none, least, most = [emit(mx_ref.quantize(np.full((128, 16), k, np.float32).astype(BF)))[1][0, 0] for k in (0.0, 2.0 ** -30, 2.0 ** 30)]
    for r in range(N):
        if ((d["wc"][r] == 0x7F) | (d["wc"][r] == 0xFF)).any(): b.append("wc: a code that is no number")
        s = mx_ref.live(d["ws"][r])
        if ((s != none) & ((s < least) | (s > most))).any(): b.append("ws: a scale out of range")
        e = gentries(d["pa"][r])
        if ((e < 0) | (e > np.maximum(np.arange(C) - 1, 0))).any(): b.append("pa: a parent out of range")
        e = gentries(d["nr"][r]).reshape(8, R, 4 * A)
        if ((e < 0) | (e >= C + A * np.arange(R)[:, None])).any(): b.append("nr: a near place out of range")
    return b
def reference(x, u, v, wc, ws, pa, nr):
    qu = [mx_ref.quantize(u[r]) for r in range(N)]
    lay = [pk(wc[r], ws[r]) for r in range(N)]
    now = [x[r] for r in range(N)]
    up = [gentries(pa[r]) for r in range(N)]
    near = [gentries(nr[r]).reshape(8, R, A, 4) for r in range(N)]
    for t in range(R):
        n = C + A * t
        sent, s, c = [], [], []
        for r in range(N):
            s.append(mx_ref.matmul(qu[r], mx_ref.quantize(now[r]))[::16])
            c.append(bottleneck(s[r], up[r]))
            sent.append(mx_ref.quantize(gcols(now[r], np.argsort(c[r], axis=1, kind="stable")[:, :A])))
        came = decode(join(*sent)).astype(BF)
        for r in range(N):
            new = np.ascontiguousarray(cut(came, (r - 1) % N, 4 * A))
            k = mx_ref.matmul(qu[r], mx_ref.quantize(new))[::16]
            i = near[r][:, t].reshape(8, 4 * A)
            gap = np.abs(at(s[r], i) - np.repeat(k, 4, axis=1))
            cost = np.maximum(at(c[r], i), gap).reshape(8, A, 4)
            parent = np.take_along_axis(near[r][:, t], np.argmin(cost, axis=2)[:, :, None], axis=2)[:, :, 0]
            price = np.maximum(np.repeat(np.min(cost, axis=2), 4, axis=1), gap)
            all_prices = np.full((8, n, A), np.inf, np.float32)
            for g in range(8): all_prices[g, i[g], np.arange(4 * A) // 4] = price[g]
            moved = np.min(all_prices, axis=2) < c[r]
            up[r] = np.concatenate([np.where(moved, n + np.argmin(all_prices, axis=2), up[r]), parent], axis=1)
            z = np.concatenate([now[r], new], axis=1)
            q = mx_ref.quantize(((z.astype(np.float32) + gcols(z, up[r]).astype(np.float32)) * np.float32(0.5)).astype(BF))
            now[r] = tile([np.maximum(mx_ref.matmul(pick(lay[r], np.arange(128 * b, 128 * b + 128)), q), np.float32(0.0)) * np.float32(0.03125) + z[:, b::4].astype(np.float32) for b in range(4)])
    n = C + A * R
    y, op = np.zeros((N, 128, n), np.float32), np.zeros((N, 8, n), np.float32)
    oc, osc = np.zeros((N, 128, 4 * n), np.uint8), np.zeros((N, 16, n), np.uint8)
    for r in range(N):
        q = mx_ref.quantize(now[r])
        y[r] = mx_ref.matmul(mx_ref.quantize(v[r]), q)
        op[r] = up[r]
        oc[r], osc[r] = emit(q)
    return {"y": y, "op": op, "oc": oc, "osc": osc}

@@ -1,0 +1,645 @@
+from concourse.mybir import dt, AluOpType as Op, ActivationFunctionType as Fn
+
+C, A = 352, 64
+NS = (C, C + A, C + 2 * A)
+CHUNKS = ((0, 176, 352), (0, 224, 416), (0, 256, 480))
+BIG = 2.0 ** 90
+HOLD = 2.0 ** 24
+KEEP = 4096.0
+X4 = "float8_e4m3fn_x4"
+
+SCRATCH = {
+    "wf": ("sbuf", [128, 14848], "float32"), "wb": ("sbuf", [128, 18432], "bfloat16"),
+    "wi": ("sbuf", [128, 512], "int32"), "wu": ("sbuf", [128, 768], "uint16"),
+    "ps": ("psum", [128, 4096], "float32"),
+    "pai": ("sbuf", [128, 22], "int32"), "nri": ("sbuf", [128, 32], "int32"),
+    "ub": ("sbuf", [128, 512], "bfloat16"), "vb": ("sbuf", [128, 512], "bfloat16"),
+    "qu": ("sbuf", [128, 128], X4), "su": ("sbuf", [128, 128], "uint8"),
+    "qr": ("sbuf", [128, 128], X4), "sr": ("sbuf", [128, 128], "uint8"),
+    "qv": ("sbuf", [128, 128], X4), "sv": ("sbuf", [128, 128], "uint8"),
+    "wq": ("sbuf", [128, 512], X4), "wsc": ("sbuf", [128, 512], "uint8"),
+    "repi": ("sbuf", [128, 8], "int32"), "repu": ("sbuf", [128, 8], "uint16"),
+    "one": ("sbuf", [128, 528], "bfloat16"), "eye": ("sbuf", [128, 528], "bfloat16"),
+    "qe": ("sbuf", [128, 512], X4), "se": ("sbuf", [128, 512], "uint8"),
+    "x2": ("sbuf", [128, 4 * NS[2]], "bfloat16"),
+    "qx2": ("sbuf", [128, NS[2]], X4), "sx2": ("sbuf", [128, NS[2]], "uint8"),
+    "ysb": ("sbuf", [128, NS[2]], "float32"), "osb": ("sbuf", [128, NS[2]], "float32"),
+}
+for _t in range(2):
+    _n, _m = NS[_t], NS[_t + 1]
+    SCRATCH.update({
+        "x%d" % _t: ("sbuf", [128, 4 * _m], "bfloat16"), "xh%d" % _t: ("sbuf", [128, 4 * _m], "bfloat16"),
+        "xo%d" % _t: ("sbuf", [128, 4 * _m], "bfloat16"),
+        "yt%d" % _t: ("sbuf", [128, 4 * _m], "bfloat16"), "ru%d" % _t: ("sbuf", [128, 4 * _m], "float32"),
+        "dd%d" % _t: ("sbuf", [128, 4 * _n], "bfloat16"),
+        "qx%d" % _t: ("sbuf", [128, _n], X4), "sx%d" % _t: ("sbuf", [128, _n], "uint8"),
+        "qh%d" % _t: ("sbuf", [128, 128], X4), "sh%d" % _t: ("sbuf", [128, 128], "uint8"),
+        "qy%d" % _t: ("sbuf", [128, _m], X4), "sy%d" % _t: ("sbuf", [128, _m], "uint8"),
+        "rq%d" % _t: ("sbuf", [128, 224], X4), "rs%d" % _t: ("sbuf", [128, 224], "uint8"),
+        "lq%d" % _t: ("sbuf", [128, _n], X4), "ls%d" % _t: ("sbuf", [128, _n], "uint8"),
+        "el%d" % _t: ("sbuf", [128, 16], "uint16"), "rl%d" % _t: ("sbuf", [128, 16], "uint16"),
+        "ll%d" % _t: ("sbuf", [128, 16], "uint16"),
+    })
+SEMAPHORES = (["ev", "ea", "ep", "eg", "sent"] + ["dm%d" % _i for _i in range(28)]
+              + ["%s%d" % (_s, _t) for _s in ("rc", "rp", "rn", "aq", "an") for _t in range(2)])
+
+CY, WAKE = 1.04, 90.0
+LAT = (9000.0, 4000.0, 2500.0)
+NA = (5, 6, 0)
+EARLY = {"k0": 3000, "p0": 5000, "o1": 5000, "e1": 3000, "o0": 2000, "q1": 12000, "p1": 2000, "s0": 5000, "u10": 2000, "e0": 1000,
+         "h0": 300, "s1": 2000, "u00": 1000, "d1": 8000, "d0": 300, "u01": 300, "f0": 2000, "u02": 300, "q0": 600, "v": 600,
+         "x1": 5000, "u11": 300, "k1": 2000, "u12": 1000}
+
+
+def relays_of(T, topo, r):
+    me, nxt = T.cores[r], T.cores[(r + 1) % len(T.cores)]
+    return [c for c in topo.cores_of(me) if T.rank_of(c) is None and topo.die(c) == topo.die(me) and topo.may_write(c, nxt)][:2]
+
+
+def relay_program(g, core, T, topo, r, k):
+    nxt = T.cores[(r + 1) % len(T.cores)]
+    rid, pid = topo.addr(nxt, core)
+    m, ne = topo.mask(core, nxt), len(topo.engines(core, nxt))
+    nin = len(topo.engines(T.cores[r], core))
+    calls = 0
+    for t in range(2):
+        a, b = CHUNKS[t][k], CHUNKS[t][k + 1]
+        g.wait_ge(T.sem["rc%d" % t], nin)
+        g.remote_dma(T["lq%d" % t][:, a:b].bitcast(dt.uint8), T["rq%d" % t][:, 0:b - a].bitcast(dt.uint8), T.sem["aq%d" % t], T.sem.sent, pid, rid, m)
+        g.wait_ge(T.sem["rp%d" % t], nin)
+        g.remote_dma(T["ls%d" % t][:, a:b], T["rs%d" % t][:, 0:b - a], T.sem["aq%d" % t], T.sem.sent, pid, rid, m)
+        calls += 2
+        if k == 0:
+            g.wait_ge(T.sem["rn%d" % t], nin)
+            g.remote_dma(T["ll%d" % t][:], T["rl%d" % t][:], T.sem["an%d" % t], T.sem.sent, pid, rid, m)
+            calls += 1
+    g.wait_ge(T.sem.sent, calls * ne)
+
+
+def rank_program(g, core, T, topo):
+    rank = T.rank_of(core)
+    if rank is None:
+        for r in range(len(T.cores)):
+            rl = relays_of(T, topo, r)
+            if core in rl:
+                relay_program(g, core, T, topo, r, rl.index(core))
+        return
+    room = {}
+    plan(g, core, T, topo, rank, room)
+    emit(g, T, plan(g, core, T, topo, rank, room))
+
+
+def V(name, lo, hi, step=1):
+    return (name, lo, hi, step)
+
+
+def sub(v, lo, hi, step=1):
+    return (v[0], v[1] + lo, v[1] + hi, step)
+
+
+def size(v):
+    return (v[2] - v[1] + v[3] - 1) // v[3]
+
+
+def clash(a, b):
+    if a[0] != b[0]:
+        return False
+    if a[0] == "ps":
+        return a[1] // 512 == b[1] // 512
+    if a[2] <= b[1] or b[2] <= a[1]:
+        return False
+    if a[3] > 1 and a[3] == b[3] and (a[1] - b[1]) % a[3]:
+        return False
+    return True
+
+
+def link(ops):
+    for i, o in enumerate(ops):
+        d = set(o["after"])
+        for j in range(i):
+            p = ops[j]
+            hit = any(clash(a, b) for a in p["w"] for b in o["r"] + o["w"]) or any(clash(a, b) for a in p["r"] for b in o["w"])
+            if not hit and p["q"] != o["q"]:
+                hit = any(a[0] == "ps" and clash(a, b) for a in p["r"] for b in o["r"])
+            if hit:
+                d.add(j)
+        o["deps"] = sorted(d)
+
+
+def schedule(ops):
+    n = len(ops)
+    level = [0.0] * n
+    for i in range(n - 1, -1, -1):
+        level[i] += ops[i]["cost"] + ops[i]["lat"] + EARLY.get(ops[i].get("mark"), 0.0)
+        for j in ops[i]["deps"]:
+            level[j] = max(level[j], level[i] + WAKE)
+    busy, done = {}, [0.0] * n
+    for i in sorted(range(n), key=lambda i: (-level[i], i)):
+        o = ops[i]
+        t0 = max([done[j] + WAKE for j in o["deps"]] + [0.0])
+        if o["q"] != "x":
+            line = busy.setdefault(o["q"], [])
+            k = 0
+            while k < len(line):
+                if t0 + o["cost"] <= line[k][0]:
+                    break
+                t0 = max(t0, line[k][1])
+                k += 1
+            line.insert(k, (t0, t0 + o["cost"], i))
+        o["start"] = t0
+        done[i] = t0 + o["cost"] + o["lat"]
+    return sorted(range(n), key=lambda i: (ops[i]["start"], i)), max(done)
+
+
+def emit(g, T, ops):
+    link(ops)
+    order, _ = schedule(ops)
+    queue = {"v": g.vector, "a": g.scalar, "p": g.tensor, "g": g, "s": g.sync}
+    count, seen, dmas = {"v": 0, "a": 0, "p": 0, "g": 0}, {}, 0
+    sent = 0
+    for i in order:
+        o = ops[i]
+        if o["kind"] == "c":
+            count[o["q"]] += 1
+            o["sig"] = ("e" + o["q"], count[o["q"]])
+        elif o["kind"] == "d":
+            o["sig"] = ("dm%d" % dmas, 16)
+            dmas += 1
+    for i in order:
+        o = ops[i]
+        if o["kind"] == "x":
+            continue
+        need = {}
+        for j in o["deps"]:
+            s, v = ops[j]["sig"]
+            need[s] = max(need.get(s, 0), v)
+        for s in sorted(need):
+            if seen.get((o["q"], s), 0) < need[s]:
+                queue[o["q"]].wait_ge(T.sem[s], need[s])
+                seen[(o["q"], s)] = need[s]
+        ins = o["fn"]()
+        if o["kind"] == "r":
+            sent += o["inc"]
+        else:
+            ins.then_inc(T.sem[o["sig"][0]], 16 if o["kind"] == "d" else 1)
+    g.wait_ge(T.sem.sent, sent)
+    for q in count:
+        g.sync.wait_ge(T.sem["e" + q], count[q])
+    for k in range(dmas):
+        g.sync.wait_ge(T.sem["dm%d" % k], 16)
+
+
+def plan(g, core, T, topo, rank, room):
+    ops, top, turn = [], {"wf": 0, "wb": 0, "wi": 0, "wu": 0}, [None]
+    wide = {"float32": 4, "int32": 4, "bfloat16": 2, "uint16": 2, "uint8": 1, X4: 4}
+
+    def new(kind, n):
+        lo, w = top[kind], (n + 15) // 16 * 16
+        if turn[0] is not None:
+            turn[0] += 1
+            w = room[turn[0]] = max(room.get(turn[0], 0), w)
+        top[kind] = lo + w
+        return V(kind, lo, lo + n)
+
+    def whole(name):
+        return V(name, 0, SCRATCH[name][1][1])
+
+    def ap(v):
+        if len(v) == 2:
+            return ap(v[0]).indirect(ap(v[1]))
+        return T[v[0]][:, v[1]:v[2]:v[3]] if v[3] > 1 else T[v[0]][:, v[1]:v[2]]
+
+    def sc(x):
+        return ap(x) if isinstance(x, tuple) else x
+
+    def add(q, kind, fn, r, w, cost, lat=0.0, after=(), **more):
+        rr = []
+        for v in r:
+            if isinstance(v, tuple):
+                rr += list(v) if len(v) == 2 else [v]
+        ops.append(dict(q=q, kind=kind, fn=fn, r=rr, w=list(w), cost=cost, lat=lat, after=list(after), **more))
+        return len(ops) - 1
+
+    def price(out, ins, two=False):
+        n = size(out)
+        if any(len(v) == 2 for v in ins):
+            return 50 + 1.56 * CY * n
+        half = all(wide[SCRATCH[v[0]][2]] == 2 for v in [out] + ins)
+        if two:
+            return CY * max(64, n if any(v[0] == "ps" for v in ins) else (1.5 if half else 2) * n)
+        return CY * max(64, n / 2 if half else n)
+
+    def tt(out, a, b, op):
+        add("v", "c", lambda: g.vector.tensor_tensor(ap(out), ap(a), ap(b), op), [a, b], [out], price(out, [a, b], True))
+
+    def ts(out, a, s1, op0, s2=None, op1=None):
+        if op1 is None:
+            fn = lambda: g.vector.tensor_scalar(ap(out), ap(a), sc(s1), None, op0)
+        else:
+            fn = lambda: g.vector.tensor_scalar(ap(out), ap(a), sc(s1), sc(s2), op0, op1)
+        add("v", "c", fn, [a, s1, s2], [out], price(out, [a]))
+
+    def cp(out, a):
+        add("v", "c", lambda: g.vector.tensor_copy(ap(out), ap(a)), [a], [out], price(out, [a]))
+
+    def scatter(win, off, a):
+        add("v", "c", lambda: g.vector.tensor_copy(ap((win, off)), ap(a)), [a, off], [win], 50 + 3.8 * CY * size(a))
+
+    def scan(out, d0, d1, op0, op1):
+        add("v", "c", lambda: g.vector.tensor_tensor_scan(ap(out), ap(d0), ap(d1), 0.0, op0, op1), [d0, d1], [out], price(out, [d0, d1]))
+
+    def fill(out, k):
+        add("v", "c", lambda: g.vector.memset(ap(out), k), [], [out], price(out, []))
+
+    def act(out, a, f, bias=None, scale=None, acc=None):
+        kw = {}
+        if bias is not None:
+            kw["bias"] = sc(bias)
+        if scale is not None:
+            kw["scale"] = sc(scale)
+        if acc is not None:
+            kw["accum_out"] = ap(acc)
+        cost = 65 + 1.56 * CY * size(out) if len(a) == 2 else CY * max(64, size(out)) + (20 if acc else 0)
+        add("a", "c", lambda: g.scalar.activation(ap(out), ap(a), f, **kw), [a, bias, scale], [out] + ([acc] if acc else []), cost)
+
+    def iota(out, pattern, base=0, cm=0):
+        if SCRATCH[out[0]][2] == "int32":
+            fn = lambda: g.iota(ap(out), pattern, base, cm)
+        else:
+            fn = lambda: g.iota(ap(out), pattern, base, cm, allow_small_or_imprecise_dtypes=True)
+        add("g", "c", fn, [], [out], 130 + 2 * CY * size(out))
+
+    def quant(q, s, a):
+        add("v", "c", lambda: g.vector.quantize_mx(ap(q), ap(s), ap(a)), [a], [q, s], 15 + 0.27 * size(a))
+
+    def mm(bank, lq, ls, rq, rs):
+        out = V("ps", 512 * bank, 512 * bank + size(rq))
+        add("p", "c", lambda: g.tensor.matmul_mx(ap(out), ap(lq), ap(ls), ap(rq), ap(rs), True, True), [lq, ls, rq, rs], [out], 0.7 * (size(rq) + 16), lat=60)
+        return out
+
+    def dma(q, fn, r, w, lat):
+        add(q, "d", fn, r, w, 60, lat)
+
+    def heap(out, a, lat):
+        add("g", "d", lambda: g.dma_start(ap(out), ap(a), accum_op=Op.add), [a, out], [out], 700, lat)
+
+    def u8(v):
+        return ap(v).bitcast(dt.uint8)
+
+    def mark(name):
+        ops[-1]["mark"] = name
+
+    rl = relays_of(T, topo, rank)
+    ne = len(topo.engines(rl[0], T.cores[(rank + 1) % len(T.cores)]))
+
+    def hand(k, dst, src, sem, codes=False):
+        rid, pid = topo.addr(rl[k], core)
+        f = u8 if codes else ap
+        return add("g", "r", lambda: g.remote_dma(f(dst), f(src), T.sem[sem], T.sem.sent, pid, rid, topo.mask(core, rl[k])), [src], [], 400,
+                   inc=len(topo.engines(core, rl[k])))
+
+    def arrival(after, w, sem, v, lat):
+        add("x", "x", None, [], w, 0.0, lat, after=after, sig=(sem, v))
+
+    dma("s", lambda: g.sync.dma_start(T.pai[:], T.pa[:]), [], [whole("pai")], 2000)
+    dma("a", lambda: g.scalar.dma_start(T.ub[:], T.u[:]), [], [whole("ub")], 2200)
+    dma("s", lambda: g.sync.dma_start(T.x0[:, 0:704], T.x[:, 0:704]), [], [V("x0", 0, 704)], 2600)
+    dma("a", lambda: g.scalar.dma_start(T.x0[:, 704:1408], T.x[:, 704:1408]), [], [V("x0", 704, 1408)], 2900)
+    dma("s", lambda: g.sync.dma_start(T.nri[:], T.nr[:]), [], [whole("nri")], 3000)
+    gate = [V("x0", 704, 1408)]
+    dma("s", lambda: g.sync.dma_start(T.wq[:].bitcast(dt.uint8), T.wc[:]), gate, [whole("wq")], 3000)
+    dma("s", lambda: g.sync.dma_start(T.wsc[:], T.ws[:]), gate, [whole("wsc")], 2500)
+    add("g", "d", lambda: g.dma_start(T.vb[:], T.v[:]), gate, [whole("vb")], 1500, 2500)
+    mark("v")
+
+    pi, cols, cf = new("wi", 1), new("wi", 4), new("wf", 16)
+    col = lambda k: sub(cf, k, k + 1)
+    fill(col(14), 0.5)
+    fill(col(15), -0.5)
+    fill(col(12), -256.0)
+    iota(pi, [[1, 1]], 0, 1)
+    ts(sub(cols, 0, 1), pi, 15, Op.bitwise_and)
+    ts(sub(cols, 1, 2), pi, 2, Op.logical_shift_right, 3, Op.bitwise_and)
+    ts(sub(cols, 2, 3), pi, 3, Op.bitwise_and)
+    cp(sub(cf, 0, 3), sub(cols, 0, 3))
+    q16, q4, qt, q16n, q4n, s16, s4p, s4n, qto = [col(k) for k in range(9)]
+    ts(sub(cf, 3, 5), sub(cf, 0, 2), 1.0, Op.add)
+    ts(s16, q16, 15.0, Op.is_equal, 1.0 / HOLD, Op.max)
+    ts(col(10), q4, 3.0, Op.is_equal, 1.0 / HOLD, Op.max)
+    ts(s4p, col(10), 4.0, Op.mult)
+    ts(s4n, col(10), -4.0, Op.mult)
+    ts(qto, qt, 0.25, Op.add)
+    jf, jc, rr = new("wf", 416), new("wb", 352), new("wb", 32)
+    r16, r4 = sub(rr, 0, 16), sub(rr, 16, 32)
+    iota(r16, [[1, 16]])
+    iota(jc, [[1, 352]], -256)
+    iota(r4, [[0, 4], [1, 4]])
+    iota(jf, [[1, 416]])
+    ones = V("one", 0, 528)
+    fill(ones, 1.0)
+    qoff = new("wu", 30)
+    ts(qoff, sub(ones, 0, 30), q16, Op.mult)
+
+    def spread(p, n, on_vector=False):
+        m = new(p[0], n)
+        if on_vector:
+            cp(m, (p, sub(qoff, 0, n // 16)))
+        else:
+            act(m, (p, sub(qoff, 0, n // 16)), Fn.Copy)
+        return m
+
+    def hold(r, q, qn):
+        a, b, m = new("wb", 16), new("wb", 16), new("wb", 16)
+        ts(a, r, q, Op.not_equal)
+        ts(b, r, qn, Op.is_equal, HOLD, Op.mult)
+        tt(m, a, b, Op.max)
+        return m, a
+    p16, poff = hold(r16, q16, q16n)
+    p4, _ = hold(r4, q4, q4n)
+    pdiag, w16, pns, pbig = new("wb", 16), new("wb", 16), new("wb", 16), new("wb", 16)
+    ts(pdiag, r16, q16, Op.is_equal)
+    ts(w16, r16, q16, Op.is_ge, -0.5, Op.add)
+    ts(pns, r16, 0.0, Op.not_equal)
+    ts(pbig, r4, 0.0, Op.is_equal, BIG, Op.mult)
+    m16, m4, off16, diag, ns16, big4 = spread(p16, 416, True), spread(p4, 480), spread(poff, 208), spread(pdiag, 208), spread(pns, 128), spread(pbig, 256)
+    mr = {}
+    for h in (176, 208, 128):
+        mr[h] = new("wb", h + 16)
+        act(sub(mr[h], 0, 16), poff, Fn.Copy)
+        act(sub(mr[h], 16, h), sub(ones, 16, h), Fn.Copy)
+        ts(sub(mr[h], h, h + 16), pdiag, KEEP, Op.mult, 1.0, Op.max)
+    lut64, lutb, pick = new("wb", 208), new("wf", 8), new("wf", 256)
+    ts(lut64, sub(jc, 0, 208), -192.0, Op.is_lt)
+    act(lutb, sub(jf, 0, 8), Fn.Copy, scale=BIG)
+    m16i, xi, xf, kh, rep4, picki = new("wi", 16), new("wi", 16), new("wf", 16), new("wf", 4), new("wu", 16), new("wf", 256)
+    iota(m16i, [[16, 16]])
+    ts(xf, m16i, q16, Op.add)
+    cp(xi, xf)
+    ts(kh, sub(xf, 0, 4), 0.5, Op.add)
+    ts(col(13), q4, 4.0, Op.mult, 3.0, Op.add)
+    ts(rep4, m16i, col(13), Op.add)
+    iota(picki, [[-2048, 64], [512, 4]], 63 * 2048)
+    act(pick, picki, Fn.Copy, scale=2.0 ** -17)
+    add("g", "c", lambda: g.affine_select(T.eye[:], T.one[:], [[1, 528]], Op.is_equal, 0.0, -3, -4), [ones], [whole("eye")], 170 + 2 * CY * 528)
+    for b in range(4):
+        quant(V("qe", 128 * b, 128 * b + 128), V("se", 128 * b, 128 * b + 128), V("eye", 3 - b, 515 - b))
+    iota(whole("repi"), [[16, 8]])
+    cp(whole("repu"), whole("repi"))
+    quant(whole("qu"), whole("su"), whole("ub"))
+    add("v", "c", lambda: g.vector.tensor_copy(T.qr[:, 0:128].bitcast(dt.uint32), T.qu[:, 0:128].bitcast(dt.uint32).indirect(T.repu[:, 0:8])),
+        [whole("qu"), whole("repu")], [whole("qr")], 260)
+    add("a", "c", lambda: g.scalar.activation(T.sr[:, 0:128], T.su[:, 0:128].indirect(T.repu[:, 0:8]), Fn.Copy),
+        [whole("su"), whole("repu")], [whole("sr")], 275)
+    quant(whole("qv"), whole("sv"), whole("vb"))
+    qr, sr = whole("qr"), whole("sr")
+    nru, nrf = new("wu", 32), new("wf", 32)
+    cp(nru, whole("nri"))
+    ts(nrf, whole("nri"), 256.0, Op.mult)
+
+    def ranks(row, h, na, out):
+        k = h // 16
+        msk, lst = new("wf", h), new("wf", h)
+        tt(msk, row, sub(diag, 0, h), Op.mult)
+        scan(lst, sub(off16, 0, h), msk, Op.mult, Op.add)
+        at = lambda m: sub(lst, 16 * m + 15, 16 * m + 16)
+        nv, w = k - na, h + 16
+        fl, cnt = new("wb", nv * w), new("wb", nv * w)
+        for m in range(nv):
+            f = sub(fl, m * w, m * w + w)
+            ts(sub(f, 0, h - 16 * m), sub(row, 16 * m, h), at(m), Op.is_lt)
+            ts(sub(f, h - 16 * m, w), sub(row, 0, 16 * m + 16), at(m), Op.is_le)
+            scan(sub(cnt, m * w, m * w + w), mr[h], f, Op.mult, Op.add)
+        ts(sub(out, 0, nv), sub(cnt, w - 1, nv * w, w), 1.0 / KEEP, Op.mult, 0.25, Op.add)
+        if na:
+            sg, junk, acc = new("wb", na * h), new("wb", na * h), new("wf", 32)
+            ib, ibs, t1 = new("wb", 16 * na), new("wb", 16 * na), new("wf", 48)
+            fill(sub(acc, 16 + na - 1, 16 + na), 0.0)
+            for a in range(na):
+                m = nv + a
+                y = sub(sg, a * h, a * h + h)
+                act(y, row, Fn.Sign, bias=at(m), scale=-1.0)
+                act(sub(junk, a * h, a * h + 16 * m), sub(y, 0, 16 * m), Fn.Sign, bias=col(14), acc=sub(acc, a, a + 1))
+                if m < k - 1:
+                    act(sub(junk, a * h + 16 * m + 16, a * h + h), sub(y, 16 * m + 16, h), Fn.Sign, bias=col(15), acc=sub(acc, 16 + a, 17 + a))
+                tt(sub(ib, 16 * a, 16 * a + 16), sub(y, 16 * m, 16 * m + 16), w16, Op.is_gt)
+            scan(ibs, sub(ns16, 0, 16 * na), ib, Op.mult, Op.add)
+            ts(sub(t1, 0, na), sub(ibs, 15, 16 * na, 16), 2.0, Op.mult, float(h - 16), Op.add)
+            tt(sub(t1, 16, 16 + na), sub(acc, 0, na), sub(acc, 16, 16 + na), Op.add)
+            tt(sub(t1, 32, 32 + na), sub(t1, 0, na), sub(t1, 16, 16 + na), Op.add)
+            ts(sub(out, nv, k), sub(t1, 32, 32 + na), 0.5, Op.mult, 0.25, Op.add)
+
+    negp, nxts = new("wf", NS[0]), [new("wf", NS[1]), new("wf", NS[2])]
+    ups = [[new("wb", n), new("wb", n), new("wb", n), new("wb", n)] for n in NS[:2]]
+    base = dict(top)
+    for t in range(2):
+        top.update(base)
+        turn[0] = 0
+        n, n2, ch, ch2 = NS[t], NS[t + 1], CHUNKS[t], CHUNKS[t + 1]
+        X, XH, XN = "x%d" % t, "xh%d" % t, "x%d" % (t + 1)
+        nm = lambda s, lo, hi, step=1, t=t: V("%s%d" % (s, t), lo, hi, step)
+        k = n // 16
+        lists = [new("wu", 32) for i in range(9)]
+        low = [0 if t or i < 5 else 2 ** i for i in range(9)]
+        up = ups[t]
+        if t == 0:
+            cp(sub(lists[0], 0, k), whole("pai"))
+            act(up[0], (jc, sub(lists[0], 0, k)), Fn.Copy)
+            act(negp, (sub(jf, 0, n), sub(lists[0], 0, k)), Fn.Copy, scale=-1.0)
+        else:
+            act(up[0], negp, Fn.Identity, bias=col(12), scale=-1.0)
+            scan(up[3], sub(m16, 0, n), up[0], Op.mult, Op.add)
+            ts(sub(lists[0], 0, k), sub(up[3], 15, n, 16), s16, Op.mult, 256.25, Op.add)
+        for i in range(8):
+            lo2, hs = low[i + 1], up[2 + i % 2]
+            act(sub(up[(i + 1) % 2], lo2, n), (up[i % 2], sub(lists[i], lo2 // 16, k)), Fn.Copy)
+            if lo2 and i < 7:
+                act(sub(up[(i + 1) % 2], 0, lo2), sub(ones, 0, lo2), Fn.Copy, scale=-256.0)
+            scan(sub(hs, lo2, n), sub(m16, lo2, n), sub(up[(i + 1) % 2], lo2, n), Op.mult, Op.add)
+            ts(sub(lists[i + 1], lo2 // 16, k), sub(hs, lo2 + 15, n, 16), s16, Op.mult, 256.25, Op.add)
+            mark("u%d%d" % (t, i // 3))
+        s, s2 = new("wf", n), new("wf", n)
+        sends = []
+        for c in range(2):
+            a, b = ch[c], ch[c + 1]
+            quant(nm("qx", a, b), nm("sx", a, b), V(X, 4 * a, 4 * b))
+            mark("x%d" % t)
+            p = mm(c, qr, sr, nm("qx", a, b), nm("sx", a, b))
+            p2 = mm(2 + c, qr, sr, nm("qx", a, b), nm("sx", a, b))
+            cp(sub(s, a, b), p)
+            act(sub(s2, a, b), p2, Fn.Copy)
+            sends.append(hand(c, nm("rq", 0, b - a), nm("qx", a, b), "rc%d" % t, True))
+            sends.append(hand(c, nm("rs", 0, b - a), nm("sx", a, b), "rp%d" % t))
+        arrival(sends, [nm("lq", 0, n), nm("ls", 0, n)], "aq%d" % t, 4 * ne, LAT[0])
+        for j in range(4):
+            act(V(XH, j * n, j * n + n), V(X, j * n, j * n + n), Fn.Copy, scale=0.5)
+            mark("h%d" % t)
+            act(nm("xo", j * n, j * n + n), V(X, j * n, j * n + n), Fn.Copy, scale=0.5)
+            mark("o%d" % t)
+        dma("s", lambda o=V(XN, 0, 4 * ch2[1]), i=V(X, 0, 4 * ch2[1]): g.sync.dma_start(ap(o), ap(i)), [V(X, 0, 4 * ch2[1])], [V(XN, 0, 4 * ch2[1])], 2500)
+        pc, other, dif = new("wf", n + 256), new("wf", n), new("wf", n)
+        cb = [other, sub(pc, 0, n)]
+        twin = [new("wf", n), new("wf", n)]
+        halves = lambda lo: ((lo, (lo + n + 32) // 64 * 32), ((lo + n + 32) // 64 * 32, n))
+        for a, b in halves(0):
+            tt(sub(dif, a, b), (s, sub(lists[0], a // 16, b // 16)), sub(s2, a, b), Op.subtract)
+            act(sub(other, a, b), sub(dif, a, b), Fn.Abs)
+        for a, b in halves(0):
+            act(sub(twin[0], a, b), sub(dif, a, b), Fn.Abs)
+        for i in range(9):
+            if low[i]:
+                act(sub(cb[(i + 1) % 2], low[i - 1], low[i]), sub(cb[i % 2], low[i - 1], low[i]), Fn.Copy)
+            for a, b in halves(low[i]):
+                tt(sub(cb[(i + 1) % 2], a, b), (cb[i % 2], sub(lists[i], a // 16, b // 16)), sub(twin[i % 2], a, b), Op.max)
+            if i < 8:
+                for a, b in halves(low[i]):
+                    a = max(a, low[i + 1])
+                    if a < b:
+                        act(sub(twin[(i + 1) % 2], a, b), sub(cb[(i + 1) % 2], a, b), Fn.Copy)
+        cc = cb[1]
+        h = n // 2
+        win, rk = new("wf", h), new("wu", 16)
+        tt(win, sub(cc, 0, n, 2), sub(cc, 1, n, 2), Op.min)
+        ranks(win, h, NA[t], rk)
+        flag, pre, fl, cnt, acc, ou = new("wb", h), new("wb", h), new("wb", 4 * h), new("wb", 2 * h), new("wf", 2), new("wu", 8)
+        cp(flag, (lut64, sub(rk, 0, h // 16)))
+        scan(pre, sub(ones, 0, h), flag, Op.mult, Op.add)
+        for u in range(2):
+            ts(sub(fl, u * h, u * h + h), pre, sub(kh, u, u + 1), Op.is_lt)
+            scan(sub(cnt, u * h, u * h + h), sub(ones, 0, h), sub(fl, u * h, u * h + h), Op.mult, Op.add)
+            act(sub(fl, (2 + u) * h, (3 + u) * h), pre, Fn.Sign, bias=sub(kh, 2 + u, 3 + u), scale=-1.0, acc=sub(acc, u, u + 1))
+        for e in range(2):
+            ts(sub(ou, 4 * e, 4 * e + 2), sub(cnt, h - 1, 2 * h, h), 2.0, Op.mult, e + 0.25, Op.add)
+            ts(sub(ou, 4 * e + 2, 4 * e + 4), acc, h + e + 0.25, Op.add)
+        c2, j2, rk2, srt, hs = new("wf", 128), new("wf", 128), new("wu", 8), new("wf", 128), new("wf", 64)
+        cp(sub(c2, 0, 128, 2), (cc, sub(ou, 0, 4)))
+        act(sub(c2, 1, 128, 2), (cc, sub(ou, 4, 8)), Fn.Copy)
+        for e in range(2):
+            act(sub(j2, e, 128, 2), (sub(jf, 0, n), sub(ou, 4 * e, 4 * e + 4)), Fn.Copy)
+        ranks(c2, 128, NA[2], rk2)
+        scatter(srt, rk2, j2)
+        scan(hs, sub(m4, 0, 64), sub(srt, 0, 64), Op.mult, Op.add)
+        ts(nm("el", 0, 16), sub(hs, 3, 64, 4), s4p, Op.mult, qto, Op.add)
+        sl = hand(0, nm("rl", 0, 16), nm("el", 0, 16), "rn%d" % t)
+        arrival([sl], [nm("ll", 0, 16)], "an%d" % t, ne, LAT[1])
+        for b in range(4):
+            p = mm(4 + b, V("qe", 128 * b, 128 * b + 128), V("se", 128 * b, 128 * b + 128), nm("lq", 0, n), nm("ls", 0, n))
+            act(nm("dd", b, 4 * n, 4), p, Fn.Copy)
+            mark("d%d" % t)
+        nu = sub(nru, 16 * t, 16 * t + 16)
+        pk, krow, klst, junk, acc = new("wf", 256), new("wf", 256), new("wf", 16), new("wb", 512), new("wf", 16)
+        act(pk, (sub(jf, 0, n), nu), Fn.Copy, scale=2.0 ** -17)
+        act(krow, (sub(jf, 0, n), nu), Fn.Copy, scale=256.0)
+        heap(pk, pick, 2500)
+        mark("p%d" % t)
+        heap(krow, sub(jf, 0, 256), 2500)
+        tt(klst, sub(nrf, 16 * t, 16 * t + 16), xf, Op.add)
+        for m in range(16):
+            act(sub(junk, 256 * (m % 2), 256 * (m % 2) + 256), krow, Fn.Sign, bias=sub(klst, m, m + 1), scale=-1.0, acc=sub(acc, m, m + 1))
+        ko, ks, kk, sh, an = new("wu", 16), new("wf", 272), new("wi", 48), new("wi", 48), new("wi", 32)
+        ts(ko, acc, 0.5, Op.mult, 127.75, Op.add)
+        mark("k%d" % t)
+        nk, ew, vs, gt = new("wf", 256), new("wf", NS[1] + 256), new("wf", 272), new("wf", 272)
+        if t == 0:
+            fill(sub(ks, 0, 8), -256.0)
+            fill(sub(ks, 264, 272), 600.0 * 256)
+            fill(sub(vs, 256, 272), 0.0)
+            fill(sub(gt, 0, 8), 1.0)
+        scatter(sub(ks, 8, 264), ko, krow)
+        for e, d in enumerate((0, -1, 1)):
+            hs = new("wf", 256)
+            scan(hs, sub(m16, 0, 256), sub(ks, 8 + d, 264 + d), Op.mult, Op.add)
+            ts(sub(kk, 16 * e, 16 * e + 16), sub(hs, 15, 256, 16), s16, Op.mult)
+        ts(sh, kk, 8, Op.arith_shift_right)
+        ts(an, sub(kk, 0, 32), 255, Op.bitwise_and)
+        plc, first, last = sub(sh, 0, 16), new("wi", 16), new("wi", 16)
+        tt(first, plc, sub(sh, 16, 32), Op.not_equal)
+        tt(last, plc, sub(sh, 32, 48), Op.not_equal)
+        sigu, firstu, d1u, endo, endu = new("wu", 16), new("wu", 16), new("wu", 16), new("wu", 16), new("wu", 32)
+        cp(sigu, sub(an, 0, 16))
+        cp(firstu, first)
+        for out, bs, flg in ((d1u, sub(an, 16, 32), first), (endo, xi, last)):
+            w = new("wi", 64)
+            tt(sub(w, 0, 16), plc, bs, Op.subtract)
+            ts(sub(w, 16, 32), sub(w, 0, 16), float(-n), Op.add)
+            tt(sub(w, 32, 48), sub(w, 16, 32), flg, Op.mult)
+            tt(sub(w, 48, 64), sub(w, 32, 48), bs, Op.add)
+            ts(out, sub(w, 48, 64), float(n), Op.add)
+            mark("f%d" % t)
+        bigs, nks, hs, sn = new("wf", 256), new("wf", 256), new("wf", n), new("wf", 256)
+        act(bigs, (lutb, firstu), Fn.Copy)
+        mark("f%d" % t)
+        iota(nk, [[-1, 64], [0, 4]], -n)
+        act(nks, (nk, sigu), Fn.Copy)
+        mark("f%d" % t)
+        act(sub(ew, 0, n), sub(ones, 0, n), Fn.Copy, scale=256.0)
+        scatter(sub(ew, 0, n + 256), endo, sub(jf, 0, 256))
+        scan(hs, sub(m16, 0, n), sub(ew, 0, n), Op.mult, Op.add)
+        ts(sub(endu, 0, k), sub(hs, 15, n, 16), s16, Op.mult, 0.25, Op.add)
+        mark("e%d" % t)
+        act(sn, (s, nu), Fn.Copy)
+        mark("s%d" % t)
+        cp(V(X, 4 * n, 4 * n + 128), (nm("dd", 0, 4 * n), nm("ll", 0, 8)))
+        act(V(X, 4 * n + 128, 4 * n + 256), (nm("dd", 0, 4 * n), nm("ll", 8, 16)), Fn.Copy)
+        quant(nm("qh", 0, 128), nm("sh", 0, 128), V(X, 4 * n - 256, 4 * n + 256))
+        z = sub(mm(2, qr, sr, nm("qh", 0, 128), nm("sh", 0, 128)), 64, 128)
+        act(V(XH, 4 * n, 4 * n2), V(X, 4 * n, 4 * n2), Fn.Copy, scale=0.5)
+        act(nm("xo", 4 * n, 4 * n2), V(X, 4 * n, 4 * n2), Fn.Copy, scale=0.5)
+        d, gap, cost, mn, gs = [new("wf", 256) for i in range(5)]
+        for i in range(4):
+            tt(sub(d, i, 256, 4), sub(sn, i, 256, 4), z, Op.subtract)
+        act(gap, d, Fn.Abs)
+        tt(cost, (cc, nu), gap, Op.max)
+        scan(mn, big4, cost, Op.add, Op.min)
+        pr = sub(pc, n, n + 256)
+        tt(pr, (mn, rep4), gap, Op.max)
+        nxt = nxts[t]
+        d1, ex, f, v, mn2 = [new("wf", 256) for i in range(5)]
+        pw = new("wi", 128)
+        act(d1, (pc, d1u), Fn.Copy)
+        act(mn2, mn, Fn.Copy)
+        tt(sub(gt, 8, 264), (mn, rep4), mn2, Op.is_lt)
+        scan(gs, sub(gt, 7, 263), pk, Op.max, Op.min)
+        ts(sub(pw, 0, 64), sub(gs, 3, 256, 4), 2.0 ** 17, Op.mult)
+        ts(sub(pw, 64, 128), sub(pw, 0, 64), 511, Op.bitwise_and)
+        ts(sub(nxt, n, n2), sub(pw, 64, 128), -1.0, Op.mult)
+        scan(ex, bigs, d1, Op.add, Op.min)
+        tt(f, (pr, sigu), ex, Op.is_lt)
+        tt(v, f, nks, Op.mult)
+        scan(sub(vs, 0, 256), bigs, v, Op.add, Op.min)
+        for a, b in ((0, ch2[1]), (ch2[1], n)):
+            tt(sub(nxt, a, b), (vs, sub(endu, a // 16, b // 16)), sub(negp, a, b), Op.min)
+        negp = nxt
+        yo, hs = new("wu", n2 // 4), new("wf", n2)
+        for c in range(2):
+            a, b = ch2[c], ch2[c + 1]
+            scan(sub(hs, a, b), sub(m4, a, b), sub(negp, a, b), Op.mult, Op.add)
+            ts(sub(yo, a // 4, b // 4), sub(hs, a + 3, b, 4), s4n, Op.mult, qto, Op.add)
+            mid = (a + b) // 2
+            for lo, hi in ((a, mid), (mid, b)):
+                tt(nm("yt", 4 * lo, 4 * hi), (V(XH, 0, 4 * n2), sub(yo, lo // 4, hi // 4)), nm("xo", 4 * lo, 4 * hi), Op.add)
+            quant(nm("qy", a, b), nm("sy", a, b), nm("yt", 4 * a, 4 * b))
+            mark("q%d" % t)
+            for e in range(4):
+                p = mm(4 * c + e, V("wq", 128 * e, 128 * e + 128), V("wsc", 128 * e, 128 * e + 128), nm("qy", a, b), nm("sy", a, b))
+                r = nm("ru", 4 * a + e, 4 * b, 4)
+                act(r, p, Fn.Relu, scale=0.03125)
+                if c:
+                    tt(V(XN, 4 * a + e, 4 * b, 4), r, V(X, 4 * a + e, 4 * b, 4), Op.add)
+            if c == 0:
+                heap(V(XN, 0, 4 * b), nm("ru", 0, 4 * b), LAT[2])
+
+    act(whole("osb"), negp, Fn.Copy, scale=-1.0)
+    dma("s", lambda: g.sync.dma_start(T.op[:], T.osb[0:128:16, :]), [whole("osb")], [], 2000)
+    for c in range(2):
+        a, b = CHUNKS[2][c], CHUNKS[2][c + 1]
+        quant(V("qx2", a, b), V("sx2", a, b), V("x2", 4 * a, 4 * b))
+        p = mm(c, whole("qv"), whole("sv"), V("qx2", a, b), V("sx2", a, b))
+        if c:
+            cp(V("ysb", a, b), p)
+        else:
+            act(V("ysb", a, b), p, Fn.Copy)
+        dma("s", lambda a=a, b=b: g.sync.dma_start(T.oc[:, 4 * a:4 * b], T.qx2[:, a:b].bitcast(dt.uint8)), [V("qx2", a, b)], [], 2300)
+        dma("s", lambda a=a, b=b: g.sync.dma_start(T.y[:, a:b], T.ysb[:, a:b]), [V("ysb", a, b)], [], 2300)
+    for j in range(4):
+        dma("a", lambda j=j: g.scalar.dma_start(T.osc[4 * j:4 * j + 4, :], T.sx2[32 * j:32 * j + 4, :]), [whole("sx2")], [], 2000)
+    return ops

@@ -9,8 +9,8 @@ KEEP = 4096.0
 X4 = "float8_e4m3fn_x4"
 
 SCRATCH = {
-    "wf": ("sbuf", [128, 14848], "float32"), "wb": ("sbuf", [128, 18432], "bfloat16"),
-    "wi": ("sbuf", [128, 512], "int32"), "wu": ("sbuf", [128, 768], "uint16"),
+    "wf": ("sbuf", [128, 15872], "float32"), "wb": ("sbuf", [128, 18432], "bfloat16"),
+    "wi": ("sbuf", [128, 640], "int32"), "wu": ("sbuf", [128, 768], "uint16"),
     "ps": ("psum", [128, 4096], "float32"),
     "pai": ("sbuf", [128, 22], "int32"), "nri": ("sbuf", [128, 32], "int32"),
     "ub": ("sbuf", [128, 512], "bfloat16"), "vb": ("sbuf", [128, 512], "bfloat16"),
@@ -43,12 +43,13 @@ for _t in range(2):
 SEMAPHORES = (["ev", "ea", "ep", "eg", "sent"] + ["dm%d" % _i for _i in range(28)]
               + ["%s%d" % (_s, _t) for _s in ("rc", "rp", "rn", "aq", "an") for _t in range(2)])
 
-CY, WAKE = 1.04, 90.0
-LAT = (9000.0, 4000.0, 2500.0)
-NA = (5, 6, 0)
-EARLY = {"k0": 3000, "p0": 5000, "o1": 5000, "e1": 3000, "o0": 2000, "q1": 12000, "p1": 2000, "s0": 5000, "u10": 2000, "e0": 1000,
-         "h0": 300, "s1": 2000, "u00": 1000, "d1": 8000, "d0": 300, "u01": 300, "f0": 2000, "u02": 300, "q0": 600, "v": 600,
-         "x1": 5000, "u11": 300, "k1": 2000, "u12": 1000}
+CY, WAKE = 0.92, 170.0
+LAT = (9000.0, 5000.0, 2500.0)
+PIECES = 2
+NA = (5, 6)
+EARLY = {"k0": 300, "p0": 600, "o1": 2000, "e1": 3000, "p1": 8000, "u10": 5000, "e0": 2000, "h0": 5000, "s1": 8000, "d1": 2000, "d0": 600,
+         "u01": 3000, "f0": 300, "u02": 1500, "v": 8000, "x1": 5000, "u11": 1500, "u12": 1500, "h1": 1500, "u15": 600, "u13": 300,
+         "q01": 600, "u17": 300, "q00": 1500, "n1": 2000, "u03": 600, "u14": 300, "o0": 1500, "f1": 600}
 
 
 def relays_of(T, topo, r):
@@ -368,8 +369,8 @@ def plan(g, core, T, topo, rank, room):
         act(sub(mr[h], 0, 16), poff, Fn.Copy)
         act(sub(mr[h], 16, h), sub(ones, 16, h), Fn.Copy)
         ts(sub(mr[h], h, h + 16), pdiag, KEEP, Op.mult, 1.0, Op.max)
-    lut64, lutb, pick = new("wb", 208), new("wf", 8), new("wf", 256)
-    ts(lut64, sub(jc, 0, 208), -192.0, Op.is_lt)
+    lut64, lutb, pick = new("wb", 416), new("wf", 8), new("wf", 256)
+    ts(lut64, jf, 128.0, Op.is_lt)
     act(lutb, sub(jf, 0, 8), Fn.Copy, scale=BIG)
     m16i, xi, xf, kh, rep4, picki = new("wi", 16), new("wi", 16), new("wf", 16), new("wf", 4), new("wu", 16), new("wf", 256)
     iota(m16i, [[16, 16]])
@@ -396,10 +397,9 @@ def plan(g, core, T, topo, rank, room):
     cp(nru, whole("nri"))
     ts(nrf, whole("nri"), 256.0, Op.mult)
 
-    def ranks(row, h, na, out):
+    def ranks(row, msk, h, na, out, times):
         k = h // 16
-        msk, lst = new("wf", h), new("wf", h)
-        tt(msk, row, sub(diag, 0, h), Op.mult)
+        lst = new("wf", h)
         scan(lst, sub(off16, 0, h), msk, Op.mult, Op.add)
         at = lambda m: sub(lst, 16 * m + 15, 16 * m + 16)
         nv, w = k - na, h + 16
@@ -409,11 +409,10 @@ def plan(g, core, T, topo, rank, room):
             ts(sub(f, 0, h - 16 * m), sub(row, 16 * m, h), at(m), Op.is_lt)
             ts(sub(f, h - 16 * m, w), sub(row, 0, 16 * m + 16), at(m), Op.is_le)
             scan(sub(cnt, m * w, m * w + w), mr[h], f, Op.mult, Op.add)
-        ts(sub(out, 0, nv), sub(cnt, w - 1, nv * w, w), 1.0 / KEEP, Op.mult, 0.25, Op.add)
+        ts(sub(out, 0, nv), sub(cnt, w - 1, nv * w, w), times / KEEP, Op.mult, 0.25, Op.add)
         if na:
             sg, junk, acc = new("wb", na * h), new("wb", na * h), new("wf", 32)
-            ib, ibs, t1 = new("wb", 16 * na), new("wb", 16 * na), new("wf", 48)
-            fill(sub(acc, 16 + na - 1, 16 + na), 0.0)
+            ib, ibs, t1 = new("wb", 16 * na), new("wb", 16 * na), new("wf", 16)
             for a in range(na):
                 m = nv + a
                 y = sub(sg, a * h, a * h + h)
@@ -423,10 +422,12 @@ def plan(g, core, T, topo, rank, room):
                     act(sub(junk, a * h + 16 * m + 16, a * h + h), sub(y, 16 * m + 16, h), Fn.Sign, bias=col(15), acc=sub(acc, 16 + a, 17 + a))
                 tt(sub(ib, 16 * a, 16 * a + 16), sub(y, 16 * m, 16 * m + 16), w16, Op.is_gt)
             scan(ibs, sub(ns16, 0, 16 * na), ib, Op.mult, Op.add)
-            ts(sub(t1, 0, na), sub(ibs, 15, 16 * na, 16), 2.0, Op.mult, float(h - 16), Op.add)
-            tt(sub(t1, 16, 16 + na), sub(acc, 0, na), sub(acc, 16, 16 + na), Op.add)
-            tt(sub(t1, 32, 32 + na), sub(t1, 0, na), sub(t1, 16, 16 + na), Op.add)
-            ts(sub(out, nv, k), sub(t1, 32, 32 + na), 0.5, Op.mult, 0.25, Op.add)
+            ts(sub(t1, 0, na), sub(ibs, 15, 16 * na, 16), 2.0, Op.mult, h - 15.75, Op.add)
+            for a in range(na):
+                if a < na - 1:
+                    ts(sub(out, nv + a, nv + a + 1), sub(t1, a, a + 1), sub(acc, a, a + 1), Op.add, sub(acc, 16 + a, 17 + a), Op.add)
+                else:
+                    ts(sub(out, nv + a, nv + a + 1), sub(t1, a, a + 1), sub(acc, a, a + 1), Op.add)
 
     negp, nxts = new("wf", NS[0]), [new("wf", NS[1]), new("wf", NS[2])]
     ups = [[new("wb", n), new("wb", n), new("wb", n), new("wb", n)] for n in NS[:2]]
@@ -456,7 +457,7 @@ def plan(g, core, T, topo, rank, room):
                 act(sub(up[(i + 1) % 2], 0, lo2), sub(ones, 0, lo2), Fn.Copy, scale=-256.0)
             scan(sub(hs, lo2, n), sub(m16, lo2, n), sub(up[(i + 1) % 2], lo2, n), Op.mult, Op.add)
             ts(sub(lists[i + 1], lo2 // 16, k), sub(hs, lo2 + 15, n, 16), s16, Op.mult, 256.25, Op.add)
-            mark("u%d%d" % (t, i // 3))
+            mark("u%d%d" % (t, i))
         s, s2 = new("wf", n), new("wf", n)
         sends = []
         for c in range(2):
@@ -495,11 +496,14 @@ def plan(g, core, T, topo, rank, room):
                     a = max(a, low[i + 1])
                     if a < b:
                         act(sub(twin[(i + 1) % 2], a, b), sub(cb[(i + 1) % 2], a, b), Fn.Copy)
+                        mark("t%d" % t)
         cc = cb[1]
         h = n // 2
         win, rk = new("wf", h), new("wu", 16)
         tt(win, sub(cc, 0, n, 2), sub(cc, 1, n, 2), Op.min)
-        ranks(win, h, NA[t], rk)
+        msk = new("wf", h)
+        tt(msk, win, sub(diag, 0, h), Op.mult)
+        ranks(win, msk, h, NA[t], rk, 2.0)
         flag, pre, fl, cnt, acc, ou = new("wb", h), new("wb", h), new("wb", 4 * h), new("wb", 2 * h), new("wf", 2), new("wu", 8)
         cp(flag, (lut64, sub(rk, 0, h // 16)))
         scan(pre, sub(ones, 0, h), flag, Op.mult, Op.add)
@@ -511,11 +515,13 @@ def plan(g, core, T, topo, rank, room):
             ts(sub(ou, 4 * e, 4 * e + 2), sub(cnt, h - 1, 2 * h, h), 2.0, Op.mult, e + 0.25, Op.add)
             ts(sub(ou, 4 * e + 2, 4 * e + 4), acc, h + e + 0.25, Op.add)
         c2, j2, rk2, srt, hs = new("wf", 128), new("wf", 128), new("wu", 8), new("wf", 128), new("wf", 64)
-        cp(sub(c2, 0, 128, 2), (cc, sub(ou, 0, 4)))
-        act(sub(c2, 1, 128, 2), (cc, sub(ou, 4, 8)), Fn.Copy)
+        msk = new("wf", 128)
+        for e in range(2):
+            tt(sub(msk, e, 128, 2), (cc, sub(ou, 4 * e, 4 * e + 4)), sub(diag, e, 128, 2), Op.mult)
+            act(sub(c2, e, 128, 2), (cc, sub(ou, 4 * e, 4 * e + 4)), Fn.Copy)
         for e in range(2):
             act(sub(j2, e, 128, 2), (sub(jf, 0, n), sub(ou, 4 * e, 4 * e + 4)), Fn.Copy)
-        ranks(c2, 128, NA[2], rk2)
+        ranks(c2, msk, 128, 0, rk2, 1.0)
         scatter(srt, rk2, j2)
         scan(hs, sub(m4, 0, 64), sub(srt, 0, 64), Op.mult, Op.add)
         ts(nm("el", 0, 16), sub(hs, 3, 64, 4), s4p, Op.mult, qto, Op.add)
@@ -538,12 +544,13 @@ def plan(g, core, T, topo, rank, room):
         ko, ks, kk, sh, an = new("wu", 16), new("wf", 272), new("wi", 48), new("wi", 48), new("wi", 32)
         ts(ko, acc, 0.5, Op.mult, 127.75, Op.add)
         mark("k%d" % t)
-        nk, ew, vs, gt = new("wf", 256), new("wf", NS[1] + 256), new("wf", 272), new("wf", 272)
+        nk, ew, vs, gt, gz = new("wf", 256), new("wf", NS[1] + 256), new("wf", 272), new("wf", 272), new("wf", 272)
         if t == 0:
             fill(sub(ks, 0, 8), -256.0)
             fill(sub(ks, 264, 272), 600.0 * 256)
             fill(sub(vs, 256, 272), 0.0)
             fill(sub(gt, 0, 8), 1.0)
+            fill(sub(gz, 256, 272), 0.0)
         scatter(sub(ks, 8, 264), ko, krow)
         for e, d in enumerate((0, -1, 1)):
             hs = new("wf", 256)
@@ -557,13 +564,21 @@ def plan(g, core, T, topo, rank, room):
         sigu, firstu, d1u, endo, endu = new("wu", 16), new("wu", 16), new("wu", 16), new("wu", 16), new("wu", 32)
         cp(sigu, sub(an, 0, 16))
         cp(firstu, first)
-        for out, bs, flg in ((d1u, sub(an, 16, 32), first), (endo, xi, last)):
+        a4, s3u, gdu, w = new("wi", 32), new("wu", 16), new("wu", 16), new("wi", 48)
+        ts(a4, sub(kk, 0, 32), 252, Op.bitwise_and)
+        ts(s3u, sub(a4, 0, 16), 3.0, Op.add)
+        ts(sub(w, 0, 16), sub(an, 16, 32), -1.0, Op.mult, 256.0, Op.add)
+        tt(sub(w, 16, 32), sub(w, 0, 16), first, Op.mult)
+        tt(sub(w, 32, 48), sub(w, 16, 32), sub(an, 16, 32), Op.add)
+        cp(gdu, sub(w, 32, 48))
+        mark("f%d" % t)
+        for out, bs, flg, far in ((d1u, sub(a4, 16, 32), first, n + 3.0), (endo, xi, last, n + 0.0)):
             w = new("wi", 64)
             tt(sub(w, 0, 16), plc, bs, Op.subtract)
-            ts(sub(w, 16, 32), sub(w, 0, 16), float(-n), Op.add)
+            ts(sub(w, 16, 32), sub(w, 0, 16), -far, Op.add)
             tt(sub(w, 32, 48), sub(w, 16, 32), flg, Op.mult)
             tt(sub(w, 48, 64), sub(w, 32, 48), bs, Op.add)
-            ts(out, sub(w, 48, 64), float(n), Op.add)
+            ts(out, sub(w, 48, 64), far, Op.add)
             mark("f%d" % t)
         bigs, nks, hs, sn = new("wf", 256), new("wf", 256), new("wf", n), new("wf", 256)
         act(bigs, (lutb, firstu), Fn.Copy)
@@ -584,26 +599,29 @@ def plan(g, core, T, topo, rank, room):
         z = sub(mm(2, qr, sr, nm("qh", 0, 128), nm("sh", 0, 128)), 64, 128)
         act(V(XH, 4 * n, 4 * n2), V(X, 4 * n, 4 * n2), Fn.Copy, scale=0.5)
         act(nm("xo", 4 * n, 4 * n2), V(X, 4 * n, 4 * n2), Fn.Copy, scale=0.5)
-        d, gap, cost, mn, gs = [new("wf", 256) for i in range(5)]
+        d, cost, gs, pr, gd, ga = [new("wf", 256) for i in range(6)]
+        gap, mn = sub(gz, 0, 256), sub(pc, n, n + 256)
         for i in range(4):
             tt(sub(d, i, 256, 4), sub(sn, i, 256, 4), z, Op.subtract)
-        act(gap, d, Fn.Abs)
+            act(sub(gap, i, 256, 4), sub(d, i, 256, 4), Fn.Abs)
         tt(cost, (cc, nu), gap, Op.max)
         scan(mn, big4, cost, Op.add, Op.min)
-        pr = sub(pc, n, n + 256)
-        tt(pr, (mn, rep4), gap, Op.max)
+        act(gd, (gz, gdu), Fn.Copy)
+        act(ga, (gz, sigu), Fn.Copy)
         nxt = nxts[t]
         d1, ex, f, v, mn2 = [new("wf", 256) for i in range(5)]
         pw = new("wi", 128)
-        act(d1, (pc, d1u), Fn.Copy)
+        tt(d1, (pc, d1u), gd, Op.max)
+        tt(pr, (mn, s3u), ga, Op.max)
         act(mn2, mn, Fn.Copy)
         tt(sub(gt, 8, 264), (mn, rep4), mn2, Op.is_lt)
         scan(gs, sub(gt, 7, 263), pk, Op.max, Op.min)
         ts(sub(pw, 0, 64), sub(gs, 3, 256, 4), 2.0 ** 17, Op.mult)
         ts(sub(pw, 64, 128), sub(pw, 0, 64), 511, Op.bitwise_and)
         ts(sub(nxt, n, n2), sub(pw, 64, 128), -1.0, Op.mult)
+        mark("n%d" % t)
         scan(ex, bigs, d1, Op.add, Op.min)
-        tt(f, (pr, sigu), ex, Op.is_lt)
+        tt(f, pr, ex, Op.is_lt)
         tt(v, f, nks, Op.mult)
         scan(sub(vs, 0, 256), bigs, v, Op.add, Op.min)
         for a, b in ((0, ch2[1]), (ch2[1], n)):
@@ -614,11 +632,11 @@ def plan(g, core, T, topo, rank, room):
             a, b = ch2[c], ch2[c + 1]
             scan(sub(hs, a, b), sub(m4, a, b), sub(negp, a, b), Op.mult, Op.add)
             ts(sub(yo, a // 4, b // 4), sub(hs, a + 3, b, 4), s4n, Op.mult, qto, Op.add)
-            mid = (a + b) // 2
-            for lo, hi in ((a, mid), (mid, b)):
+            cuts = [a + (b - a) * j // PIECES // 8 * 8 for j in range(PIECES)] + [b]
+            for lo, hi in zip(cuts, cuts[1:]):
                 tt(nm("yt", 4 * lo, 4 * hi), (V(XH, 0, 4 * n2), sub(yo, lo // 4, hi // 4)), nm("xo", 4 * lo, 4 * hi), Op.add)
             quant(nm("qy", a, b), nm("sy", a, b), nm("yt", 4 * a, 4 * b))
-            mark("q%d" % t)
+            mark("q%d%d" % (t, c))
             for e in range(4):
                 p = mm(4 * c + e, V("wq", 128 * e, 128 * e + 128), V("wsc", 128 * e, 128 * e + 128), nm("qy", a, b), nm("sy", a, b))
                 r = nm("ru", 4 * a + e, 4 * b, 4)

@@ -2,15 +2,19 @@ from concourse.mybir import dt, AluOpType as Op, ActivationFunctionType as Fn
 
 C, A = 352, 64
 NS = (C, C + A, C + 2 * A)
-CHUNKS = ((0, 176, 352), (0, 224, 416), (0, 256, 480))
+RUNS = ((0, 176, 352), (0, 208, 416))
+CHUNKS = ((0, 176, 352), (0, 160, 288, 416), (0, 192, 352, 480))
+BY_DMA = ((0,), (0,))
 BIG = 2.0 ** 90
 HOLD = 2.0 ** 24
 KEEP = 4096.0
+NONE = -0.53125
 X4 = "float8_e4m3fn_x4"
+DMAS = 40
 
 SCRATCH = {
-    "wf": ("sbuf", [128, 15872], "float32"), "wb": ("sbuf", [128, 18432], "bfloat16"),
-    "wi": ("sbuf", [128, 640], "int32"), "wu": ("sbuf", [128, 768], "uint16"),
+    "wf": ("sbuf", [128, 15360], "float32"), "wb": ("sbuf", [128, 29696], "bfloat16"),
+    "wi": ("sbuf", [128, 1024], "int32"), "wu": ("sbuf", [128, 1024], "uint16"),
     "ps": ("psum", [128, 4096], "float32"),
     "pai": ("sbuf", [128, 22], "int32"), "nri": ("sbuf", [128, 32], "int32"),
     "ub": ("sbuf", [128, 512], "bfloat16"), "vb": ("sbuf", [128, 512], "bfloat16"),
@@ -40,16 +44,20 @@ for _t in range(2):
         "el%d" % _t: ("sbuf", [128, 16], "uint16"), "rl%d" % _t: ("sbuf", [128, 16], "uint16"),
         "ll%d" % _t: ("sbuf", [128, 16], "uint16"),
     })
-SEMAPHORES = (["ev", "ea", "ep", "eg", "sent"] + ["dm%d" % _i for _i in range(28)]
+SEMAPHORES = (["ev", "ea", "ep", "eg", "sent"] + ["dm%d" % _i for _i in range(DMAS)]
               + ["%s%d" % (_s, _t) for _s in ("rc", "rp", "rn", "aq", "an") for _t in range(2)])
 
 CY, WAKE = 0.92, 170.0
 LAT = (9000.0, 5000.0, 2500.0)
-PIECES = 2
-NA = (5, 6)
-EARLY = {"k0": 300, "p0": 600, "o1": 2000, "e1": 3000, "p1": 8000, "u10": 5000, "e0": 2000, "h0": 5000, "s1": 8000, "d1": 2000, "d0": 600,
-         "u01": 3000, "f0": 300, "u02": 1500, "v": 8000, "x1": 5000, "u11": 1500, "u12": 1500, "h1": 1500, "u15": 600, "u13": 300,
-         "q01": 600, "u17": 300, "q00": 1500, "n1": 2000, "u03": 600, "u14": 300, "o0": 1500, "f1": 600}
+PIECES = 1
+SCALAR = (((3, 2), (1, 2)), ((3, 3), (1, 2)))
+JUMPS = ("vaaaaaaa", "aaaaaaaa")
+LOW = 5
+SCORES = ("v", "v")
+EARLY = {"u14": 1000, "c02": 5000, "y01": 300, "q12": 1500, "u06": 2000, "u10": 150, "u16": 1000, "r01": 1000, "c07": 1000, "y11": 1000,
+         "u05": 600, "y02": 1000, "q02": 300, "q01": 1500, "x1": 600, "c03": 1000, "y12": 300, "c06": 150, "r00": 600, "s0": 5000,
+         "c05": 1500, "u08": 1000, "c01": 300, "r02": 150, "r11": 150, "u04": 5000, "k0": 150, "q11": 150, "f0": 150, "u11": 2000,
+         "u02": 1000, "c16": 600, "u07": 150, "r12": 600, "c00": 300}
 
 
 def relays_of(T, topo, r):
@@ -64,7 +72,7 @@ def relay_program(g, core, T, topo, r, k):
     nin = len(topo.engines(T.cores[r], core))
     calls = 0
     for t in range(2):
-        a, b = CHUNKS[t][k], CHUNKS[t][k + 1]
+        a, b = RUNS[t][k], RUNS[t][k + 1]
         g.wait_ge(T.sem["rc%d" % t], nin)
         g.remote_dma(T["lq%d" % t][:, a:b].bitcast(dt.uint8), T["rq%d" % t][:, 0:b - a].bitcast(dt.uint8), T.sem["aq%d" % t], T.sem.sent, pid, rid, m)
         g.wait_ge(T.sem["rp%d" % t], nin)
@@ -198,7 +206,7 @@ def plan(g, core, T, topo, rank, room):
         lo, w = top[kind], (n + 15) // 16 * 16
         if turn[0] is not None:
             turn[0] += 1
-            w = room[turn[0]] = max(room.get(turn[0], 0), w)
+            w = room[(kind, turn[0])] = max(room.get((kind, turn[0]), 0), w)
         top[kind] = lo + w
         return V(kind, lo, lo + n)
 
@@ -246,8 +254,8 @@ def plan(g, core, T, topo, rank, room):
     def scatter(win, off, a):
         add("v", "c", lambda: g.vector.tensor_copy(ap((win, off)), ap(a)), [a, off], [win], 50 + 3.8 * CY * size(a))
 
-    def scan(out, d0, d1, op0, op1):
-        add("v", "c", lambda: g.vector.tensor_tensor_scan(ap(out), ap(d0), ap(d1), 0.0, op0, op1), [d0, d1], [out], price(out, [d0, d1]))
+    def scan(out, d0, d1, op0, op1, first=0.0):
+        add("v", "c", lambda: g.vector.tensor_tensor_scan(ap(out), ap(d0), ap(d1), first, op0, op1), [d0, d1], [out], price(out, [d0, d1]))
 
     def fill(out, k):
         add("v", "c", lambda: g.vector.memset(ap(out), k), [], [out], price(out, []))
@@ -262,6 +270,12 @@ def plan(g, core, T, topo, rank, room):
             kw["accum_out"] = ap(acc)
         cost = 65 + 1.56 * CY * size(out) if len(a) == 2 else CY * max(64, size(out)) + (20 if acc else 0)
         add("a", "c", lambda: g.scalar.activation(ap(out), ap(a), f, **kw), [a, bias, scale], [out] + ([acc] if acc else []), cost)
+
+    def move(who, out, a):
+        if who == "v":
+            cp(out, a)
+        else:
+            act(out, a, Fn.Copy)
 
     def iota(out, pattern, base=0, cm=0):
         if SCRATCH[out[0]][2] == "int32":
@@ -280,6 +294,9 @@ def plan(g, core, T, topo, rank, room):
 
     def dma(q, fn, r, w, lat):
         add(q, "d", fn, r, w, 60, lat)
+
+    def twin(out, a):
+        dma("s", lambda: g.sync.dma_start(ap(out), ap(a)), [a], [out], 2500)
 
     def heap(out, a, lat):
         add("g", "d", lambda: g.dma_start(ap(out), ap(a), accum_op=Op.add), [a, out], [out], 700, lat)
@@ -317,19 +334,22 @@ def plan(g, core, T, topo, rank, room):
     col = lambda k: sub(cf, k, k + 1)
     fill(col(14), 0.5)
     fill(col(15), -0.5)
-    fill(col(12), -256.0)
+    fill(col(12), 256.0)
     iota(pi, [[1, 1]], 0, 1)
     ts(sub(cols, 0, 1), pi, 15, Op.bitwise_and)
     ts(sub(cols, 1, 2), pi, 2, Op.logical_shift_right, 3, Op.bitwise_and)
     ts(sub(cols, 2, 3), pi, 3, Op.bitwise_and)
     cp(sub(cf, 0, 3), sub(cols, 0, 3))
-    q16, q4, qt, q16n, q4n, s16, s4p, s4n, qto = [col(k) for k in range(9)]
+    q16, q4, qt, q16n, q4n, s16, s4p, s4y, qto, s16y, s4, qty = [col(k) for k in range(12)]
     ts(sub(cf, 3, 5), sub(cf, 0, 2), 1.0, Op.add)
     ts(s16, q16, 15.0, Op.is_equal, 1.0 / HOLD, Op.max)
-    ts(col(10), q4, 3.0, Op.is_equal, 1.0 / HOLD, Op.max)
-    ts(s4p, col(10), 4.0, Op.mult)
-    ts(s4n, col(10), -4.0, Op.mult)
+    ts(s16y, s16, 512.0, Op.mult)
+    ts(col(13), s16, 2.0, Op.mult)
+    ts(s4, q4, 3.0, Op.is_equal, 1.0 / HOLD, Op.max)
+    ts(s4p, s4, 4.0, Op.mult)
+    ts(s4y, s4, 2048.0, Op.mult)
     ts(qto, qt, 0.25, Op.add)
+    ts(qty, qt, 1024.25, Op.add)
     jf, jc, rr = new("wf", 416), new("wb", 352), new("wb", 32)
     r16, r4 = sub(rr, 0, 16), sub(rr, 16, 32)
     iota(r16, [[1, 16]])
@@ -341,12 +361,9 @@ def plan(g, core, T, topo, rank, room):
     qoff = new("wu", 30)
     ts(qoff, sub(ones, 0, 30), q16, Op.mult)
 
-    def spread(p, n, on_vector=False):
+    def spread(p, n, who="a"):
         m = new(p[0], n)
-        if on_vector:
-            cp(m, (p, sub(qoff, 0, n // 16)))
-        else:
-            act(m, (p, sub(qoff, 0, n // 16)), Fn.Copy)
+        move(who, m, (p, sub(qoff, 0, n // 16)))
         return m
 
     def hold(r, q, qn):
@@ -362,23 +379,24 @@ def plan(g, core, T, topo, rank, room):
     ts(w16, r16, q16, Op.is_ge, -0.5, Op.add)
     ts(pns, r16, 0.0, Op.not_equal)
     ts(pbig, r4, 0.0, Op.is_equal, BIG, Op.mult)
-    m16, m4, off16, diag, ns16, big4 = spread(p16, 416, True), spread(p4, 480), spread(poff, 208), spread(pdiag, 208), spread(pns, 128), spread(pbig, 256)
+    m16, m4, off16, diag = spread(p16, 416), spread(p4, 480), spread(poff, 208), spread(pdiag, 208)
+    most = 16 * max(sum(x) for y in SCALAR for x in y)
+    ns16, ws16, big4 = spread(pns, most), spread(w16, most), spread(pbig, 256)
     mr = {}
     for h in (176, 208, 128):
         mr[h] = new("wb", h + 16)
         act(sub(mr[h], 0, 16), poff, Fn.Copy)
         act(sub(mr[h], 16, h), sub(ones, 16, h), Fn.Copy)
         ts(sub(mr[h], h, h + 16), pdiag, KEEP, Op.mult, 1.0, Op.max)
-    lut64, lutb, pick = new("wb", 416), new("wf", 8), new("wf", 256)
+    lut64, lutb, lutn, pick = new("wb", 416), new("wb", 16), new("wb", 16), new("wf", 256)
     ts(lut64, jf, 128.0, Op.is_lt)
-    act(lutb, sub(jf, 0, 8), Fn.Copy, scale=BIG)
-    m16i, xi, xf, kh, rep4, picki = new("wi", 16), new("wi", 16), new("wf", 16), new("wf", 4), new("wu", 16), new("wf", 256)
+    ts(lutb, sub(jf, 0, 16), -BIG, Op.mult, BIG, Op.add)
+    ts(lutn, sub(jf, 0, 16), NONE - 1.0, Op.mult, 1.0, Op.add)
+    m16i, xi, xf, kh, picki = new("wi", 16), new("wi", 16), new("wf", 16), new("wf", 4), new("wf", 256)
     iota(m16i, [[16, 16]])
     ts(xf, m16i, q16, Op.add)
     cp(xi, xf)
     ts(kh, sub(xf, 0, 4), 0.5, Op.add)
-    ts(col(13), q4, 4.0, Op.mult, 3.0, Op.add)
-    ts(rep4, m16i, col(13), Op.add)
     iota(picki, [[-2048, 64], [512, 4]], 63 * 2048)
     act(pick, picki, Fn.Copy, scale=2.0 ** -17)
     add("g", "c", lambda: g.affine_select(T.eye[:], T.one[:], [[1, 528]], Op.is_equal, 0.0, -3, -4), [ones], [whole("eye")], 170 + 2 * CY * 528)
@@ -397,140 +415,51 @@ def plan(g, core, T, topo, rank, room):
     cp(nru, whole("nri"))
     ts(nrf, whole("nri"), 256.0, Op.mult)
 
-    def ranks(row, msk, h, na, out, times):
-        k = h // 16
-        lst = new("wf", h)
-        scan(lst, sub(off16, 0, h), msk, Op.mult, Op.add)
+    def diagonals(h, lo, hi):
+        if not lo + hi:
+            return None
+        a, o = new("wf", lo + hi), new("wu", lo + hi)
+        for c0, c1, base in ((0, lo, 0), (lo, lo + hi, h - 16 * (lo + hi))):
+            if c1 > c0:
+                ts(sub(a, c0, c1), sub(jf, c0, c1), h + 16.0, Op.mult, float(base), Op.add)
+        ts(o, a, q16, Op.add)
+        return o
+    diags = {(h, x): diagonals(h, *x) for h, x in set([(NS[t] // 2, SCALAR[t][0]) for t in range(2)] + [(128, SCALAR[t][1]) for t in range(2)])}
+
+    def ranks(row, lst, h, share, out):
+        k, (lo, hi) = h // 16, share
         at = lambda m: sub(lst, 16 * m + 15, 16 * m + 16)
-        nv, w = k - na, h + 16
-        fl, cnt = new("wb", nv * w), new("wb", nv * w)
-        for m in range(nv):
-            f = sub(fl, m * w, m * w + w)
+        nv, na, w = k - lo - hi, lo + hi, h + 16
+        fl, cnt = new("wb", 9 * 224), new("wb", 9 * 224)
+        for i in range(nv):
+            m = lo + i
+            f = sub(fl, i * w, i * w + w)
             ts(sub(f, 0, h - 16 * m), sub(row, 16 * m, h), at(m), Op.is_lt)
             ts(sub(f, h - 16 * m, w), sub(row, 0, 16 * m + 16), at(m), Op.is_le)
-            scan(sub(cnt, m * w, m * w + w), mr[h], f, Op.mult, Op.add)
-        ts(sub(out, 0, nv), sub(cnt, w - 1, nv * w, w), times / KEEP, Op.mult, 0.25, Op.add)
+            scan(sub(cnt, i * w, i * w + w), mr[h], f, Op.mult, Op.add)
+        ts(sub(out, lo, lo + nv), sub(cnt, w - 1, nv * w, w), 2.0 / KEEP, Op.mult, 0.25, Op.add)
+        sg, junk, acc = new("wb", max(na, 1) * h), new("wb", max(na, 1) * h), new("wf", 32)
+        ib, ibs, t1 = new("wb", 128), new("wb", 128), new("wf", 16)
         if na:
-            sg, junk, acc = new("wb", na * h), new("wb", na * h), new("wf", 32)
-            ib, ibs, t1 = new("wb", 16 * na), new("wb", 16 * na), new("wf", 16)
-            for a in range(na):
-                m = nv + a
-                y = sub(sg, a * h, a * h + h)
-                act(y, row, Fn.Sign, bias=at(m), scale=-1.0)
-                act(sub(junk, a * h, a * h + 16 * m), sub(y, 0, 16 * m), Fn.Sign, bias=col(14), acc=sub(acc, a, a + 1))
-                if m < k - 1:
-                    act(sub(junk, a * h + 16 * m + 16, a * h + h), sub(y, 16 * m + 16, h), Fn.Sign, bias=col(15), acc=sub(acc, 16 + a, 17 + a))
-                tt(sub(ib, 16 * a, 16 * a + 16), sub(y, 16 * m, 16 * m + 16), w16, Op.is_gt)
-            scan(ibs, sub(ns16, 0, 16 * na), ib, Op.mult, Op.add)
+            ms = list(range(lo)) + list(range(k - hi, k))
+            for a, m in enumerate(ms):
+                act(sub(sg, a * h, a * h + h), row, Fn.Sign, bias=at(m), scale=-1.0)
+            tt(sub(ib, 0, 16 * na), (sg, diags[(h, share)]), sub(ws16, 0, 16 * na), Op.is_gt)
+            scan(sub(ibs, 0, 16 * na), sub(ns16, 0, 16 * na), sub(ib, 0, 16 * na), Op.mult, Op.add)
             ts(sub(t1, 0, na), sub(ibs, 15, 16 * na, 16), 2.0, Op.mult, h - 15.75, Op.add)
-            for a in range(na):
-                if a < na - 1:
-                    ts(sub(out, nv + a, nv + a + 1), sub(t1, a, a + 1), sub(acc, a, a + 1), Op.add, sub(acc, 16 + a, 17 + a), Op.add)
+            for a, m in enumerate(ms):
+                y, sums = sub(sg, a * h, a * h + h), []
+                for c0, c1, bias in ((0, 16 * m, col(14)), (16 * m + 16, h, col(15))):
+                    if c1 > c0:
+                        sums.append(sub(acc, 16 * len(sums) + a, 16 * len(sums) + a + 1))
+                        act(sub(junk, a * h + c0, a * h + c1), sub(y, c0, c1), Fn.Sign, bias=bias, acc=sums[-1])
+                if len(sums) == 2:
+                    ts(sub(out, m, m + 1), sub(t1, a, a + 1), sums[0], Op.add, sums[1], Op.add)
                 else:
-                    ts(sub(out, nv + a, nv + a + 1), sub(t1, a, a + 1), sub(acc, a, a + 1), Op.add)
+                    ts(sub(out, m, m + 1), sub(t1, a, a + 1), sums[0], Op.add)
 
-    negp, nxts = new("wf", NS[0]), [new("wf", NS[1]), new("wf", NS[2])]
-    ups = [[new("wb", n), new("wb", n), new("wb", n), new("wb", n)] for n in NS[:2]]
-    base = dict(top)
-    for t in range(2):
-        top.update(base)
-        turn[0] = 0
-        n, n2, ch, ch2 = NS[t], NS[t + 1], CHUNKS[t], CHUNKS[t + 1]
-        X, XH, XN = "x%d" % t, "xh%d" % t, "x%d" % (t + 1)
-        nm = lambda s, lo, hi, step=1, t=t: V("%s%d" % (s, t), lo, hi, step)
-        k = n // 16
-        lists = [new("wu", 32) for i in range(9)]
-        low = [0 if t or i < 5 else 2 ** i for i in range(9)]
-        up = ups[t]
-        if t == 0:
-            cp(sub(lists[0], 0, k), whole("pai"))
-            act(up[0], (jc, sub(lists[0], 0, k)), Fn.Copy)
-            act(negp, (sub(jf, 0, n), sub(lists[0], 0, k)), Fn.Copy, scale=-1.0)
-        else:
-            act(up[0], negp, Fn.Identity, bias=col(12), scale=-1.0)
-            scan(up[3], sub(m16, 0, n), up[0], Op.mult, Op.add)
-            ts(sub(lists[0], 0, k), sub(up[3], 15, n, 16), s16, Op.mult, 256.25, Op.add)
-        for i in range(8):
-            lo2, hs = low[i + 1], up[2 + i % 2]
-            act(sub(up[(i + 1) % 2], lo2, n), (up[i % 2], sub(lists[i], lo2 // 16, k)), Fn.Copy)
-            if lo2 and i < 7:
-                act(sub(up[(i + 1) % 2], 0, lo2), sub(ones, 0, lo2), Fn.Copy, scale=-256.0)
-            scan(sub(hs, lo2, n), sub(m16, lo2, n), sub(up[(i + 1) % 2], lo2, n), Op.mult, Op.add)
-            ts(sub(lists[i + 1], lo2 // 16, k), sub(hs, lo2 + 15, n, 16), s16, Op.mult, 256.25, Op.add)
-            mark("u%d%d" % (t, i))
-        s, s2 = new("wf", n), new("wf", n)
-        sends = []
-        for c in range(2):
-            a, b = ch[c], ch[c + 1]
-            quant(nm("qx", a, b), nm("sx", a, b), V(X, 4 * a, 4 * b))
-            mark("x%d" % t)
-            p = mm(c, qr, sr, nm("qx", a, b), nm("sx", a, b))
-            p2 = mm(2 + c, qr, sr, nm("qx", a, b), nm("sx", a, b))
-            cp(sub(s, a, b), p)
-            act(sub(s2, a, b), p2, Fn.Copy)
-            sends.append(hand(c, nm("rq", 0, b - a), nm("qx", a, b), "rc%d" % t, True))
-            sends.append(hand(c, nm("rs", 0, b - a), nm("sx", a, b), "rp%d" % t))
-        arrival(sends, [nm("lq", 0, n), nm("ls", 0, n)], "aq%d" % t, 4 * ne, LAT[0])
-        for j in range(4):
-            act(V(XH, j * n, j * n + n), V(X, j * n, j * n + n), Fn.Copy, scale=0.5)
-            mark("h%d" % t)
-            act(nm("xo", j * n, j * n + n), V(X, j * n, j * n + n), Fn.Copy, scale=0.5)
-            mark("o%d" % t)
-        dma("s", lambda o=V(XN, 0, 4 * ch2[1]), i=V(X, 0, 4 * ch2[1]): g.sync.dma_start(ap(o), ap(i)), [V(X, 0, 4 * ch2[1])], [V(XN, 0, 4 * ch2[1])], 2500)
-        pc, other, dif = new("wf", n + 256), new("wf", n), new("wf", n)
-        cb = [other, sub(pc, 0, n)]
-        twin = [new("wf", n), new("wf", n)]
-        halves = lambda lo: ((lo, (lo + n + 32) // 64 * 32), ((lo + n + 32) // 64 * 32, n))
-        for a, b in halves(0):
-            tt(sub(dif, a, b), (s, sub(lists[0], a // 16, b // 16)), sub(s2, a, b), Op.subtract)
-            act(sub(other, a, b), sub(dif, a, b), Fn.Abs)
-        for a, b in halves(0):
-            act(sub(twin[0], a, b), sub(dif, a, b), Fn.Abs)
-        for i in range(9):
-            if low[i]:
-                act(sub(cb[(i + 1) % 2], low[i - 1], low[i]), sub(cb[i % 2], low[i - 1], low[i]), Fn.Copy)
-            for a, b in halves(low[i]):
-                tt(sub(cb[(i + 1) % 2], a, b), (cb[i % 2], sub(lists[i], a // 16, b // 16)), sub(twin[i % 2], a, b), Op.max)
-            if i < 8:
-                for a, b in halves(low[i]):
-                    a = max(a, low[i + 1])
-                    if a < b:
-                        act(sub(twin[(i + 1) % 2], a, b), sub(cb[(i + 1) % 2], a, b), Fn.Copy)
-                        mark("t%d" % t)
-        cc = cb[1]
-        h = n // 2
-        win, rk = new("wf", h), new("wu", 16)
-        tt(win, sub(cc, 0, n, 2), sub(cc, 1, n, 2), Op.min)
-        msk = new("wf", h)
-        tt(msk, win, sub(diag, 0, h), Op.mult)
-        ranks(win, msk, h, NA[t], rk, 2.0)
-        flag, pre, fl, cnt, acc, ou = new("wb", h), new("wb", h), new("wb", 4 * h), new("wb", 2 * h), new("wf", 2), new("wu", 8)
-        cp(flag, (lut64, sub(rk, 0, h // 16)))
-        scan(pre, sub(ones, 0, h), flag, Op.mult, Op.add)
-        for u in range(2):
-            ts(sub(fl, u * h, u * h + h), pre, sub(kh, u, u + 1), Op.is_lt)
-            scan(sub(cnt, u * h, u * h + h), sub(ones, 0, h), sub(fl, u * h, u * h + h), Op.mult, Op.add)
-            act(sub(fl, (2 + u) * h, (3 + u) * h), pre, Fn.Sign, bias=sub(kh, 2 + u, 3 + u), scale=-1.0, acc=sub(acc, u, u + 1))
-        for e in range(2):
-            ts(sub(ou, 4 * e, 4 * e + 2), sub(cnt, h - 1, 2 * h, h), 2.0, Op.mult, e + 0.25, Op.add)
-            ts(sub(ou, 4 * e + 2, 4 * e + 4), acc, h + e + 0.25, Op.add)
-        c2, j2, rk2, srt, hs = new("wf", 128), new("wf", 128), new("wu", 8), new("wf", 128), new("wf", 64)
-        msk = new("wf", 128)
-        for e in range(2):
-            tt(sub(msk, e, 128, 2), (cc, sub(ou, 4 * e, 4 * e + 4)), sub(diag, e, 128, 2), Op.mult)
-            act(sub(c2, e, 128, 2), (cc, sub(ou, 4 * e, 4 * e + 4)), Fn.Copy)
-        for e in range(2):
-            act(sub(j2, e, 128, 2), (sub(jf, 0, n), sub(ou, 4 * e, 4 * e + 4)), Fn.Copy)
-        ranks(c2, msk, 128, 0, rk2, 1.0)
-        scatter(srt, rk2, j2)
-        scan(hs, sub(m4, 0, 64), sub(srt, 0, 64), Op.mult, Op.add)
-        ts(nm("el", 0, 16), sub(hs, 3, 64, 4), s4p, Op.mult, qto, Op.add)
-        sl = hand(0, nm("rl", 0, 16), nm("el", 0, 16), "rn%d" % t)
-        arrival([sl], [nm("ll", 0, 16)], "an%d" % t, ne, LAT[1])
-        for b in range(4):
-            p = mm(4 + b, V("qe", 128 * b, 128 * b + 128), V("se", 128 * b, 128 * b + 128), nm("lq", 0, n), nm("ls", 0, n))
-            act(nm("dd", b, 4 * n, 4), p, Fn.Copy)
-            mark("d%d" % t)
+    def near(t):
+        n = NS[t]
         nu = sub(nru, 16 * t, 16 * t + 16)
         pk, krow, klst, junk, acc = new("wf", 256), new("wf", 256), new("wf", 16), new("wb", 512), new("wf", 16)
         act(pk, (sub(jf, 0, n), nu), Fn.Copy, scale=2.0 ** -17)
@@ -541,56 +470,185 @@ def plan(g, core, T, topo, rank, room):
         tt(klst, sub(nrf, 16 * t, 16 * t + 16), xf, Op.add)
         for m in range(16):
             act(sub(junk, 256 * (m % 2), 256 * (m % 2) + 256), krow, Fn.Sign, bias=sub(klst, m, m + 1), scale=-1.0, acc=sub(acc, m, m + 1))
-        ko, ks, kk, sh, an = new("wu", 16), new("wf", 272), new("wi", 48), new("wi", 48), new("wi", 32)
+        ko, ks, kk, sh = new("wu", 16), new("wf", 272), new("wi", 48), new("wi", 48)
         ts(ko, acc, 0.5, Op.mult, 127.75, Op.add)
         mark("k%d" % t)
-        nk, ew, vs, gt, gz = new("wf", 256), new("wf", NS[1] + 256), new("wf", 272), new("wf", 272), new("wf", 272)
-        if t == 0:
-            fill(sub(ks, 0, 8), -256.0)
-            fill(sub(ks, 264, 272), 600.0 * 256)
-            fill(sub(vs, 256, 272), 0.0)
-            fill(sub(gt, 0, 8), 1.0)
-            fill(sub(gz, 256, 272), 0.0)
+        fill(sub(ks, 0, 8), -256.0)
+        fill(sub(ks, 264, 272), 600.0 * 256)
         scatter(sub(ks, 8, 264), ko, krow)
         for e, d in enumerate((0, -1, 1)):
             hs = new("wf", 256)
             scan(hs, sub(m16, 0, 256), sub(ks, 8 + d, 264 + d), Op.mult, Op.add)
             ts(sub(kk, 16 * e, 16 * e + 16), sub(hs, 15, 256, 16), s16, Op.mult)
         ts(sh, kk, 8, Op.arith_shift_right)
-        ts(an, sub(kk, 0, 32), 255, Op.bitwise_and)
-        plc, first, last = sub(sh, 0, 16), new("wi", 16), new("wi", 16)
+        plc, first, last, an = sub(sh, 0, 16), new("wi", 16), new("wi", 16), new("wi", 32)
         tt(first, plc, sub(sh, 16, 32), Op.not_equal)
         tt(last, plc, sub(sh, 32, 48), Op.not_equal)
-        sigu, firstu, d1u, endo, endu = new("wu", 16), new("wu", 16), new("wu", 16), new("wu", 16), new("wu", 32)
+        sigu, firstu, d1u, endo, endu, s3u = new("wu", 16), new("wu", 16), new("wu", 16), new("wu", 16), new("wu", 32), new("wu", 16)
+        ts(sub(an, 0, 16), sub(kk, 0, 16), 255, Op.bitwise_and)
+        ts(sub(an, 16, 32), sub(kk, 0, 16), 252, Op.bitwise_and)
         cp(sigu, sub(an, 0, 16))
+        ts(s3u, sub(an, 16, 32), 3.0, Op.add)
         cp(firstu, first)
-        a4, s3u, gdu, w = new("wi", 32), new("wu", 16), new("wu", 16), new("wi", 48)
-        ts(a4, sub(kk, 0, 32), 252, Op.bitwise_and)
-        ts(s3u, sub(a4, 0, 16), 3.0, Op.add)
-        ts(sub(w, 0, 16), sub(an, 16, 32), -1.0, Op.mult, 256.0, Op.add)
+        mark("f%d" % t)
+        w = new("wi", 96)
+        ts(sub(w, 0, 16), plc, -n + 0.0, Op.add)
         tt(sub(w, 16, 32), sub(w, 0, 16), first, Op.mult)
-        tt(sub(w, 32, 48), sub(w, 16, 32), sub(an, 16, 32), Op.add)
-        cp(gdu, sub(w, 32, 48))
+        ts(d1u, sub(w, 16, 32), n + 0.0, Op.add)
         mark("f%d" % t)
-        for out, bs, flg, far in ((d1u, sub(a4, 16, 32), first, n + 3.0), (endo, xi, last, n + 0.0)):
-            w = new("wi", 64)
-            tt(sub(w, 0, 16), plc, bs, Op.subtract)
-            ts(sub(w, 16, 32), sub(w, 0, 16), -far, Op.add)
-            tt(sub(w, 32, 48), sub(w, 16, 32), flg, Op.mult)
-            tt(sub(w, 48, 64), sub(w, 32, 48), bs, Op.add)
-            ts(out, sub(w, 48, 64), far, Op.add)
-            mark("f%d" % t)
-        bigs, nks, hs, sn = new("wf", 256), new("wf", 256), new("wf", n), new("wf", 256)
-        act(bigs, (lutb, firstu), Fn.Copy)
+        tt(sub(w, 32, 48), sub(w, 0, 16), xi, Op.subtract)
+        tt(sub(w, 48, 64), sub(w, 32, 48), last, Op.mult)
+        tt(sub(w, 64, 80), sub(w, 48, 64), xi, Op.add)
+        ts(endo, sub(w, 64, 80), n + 0.0, Op.add)
         mark("f%d" % t)
-        iota(nk, [[-1, 64], [0, 4]], -n)
-        act(nks, (nk, sigu), Fn.Copy)
+        a0, b1, nk, ew, hs = new("wf", 512), new("wb", 512), new("wb", 256), new("wb", n + 256), new("wb", n)
+        act(sub(a0, 0, 512, 2), (lutb, firstu), Fn.Copy)
+        mark("f%d" % t)
+        act(sub(b1, 0, 512, 2), (lutn, firstu), Fn.Copy)
+        mark("f%d" % t)
+        iota(nk, [[1, 64], [0, 4]], n - 256)
+        act(sub(b1, 1, 512, 2), (nk, sigu), Fn.Copy, scale=1.0 / 512)
         mark("f%d" % t)
         act(sub(ew, 0, n), sub(ones, 0, n), Fn.Copy, scale=256.0)
-        scatter(sub(ew, 0, n + 256), endo, sub(jf, 0, 256))
+        scatter(ew, endo, sub(jf, 0, 256))
         scan(hs, sub(m16, 0, n), sub(ew, 0, n), Op.mult, Op.add)
-        ts(sub(endu, 0, k), sub(hs, 15, n, 16), s16, Op.mult, 0.25, Op.add)
+        ts(sub(endu, 0, n // 16), sub(hs, 15, n, 16), col(13), Op.mult, 1.25, Op.add)
         mark("e%d" % t)
+        return nu, pk, sigu, s3u, d1u, endu, a0, b1
+
+    pars = [new("wb", n) for n in NS]
+    ups = [[new("wb", n), new("wb", n), new("wb", n), new("wb", n)] for n in NS[:2]]
+    nears = [near(t) for t in range(2)]
+    vs, gt, a1, b0 = new("wb", 528), new("wf", 272), new("wf", 512), new("wb", 512)
+    fill(sub(vs, 512, 528), NONE)
+    iota(gt, [[0, 272]])
+    iota(sub(a1, 1, 512, 2), [[0, 256]])
+    iota(sub(b0, 0, 512, 2), [[0, 256]])
+    base = dict(top)
+    for t in range(2):
+        top.update(base)
+        turn[0] = 0
+        n, n2, ch, ch2 = NS[t], NS[t + 1], CHUNKS[t], CHUNKS[t + 1]
+        X, XH, XN = "x%d" % t, "xh%d" % t, "x%d" % (t + 1)
+        nm = lambda s, lo, hi, step=1, t=t: V("%s%d" % (s, t), lo, hi, step)
+        k = n // 16
+        par, nxt = pars[t], pars[t + 1]
+        halves = lambda lo: ((lo, (lo + n + 32) // 64 * 32), ((lo + n + 32) // 64 * 32, n))
+        lists = [new("wu", 32) for i in range(9)]
+        low = [0 if t or i < LOW else 2 ** i for i in range(9)]
+        cut = [halves(low[i])[0][1] if t == 0 or i == 8 else n // 2 for i in range(9)]
+        part = lambda i, lo=0: [(a, b) for a, b in ((lo, cut[i]), (max(lo, cut[i]), n)) if a < b]
+
+        def listed(i, a, b):
+            pad = cut[i] // 16 % 2 if a >= cut[i] else 0
+            return sub(lists[i], a // 16 + pad, b // 16 + pad)
+
+        def to_list(i, hs):
+            for a, b in part(i, low[i]):
+                ts(listed(i, a, b), sub(hs, a + 15, b, 16), s16y, Op.mult, 256.25, Op.add)
+                mark("u%d%d" % (t, i))
+        up = ups[t]
+        if t == 0:
+            cp(sub(lists[0], 0, k), whole("pai"))
+            for a, b in part(0):
+                if a:
+                    act(sub(par, a, b), (jc, listed(0, a, b)), Fn.Copy, scale=1.0 / 512)
+                else:
+                    ts(sub(par, a, b), (jc, listed(0, a, b)), 1.0 / 512, Op.mult)
+        else:
+            for a, b in part(0):
+                scan(sub(up[3], a, b), sub(m16, a, b), sub(par, a, b), Op.mult, Op.add)
+            to_list(0, up[3])
+        for i in range(8):
+            lo2, hs, src, dst = low[i + 1], up[2 + i % 2], up[i % 2] if i else par, up[(i + 1) % 2]
+            for a, b in part(i if t else i + 1, lo2):
+                move("a" if a > lo2 else JUMPS[t][i], sub(dst, a, b), (src, listed(i, a, b)))
+                scan(sub(hs, a, b), sub(m16, a, b), sub(dst, a, b), Op.mult, Op.add)
+            if lo2 and i < 7:
+                act(sub(dst, 0, lo2), sub(ones, 0, lo2), Fn.Copy, scale=-0.5)
+            to_list(i + 1, hs)
+        s, s2 = new("wf", n), new("wf", n)
+        for c in range(len(ch) - 1):
+            a, b = ch[c], ch[c + 1]
+            quant(nm("qx", a, b), nm("sx", a, b), V(X, 4 * a, 4 * b))
+            mark("x%d" % t)
+            p = mm(c % 2, qr, sr, nm("qx", a, b), nm("sx", a, b))
+            p2 = mm(2 + c % 2, qr, sr, nm("qx", a, b), nm("sx", a, b)) if SCORES[t] == "v" else p
+            move(SCORES[t], sub(s, a, b), p)
+            act(sub(s2, a, b), p2, Fn.Copy)
+        sends = []
+        for c in range(2):
+            a, b = RUNS[t][c], RUNS[t][c + 1]
+            sends.append(hand(c, nm("rq", 0, b - a), nm("qx", a, b), "rc%d" % t, True))
+            sends.append(hand(c, nm("rs", 0, b - a), nm("sx", a, b), "rp%d" % t))
+        arrival(sends, [nm("lq", 0, n), nm("ls", 0, n)], "aq%d" % t, 4 * ne, LAT[0])
+        for j in range(4):
+            act(V(XH, j * n, j * n + n), V(X, j * n, j * n + n), Fn.Copy, scale=0.5)
+            mark("h%d" % t)
+        twin(nm("xo", 0, 4 * n), V(XH, 0, 4 * n))
+        for c in BY_DMA[t]:
+            twin(V(XN, 4 * ch2[c], 4 * ch2[c + 1]), V(X, 4 * ch2[c], 4 * ch2[c + 1]))
+        pc, other, dif = new("wf", n + 16), new("wf", n), new("wf", n)
+        cb = [other, sub(pc, 0, n)]
+        tw = [new("wf", n), new("wf", n)]
+        fill(sub(pc, n, n + 16), 0.0)
+        for a, b in part(0):
+            tt(sub(dif, a, b), (s, listed(0, a, b)), sub(s2, a, b), Op.subtract)
+            act(sub(other, a, b), sub(dif, a, b), Fn.Abs)
+        for a, b in part(0):
+            act(sub(tw[0], a, b), sub(dif, a, b), Fn.Abs)
+        for i in range(9):
+            if low[i]:
+                act(sub(cb[(i + 1) % 2], low[i - 1], low[i]), sub(cb[i % 2], low[i - 1], low[i]), Fn.Copy)
+            for a, b in part(i, low[i]):
+                tt(sub(cb[(i + 1) % 2], a, b), (cb[i % 2], listed(i, a, b)), sub(tw[i % 2], a, b), Op.max)
+                mark("c%d%d" % (t, i))
+            if i < 8:
+                for a, b in part(i, low[i]):
+                    a = max(a, low[i + 1])
+                    if a < b:
+                        act(sub(tw[(i + 1) % 2], a, b), sub(cb[(i + 1) % 2], a, b), Fn.Copy)
+                        mark("t%d" % t)
+        cc = cb[1]
+        h = n // 2
+        win, msk, lst, rk = new("wf", h), new("wf", h), new("wf", h), new("wu", 16)
+        for a, b in halves(0):
+            tt(sub(win, a // 2, b // 2), sub(cc, a, b, 2), sub(cc, a + 1, b, 2), Op.min)
+            tt(sub(msk, a // 2, b // 2), sub(win, a // 2, b // 2), sub(diag, a // 2, b // 2), Op.mult)
+            scan(sub(lst, a // 2, b // 2), sub(off16, a // 2, b // 2), sub(msk, a // 2, b // 2), Op.mult, Op.add)
+        ranks(win, lst, h, SCALAR[t][0], rk)
+        flag, pre, fl, cnt, acc, ou = new("wb", h), new("wb", h), new("wb", 4 * h), new("wb", 2 * h), new("wf", 2), new("wu", 8)
+        cp(flag, (lut64, sub(rk, 0, h // 16)))
+        scan(pre, sub(ones, 0, h), flag, Op.mult, Op.add)
+        for u in range(2):
+            ts(sub(fl, u * h, u * h + h), pre, sub(kh, u, u + 1), Op.is_lt)
+            scan(sub(cnt, u * h, u * h + h), sub(ones, 0, h), sub(fl, u * h, u * h + h), Op.mult, Op.add)
+            act(sub(fl, (2 + u) * h, (3 + u) * h), pre, Fn.Sign, bias=sub(kh, 2 + u, 3 + u), scale=-1.0, acc=sub(acc, u, u + 1))
+        for e in range(2):
+            ts(sub(ou, 4 * e, 4 * e + 2), sub(cnt, h - 1, 2 * h, h), 2.0, Op.mult, e + 0.25, Op.add)
+            ts(sub(ou, 4 * e + 2, 4 * e + 4), acc, h + e + 0.25, Op.add)
+        c2, j2, rk2, srt, hs = new("wf", 128), new("wf", 128), new("wu", 8), new("wf", 256), new("wf", 64)
+        msk, lst = new("wf", 128), new("wf", 128)
+        for e in range(2):
+            tt(sub(msk, e, 128, 2), (cc, sub(ou, 4 * e, 4 * e + 4)), sub(diag, e, 128, 2), Op.mult)
+            act(sub(c2, e, 128, 2), (cc, sub(ou, 4 * e, 4 * e + 4)), Fn.Copy)
+        for e in range(2):
+            act(sub(j2, e, 128, 2), (sub(jf, 0, n), sub(ou, 4 * e, 4 * e + 4)), Fn.Copy)
+        scan(lst, sub(off16, 0, 128), msk, Op.mult, Op.add)
+        ranks(c2, lst, 128, SCALAR[t][1], rk2)
+        scatter(srt, rk2, j2)
+        scan(hs, sub(m4, 0, 64), sub(srt, 0, 128, 2), Op.mult, Op.add)
+        ts(nm("el", 0, 16), sub(hs, 3, 64, 4), s4p, Op.mult, qto, Op.add)
+        sl = hand(0, nm("rl", 0, 16), nm("el", 0, 16), "rn%d" % t)
+        arrival([sl], [nm("ll", 0, 16)], "an%d" % t, ne, LAT[1])
+        for b in range(4):
+            p = mm(4 + b, V("qe", 128 * b, 128 * b + 128), V("se", 128 * b, 128 * b + 128), nm("lq", 0, n), nm("ls", 0, n))
+            act(nm("dd", b, 4 * n, 4), p, Fn.Copy)
+            mark("d%d" % t)
+        nu, pk, sigu, s3u, d1u, endu, a0, b1 = nears[t]
+        act(sub(a1, 0, 512, 2), (pc, d1u), Fn.Copy)
+        mark("s%d" % t)
+        sn = new("wf", 256)
         act(sn, (s, nu), Fn.Copy)
         mark("s%d" % t)
         cp(V(X, 4 * n, 4 * n + 128), (nm("dd", 0, 4 * n), nm("ll", 0, 8)))
@@ -599,65 +657,58 @@ def plan(g, core, T, topo, rank, room):
         z = sub(mm(2, qr, sr, nm("qh", 0, 128), nm("sh", 0, 128)), 64, 128)
         act(V(XH, 4 * n, 4 * n2), V(X, 4 * n, 4 * n2), Fn.Copy, scale=0.5)
         act(nm("xo", 4 * n, 4 * n2), V(X, 4 * n, 4 * n2), Fn.Copy, scale=0.5)
-        d, cost, gs, pr, gd, ga = [new("wf", 256) for i in range(6)]
-        gap, mn = sub(gz, 0, 256), sub(pc, n, n + 256)
+        d, gap, cost, mn, gs, ga = [new("wf", 256) for i in range(6)]
+        best, pw = new("wf", 512), new("wi", 128)
         for i in range(4):
             tt(sub(d, i, 256, 4), sub(sn, i, 256, 4), z, Op.subtract)
             act(sub(gap, i, 256, 4), sub(d, i, 256, 4), Fn.Abs)
         tt(cost, (cc, nu), gap, Op.max)
         scan(mn, big4, cost, Op.add, Op.min)
-        act(gd, (gz, gdu), Fn.Copy)
-        act(ga, (gz, sigu), Fn.Copy)
-        nxt = nxts[t]
-        d1, ex, f, v, mn2 = [new("wf", 256) for i in range(5)]
-        pw = new("wi", 128)
-        tt(d1, (pc, d1u), gd, Op.max)
-        tt(pr, (mn, s3u), ga, Op.max)
-        act(mn2, mn, Fn.Copy)
-        tt(sub(gt, 8, 264), (mn, rep4), mn2, Op.is_lt)
-        scan(gs, sub(gt, 7, 263), pk, Op.max, Op.min)
+        act(ga, (gap, sigu), Fn.Copy)
+        tt(sub(a0, 1, 512, 2), (mn, s3u), ga, Op.max)
+        for i in range(3):
+            tt(sub(gt, 8 + i, 264, 4), sub(mn, i, 256, 4), sub(mn, 3, 256, 4), Op.is_gt)
+        for a in (0, 128):
+            scan(sub(gs, a, a + 128), sub(gt, a + 7, a + 135), sub(pk, a, a + 128), Op.max, Op.min, 1.0)
         ts(sub(pw, 0, 64), sub(gs, 3, 256, 4), 2.0 ** 17, Op.mult)
         ts(sub(pw, 64, 128), sub(pw, 0, 64), 511, Op.bitwise_and)
-        ts(sub(nxt, n, n2), sub(pw, 64, 128), -1.0, Op.mult)
+        ts(sub(nxt, n, n2), sub(pw, 64, 128), 1.0 / 512, Op.mult, -0.5, Op.add)
         mark("n%d" % t)
-        scan(ex, bigs, d1, Op.add, Op.min)
-        tt(f, pr, ex, Op.is_lt)
-        tt(v, f, nks, Op.mult)
-        scan(sub(vs, 0, 256), bigs, v, Op.add, Op.min)
-        for a, b in ((0, ch2[1]), (ch2[1], n)):
-            tt(sub(nxt, a, b), (vs, sub(endu, a // 16, b // 16)), sub(negp, a, b), Op.min)
-        negp = nxt
-        yo, hs = new("wu", n2 // 4), new("wf", n2)
-        for c in range(2):
+        scan(best, a0, a1, Op.min, Op.max)
+        tt(sub(b0, 1, 512, 2), sub(best, 1, 512, 2), sub(best, 0, 512, 2), Op.is_lt)
+        scan(sub(vs, 0, 512), b0, b1, Op.add, Op.min)
+        yo, hs = new("wu", n2 // 4), new("wb", n2)
+        for c in range(len(ch2) - 1):
             a, b = ch2[c], ch2[c + 1]
-            scan(sub(hs, a, b), sub(m4, a, b), sub(negp, a, b), Op.mult, Op.add)
-            ts(sub(yo, a // 4, b // 4), sub(hs, a + 3, b, 4), s4n, Op.mult, qto, Op.add)
+            if a < n:
+                tt(sub(nxt, a, min(b, n)), (vs, sub(endu, a // 16, min(b, n) // 16)), sub(par, a, min(b, n)), Op.max)
+            scan(sub(hs, a, b), sub(m4, a, b), sub(nxt, a, b), Op.mult, Op.add)
+            ts(sub(yo, a // 4, b // 4), sub(hs, a + 3, b, 4), s4y, Op.mult, qty, Op.add)
+            mark("y%d%d" % (t, c))
             cuts = [a + (b - a) * j // PIECES // 8 * 8 for j in range(PIECES)] + [b]
             for lo, hi in zip(cuts, cuts[1:]):
                 tt(nm("yt", 4 * lo, 4 * hi), (V(XH, 0, 4 * n2), sub(yo, lo // 4, hi // 4)), nm("xo", 4 * lo, 4 * hi), Op.add)
             quant(nm("qy", a, b), nm("sy", a, b), nm("yt", 4 * a, 4 * b))
             mark("q%d%d" % (t, c))
             for e in range(4):
-                p = mm(4 * c + e, V("wq", 128 * e, 128 * e + 128), V("wsc", 128 * e, 128 * e + 128), nm("qy", a, b), nm("sy", a, b))
+                p = mm(4 * (c % 2) + e, V("wq", 128 * e, 128 * e + 128), V("wsc", 128 * e, 128 * e + 128), nm("qy", a, b), nm("sy", a, b))
                 r = nm("ru", 4 * a + e, 4 * b, 4)
                 act(r, p, Fn.Relu, scale=0.03125)
-                if c:
+                mark("r%d%d" % (t, c))
+                if c not in BY_DMA[t]:
                     tt(V(XN, 4 * a + e, 4 * b, 4), r, V(X, 4 * a + e, 4 * b, 4), Op.add)
-            if c == 0:
-                heap(V(XN, 0, 4 * b), nm("ru", 0, 4 * b), LAT[2])
+            if c in BY_DMA[t]:
+                heap(V(XN, 4 * a, 4 * b), nm("ru", 4 * a, 4 * b), LAT[2])
 
-    act(whole("osb"), negp, Fn.Copy, scale=-1.0)
+    act(whole("osb"), pars[2], Fn.Identity, bias=col(12), scale=512.0)
     dma("s", lambda: g.sync.dma_start(T.op[:], T.osb[0:128:16, :]), [whole("osb")], [], 2000)
-    for c in range(2):
+    for c in range(len(CHUNKS[2]) - 1):
         a, b = CHUNKS[2][c], CHUNKS[2][c + 1]
         quant(V("qx2", a, b), V("sx2", a, b), V("x2", 4 * a, 4 * b))
-        p = mm(c, whole("qv"), whole("sv"), V("qx2", a, b), V("sx2", a, b))
-        if c:
-            cp(V("ysb", a, b), p)
-        else:
-            act(V("ysb", a, b), p, Fn.Copy)
+        p = mm(c % 2, whole("qv"), whole("sv"), V("qx2", a, b), V("sx2", a, b))
+        move("a", V("ysb", a, b), p)
         dma("s", lambda a=a, b=b: g.sync.dma_start(T.oc[:, 4 * a:4 * b], T.qx2[:, a:b].bitcast(dt.uint8)), [V("qx2", a, b)], [], 2300)
         dma("s", lambda a=a, b=b: g.sync.dma_start(T.y[:, a:b], T.ysb[:, a:b]), [V("ysb", a, b)], [], 2300)
     for j in range(4):
-        dma("a", lambda j=j: g.scalar.dma_start(T.osc[4 * j:4 * j + 4, :], T.sx2[32 * j:32 * j + 4, :]), [whole("sx2")], [], 2000)
+        dma("s", lambda j=j: g.sync.dma_start(T.osc[4 * j:4 * j + 4, :], T.sx2[32 * j:32 * j + 4, :]), [whole("sx2")], [], 2000)
     return ops

@@ -1,19 +1,27 @@
+import math
+import numpy as np
 from concourse.mybir import dt, AluOpType as Op, ActivationFunctionType as Fn
 
 C, A = 352, 64
 NS = (C, C + A, C + 2 * A)
-RUNS = ((0, 176, 352), (0, 208, 416))
-CHUNKS = ((0, 176, 352), (0, 160, 288, 416), (0, 192, 352, 480))
+RUNS = ((0, 192, 352), (0, 208, 416))
+CHUNKS = ((0, 192, 352), (0, 160, 288, 416), (0, 160, 320, 480))
 BY_DMA = ((0,), (0,))
+BLEND = ("vvv", "vvv")
+TT2 = 2.0
+JOIN = (1, 1)
+PARENTS = ("aaa", "aaa")
+LAST = "aav"
+ORDER = ((0, 1), (0, 1, 2), (0, 1, 2))
+READY = ((0, 1), (1, 0, 2))
 BIG = 2.0 ** 90
 HOLD = 2.0 ** 24
 KEEP = 4096.0
-NONE = -0.53125
 X4 = "float8_e4m3fn_x4"
 DMAS = 40
 
 SCRATCH = {
-    "wf": ("sbuf", [128, 15360], "float32"), "wb": ("sbuf", [128, 29696], "bfloat16"),
+    "wf": ("sbuf", [128, 16384], "float32"), "wb": ("sbuf", [128, 29696], "bfloat16"),
     "wi": ("sbuf", [128, 1024], "int32"), "wu": ("sbuf", [128, 1024], "uint16"),
     "ps": ("psum", [128, 4096], "float32"),
     "pai": ("sbuf", [128, 22], "int32"), "nri": ("sbuf", [128, 32], "int32"),
@@ -48,16 +56,24 @@ SEMAPHORES = (["ev", "ea", "ep", "eg", "sent"] + ["dm%d" % _i for _i in range(DM
               + ["%s%d" % (_s, _t) for _s in ("rc", "rp", "rn", "aq", "an") for _t in range(2)])
 
 CY, WAKE = 0.92, 170.0
-LAT = (9000.0, 5000.0, 2500.0)
-PIECES = 1
+LAT = (12000.0, 4300.0, 1900.0)
+HOLDS = (1100.0, 1300.0, 1.25)
+PIECES = (1, 1)
 SCALAR = (((3, 2), (1, 2)), ((3, 3), (1, 2)))
 JUMPS = ("vaaaaaaa", "aaaaaaaa")
 LOW = 5
-SCORES = ("v", "v")
-EARLY = {"u14": 1000, "c02": 5000, "y01": 300, "q12": 1500, "u06": 2000, "u10": 150, "u16": 1000, "r01": 1000, "c07": 1000, "y11": 1000,
-         "u05": 600, "y02": 1000, "q02": 300, "q01": 1500, "x1": 600, "c03": 1000, "y12": 300, "c06": 150, "r00": 600, "s0": 5000,
-         "c05": 1500, "u08": 1000, "c01": 300, "r02": 150, "r11": 150, "u04": 5000, "k0": 150, "q11": 150, "f0": 150, "u11": 2000,
-         "u02": 1000, "c16": 600, "u07": 150, "r12": 600, "c00": 300}
+PAR0 = "v"
+FULL = (5, 9)
+WINS = (3, 2)
+SPLIT = 2
+SPREAD = "aaaaa"
+HALVE = ("aaaa", "aaaa")
+TRIES, SLACK, SEED, ORDERED = 40000, 30.0, 1, []
+SCORES = ("v", "a")
+EARLY = {"r11": 3000, "c04": 1000, "u15": 1000, "q02": 1000, "x11": 1500, "u14": 1500, "u16": 1000, "u17": 1500, "u02": 8000, "c03": 1500,
+         "c15": 600, "u03": 1000, "c00": 8000, "r00": 1000, "y01": 2000, "c11": 600, "c14": 1000, "c12": 300, "b01": 2000, "u12": 2000,
+         "q00": 1500, "r01": 600, "b10": 8000, "k0": 2000, "y11": 2000, "e0": 2000, "m01": 8000, "q10": 2000, "o0": 5000, "u05": 1000,
+         "q01": 3000, "y00": 8000, "u01": 150, "x10": 5000, "x12": 1500}
 
 
 def relays_of(T, topo, r):
@@ -160,9 +176,88 @@ def schedule(ops):
     return sorted(range(n), key=lambda i: (ops[i]["start"], i)), max(done)
 
 
+def thin(ops):
+    above = []
+    for o in ops:
+        seen, kept = 0, []
+        for j in sorted(o["deps"], reverse=True):
+            if not seen >> j & 1:
+                kept.append(j)
+            seen |= above[j] | 1 << j
+        above.append(seen)
+        o["deps"] = kept
+
+
+def exchange(ops, order, tries):
+    n = len(ops)
+    q, cost = ["xvapgs".index(o["q"]) for o in ops], [o["cost"] for o in ops]
+    tail, deps, after = [o["cost"] + o["lat"] + WAKE for o in ops], [o["deps"] for o in ops], [[] for o in ops]
+    for i in range(n):
+        for j in deps[i]:
+            after[j].append(i)
+
+    def times(seq):
+        free, last, start, done, why = [0.0] * 6, [-1] * 6, [0.0] * n, [0.0] * n, [-1] * n
+        for i in seq:
+            t, w, k = 0.0, -1, q[i]
+            for j in deps[i]:
+                if done[j] > t:
+                    t, w = done[j], j
+            if k:
+                if free[k] > t:
+                    t, w = free[k], -2 - last[k]
+                free[k], last[k] = t + cost[i], i
+            start[i], done[i], why[i] = t, t + tail[i], w
+        return start, done, why
+    draw = np.random.default_rng(SEED)
+    seq = list(order)
+    start, done, why = times(seq)
+    now = max(done)
+    best = (now, seq)
+    for it in range(tries):
+        i, pairs = done.index(now), []
+        while i >= 0:
+            w = why[i]
+            if w <= -2:
+                pairs.append((-2 - w, i))
+            i = -2 - w if w <= -2 else w
+        a, b, c, d, e = draw.random(5)
+        u, v = pairs[int(a * len(pairs))]
+        pos = {x: k for k, x in enumerate(seq)}
+        if b < 0.65:
+            x, hi = (v, pos[u]) if b < 0.5 else (u, pos[u] - 1)
+            lo = max([pos[j] for j in deps[x]] + [-1]) + 1
+            near = hi if b < 0.5 else None
+        else:
+            x, lo = u, pos[v]
+            hi = min([pos[j] for j in after[u]] + [n]) - 1
+            near = lo
+        if lo > hi:
+            continue
+        k = near if near is not None and c < 0.5 else lo + int(d * (hi - lo + 1))
+        new = list(seq)
+        new.pop(pos[x])
+        new.insert(k, x)
+        s2, d2, w2 = times(new)
+        t = max(d2)
+        if t <= now or e < math.exp((now - t) / (SLACK * (1 - it / tries) + 1)):
+            start, done, why, now = s2, d2, w2, t
+            pos = {x: k for k, x in enumerate(new)}
+            seq = sorted(new, key=lambda x: (start[x], pos[x]))
+            if now < best[0]:
+                best = (now, seq)
+    start = times(best[1])[0]
+    for i in range(n):
+        ops[i]["start"] = start[i]
+    return best[1], best[0] - WAKE
+
+
 def emit(g, T, ops):
     link(ops)
-    order, _ = schedule(ops)
+    thin(ops)
+    if not ORDERED:
+        ORDERED.append(exchange(ops, schedule(ops)[0], TRIES)[0])
+    order = ORDERED[0]
     queue = {"v": g.vector, "a": g.scalar, "p": g.tensor, "g": g, "s": g.sync}
     count, seen, dmas = {"v": 0, "a": 0, "p": 0, "g": 0}, {}, 0
     sent = 0
@@ -226,7 +321,7 @@ def plan(g, core, T, topo, rank, room):
         for v in r:
             if isinstance(v, tuple):
                 rr += list(v) if len(v) == 2 else [v]
-        ops.append(dict(q=q, kind=kind, fn=fn, r=rr, w=list(w), cost=cost, lat=lat, after=list(after), **more))
+        ops.append(dict(q=q, kind=kind, fn=fn, r=rr, w=list(w), cost=cost * (HOLDS[2] if q + kind == "gc" else 1), lat=lat, after=list(after), **more))
         return len(ops) - 1
 
     def price(out, ins, two=False):
@@ -235,7 +330,7 @@ def plan(g, core, T, topo, rank, room):
             return 50 + 1.56 * CY * n
         half = all(wide[SCRATCH[v[0]][2]] == 2 for v in [out] + ins)
         if two:
-            return CY * max(64, n if any(v[0] == "ps" for v in ins) else (1.5 if half else 2) * n)
+            return CY * max(64, n if any(v[0] == "ps" for v in ins) else (TT2 if half and max(v[3] for v in [out] + ins) == 1 else 2) * n)
         return CY * max(64, n / 2 if half else n)
 
     def tt(out, a, b, op):
@@ -255,7 +350,7 @@ def plan(g, core, T, topo, rank, room):
         add("v", "c", lambda: g.vector.tensor_copy(ap((win, off)), ap(a)), [a, off], [win], 50 + 3.8 * CY * size(a))
 
     def scan(out, d0, d1, op0, op1, first=0.0):
-        add("v", "c", lambda: g.vector.tensor_tensor_scan(ap(out), ap(d0), ap(d1), first, op0, op1), [d0, d1], [out], price(out, [d0, d1]))
+        add("v", "c", lambda: g.vector.tensor_tensor_scan(ap(out), ap(d0), ap(d1), sc(first), op0, op1), [d0, d1, first], [out], price(out, [d0, d1]))
 
     def fill(out, k):
         add("v", "c", lambda: g.vector.memset(ap(out), k), [], [out], price(out, []))
@@ -284,6 +379,10 @@ def plan(g, core, T, topo, rank, room):
             fn = lambda: g.iota(ap(out), pattern, base, cm, allow_small_or_imprecise_dtypes=True)
         add("g", "c", fn, [], [out], 130 + 2 * CY * size(out))
 
+    def keep(out, a, pattern=None, k=0.0):
+        pattern, base = pattern or [[0, size(out)]], 0 if pattern else 1
+        add("g", "c", lambda: g.affine_select(ap(out), ap(a), pattern, Op.not_equal, k, base, 0), [a], [out], 170 + 2 * CY * size(out))
+
     def quant(q, s, a):
         add("v", "c", lambda: g.vector.quantize_mx(ap(q), ap(s), ap(a)), [a], [q, s], 15 + 0.27 * size(a))
 
@@ -295,11 +394,11 @@ def plan(g, core, T, topo, rank, room):
     def dma(q, fn, r, w, lat):
         add(q, "d", fn, r, w, 60, lat)
 
-    def twin(out, a):
-        dma("s", lambda: g.sync.dma_start(ap(out), ap(a)), [a], [out], 2500)
+    def twin(out, a, gate):
+        dma("s", lambda: g.sync.dma_start(ap(out), ap(a)), [a, gate], [out], 3500)
 
     def heap(out, a, lat):
-        add("g", "d", lambda: g.dma_start(ap(out), ap(a), accum_op=Op.add), [a, out], [out], 700, lat)
+        add("g", "d", lambda: g.dma_start(ap(out), ap(a), accum_op=Op.add), [a, out], [out], HOLDS[1], lat)
 
     def u8(v):
         return ap(v).bitcast(dt.uint8)
@@ -313,7 +412,7 @@ def plan(g, core, T, topo, rank, room):
     def hand(k, dst, src, sem, codes=False):
         rid, pid = topo.addr(rl[k], core)
         f = u8 if codes else ap
-        return add("g", "r", lambda: g.remote_dma(f(dst), f(src), T.sem[sem], T.sem.sent, pid, rid, topo.mask(core, rl[k])), [src], [], 400,
+        return add("g", "r", lambda: g.remote_dma(f(dst), f(src), T.sem[sem], T.sem.sent, pid, rid, topo.mask(core, rl[k])), [src], [], HOLDS[0],
                    inc=len(topo.engines(core, rl[k])))
 
     def arrival(after, w, sem, v, lat):
@@ -321,14 +420,14 @@ def plan(g, core, T, topo, rank, room):
 
     dma("s", lambda: g.sync.dma_start(T.pai[:], T.pa[:]), [], [whole("pai")], 2000)
     dma("a", lambda: g.scalar.dma_start(T.ub[:], T.u[:]), [], [whole("ub")], 2200)
-    dma("s", lambda: g.sync.dma_start(T.x0[:, 0:704], T.x[:, 0:704]), [], [V("x0", 0, 704)], 2600)
-    dma("a", lambda: g.scalar.dma_start(T.x0[:, 704:1408], T.x[:, 704:1408]), [], [V("x0", 704, 1408)], 2900)
+    x1 = 4 * CHUNKS[0][1]
+    dma("s", lambda: g.sync.dma_start(T.x0[:, 0:x1], T.x[:, 0:x1]), [], [V("x0", 0, x1)], 2600)
+    dma("a", lambda: g.scalar.dma_start(T.x0[:, x1:4 * C], T.x[:, x1:4 * C]), [], [V("x0", x1, 4 * C)], 2900)
     dma("s", lambda: g.sync.dma_start(T.nri[:], T.nr[:]), [], [whole("nri")], 3000)
-    gate = [V("x0", 704, 1408)]
+    gate = [V("x0", x1, 4 * C)]
     dma("s", lambda: g.sync.dma_start(T.wq[:].bitcast(dt.uint8), T.wc[:]), gate, [whole("wq")], 3000)
     dma("s", lambda: g.sync.dma_start(T.wsc[:], T.ws[:]), gate, [whole("wsc")], 2500)
-    add("g", "d", lambda: g.dma_start(T.vb[:], T.v[:]), gate, [whole("vb")], 1500, 2500)
-    mark("v")
+    dma("s", lambda: g.sync.dma_start(T.vb[:], T.v[:]), [whole("wsc")], [whole("vb")], 3500)
 
     pi, cols, cf = new("wi", 1), new("wi", 4), new("wf", 16)
     col = lambda k: sub(cf, k, k + 1)
@@ -344,7 +443,6 @@ def plan(g, core, T, topo, rank, room):
     ts(sub(cf, 3, 5), sub(cf, 0, 2), 1.0, Op.add)
     ts(s16, q16, 15.0, Op.is_equal, 1.0 / HOLD, Op.max)
     ts(s16y, s16, 512.0, Op.mult)
-    ts(col(13), s16, 2.0, Op.mult)
     ts(s4, q4, 3.0, Op.is_equal, 1.0 / HOLD, Op.max)
     ts(s4p, s4, 4.0, Op.mult)
     ts(s4y, s4, 2048.0, Op.mult)
@@ -362,8 +460,17 @@ def plan(g, core, T, topo, rank, room):
     ts(qoff, sub(ones, 0, 30), q16, Op.mult)
 
     def spread(p, n, who="a"):
-        m = new(p[0], n)
-        move(who, m, (p, sub(qoff, 0, n // 16)))
+        m, w = new(p[0], n), 16
+        if who != "g":
+            for lo in range(0, n, 192):
+                hi = min(n, lo + 192)
+                move(who, sub(m, lo, hi), (p, sub(qoff, 0, (hi - lo) // 16)))
+            return m
+        for lo in (0, 16):
+            keep(sub(m, lo, lo + 16), p)
+        while 2 * w < n:
+            w *= 2
+            keep(sub(m, w, min(2 * w, n)), sub(m, 0, min(w, n - w)))
         return m
 
     def hold(r, q, qn):
@@ -374,31 +481,30 @@ def plan(g, core, T, topo, rank, room):
         return m, a
     p16, poff = hold(r16, q16, q16n)
     p4, _ = hold(r4, q4, q4n)
-    pdiag, w16, pns, pbig = new("wb", 16), new("wb", 16), new("wb", 16), new("wb", 16)
+    pdiag, w16, gt = new("wb", 16), new("wb", 16), new("wf", 256)
     ts(pdiag, r16, q16, Op.is_equal)
     ts(w16, r16, q16, Op.is_ge, -0.5, Op.add)
-    ts(pns, r16, 0.0, Op.not_equal)
-    ts(pbig, r4, 0.0, Op.is_equal, BIG, Op.mult)
-    m16, m4, off16, diag = spread(p16, 416), spread(p4, 480), spread(poff, 208), spread(pdiag, 208)
+    act(gt, sub(ones, 0, 256), Fn.Copy, scale=0.0)
     most = 16 * max(sum(x) for y in SCALAR for x in y)
-    ns16, ws16, big4 = spread(pns, most), spread(w16, most), spread(pbig, 256)
+    m16, m4, off16, diag, ws16 = [spread(p, n, who) for p, n, who in zip((p16, p4, poff, pdiag, w16), (416, 480, 208, 208, most), SPREAD)]
+    ns16, big4 = new("wb", most), new("wb", 128)
+    keep(ns16, sub(ones, 0, most), [[0, most // 16], [1, 16]])
+    keep(big4, sub(gt, 0, 128), [[0, 32], [1, 4]], BIG)
     mr = {}
     for h in (176, 208, 128):
         mr[h] = new("wb", h + 16)
-        act(sub(mr[h], 0, 16), poff, Fn.Copy)
+        cp(sub(mr[h], 0, 16), poff)
         act(sub(mr[h], 16, h), sub(ones, 16, h), Fn.Copy)
         ts(sub(mr[h], h, h + 16), pdiag, KEEP, Op.mult, 1.0, Op.max)
-    lut64, lutb, lutn, pick = new("wb", 416), new("wb", 16), new("wb", 16), new("wf", 256)
-    ts(lut64, jf, 128.0, Op.is_lt)
+    lut64, lutb = new("wb", 416), new("wb", 16)
+    act(sub(lut64, 0, 128), sub(ones, 0, 128), Fn.Copy)
+    act(sub(lut64, 128, 416), sub(ones, 128, 416), Fn.Copy, scale=0.0)
     ts(lutb, sub(jf, 0, 16), -BIG, Op.mult, BIG, Op.add)
-    ts(lutn, sub(jf, 0, 16), NONE - 1.0, Op.mult, 1.0, Op.add)
-    m16i, xi, xf, kh, picki = new("wi", 16), new("wi", 16), new("wf", 16), new("wf", 4), new("wf", 256)
+    m16i, xi, xf, kh = new("wi", 16), new("wi", 16), new("wf", 16), new("wf", 4)
     iota(m16i, [[16, 16]])
     ts(xf, m16i, q16, Op.add)
     cp(xi, xf)
     ts(kh, sub(xf, 0, 4), 0.5, Op.add)
-    iota(picki, [[-2048, 64], [512, 4]], 63 * 2048)
-    act(pick, picki, Fn.Copy, scale=2.0 ** -17)
     add("g", "c", lambda: g.affine_select(T.eye[:], T.one[:], [[1, 528]], Op.is_equal, 0.0, -3, -4), [ones], [whole("eye")], 170 + 2 * CY * 528)
     for b in range(4):
         quant(V("qe", 128 * b, 128 * b + 128), V("se", 128 * b, 128 * b + 128), V("eye", 3 - b, 515 - b))
@@ -462,11 +568,16 @@ def plan(g, core, T, topo, rank, room):
         n = NS[t]
         nu = sub(nru, 16 * t, 16 * t + 16)
         pk, krow, klst, junk, acc = new("wf", 256), new("wf", 256), new("wf", 16), new("wb", 512), new("wf", 16)
-        act(pk, (sub(jf, 0, n), nu), Fn.Copy, scale=2.0 ** -17)
         act(krow, (sub(jf, 0, n), nu), Fn.Copy, scale=256.0)
-        heap(pk, pick, 2500)
+        less = new("wf", 256)
+        for i in range(4):
+            act(sub(pk, 3 - i, 256, 4), sub(krow, i, 256, 4), Fn.Copy, scale=2.0 ** -17)
+            if i < 3:
+                act(sub(less, 2 - i, 256, 4), sub(krow, i, 256, 4), Fn.Copy, scale=-2.0 ** -17)
+        act(sub(less, 3, 256, 4), sub(ones, 0, 64), Fn.Copy, scale=-0.5)
+        heap(pk, less, 3500)
         mark("p%d" % t)
-        heap(krow, sub(jf, 0, 256), 2500)
+        heap(krow, sub(jf, 0, 256), 3500)
         tt(klst, sub(nrf, 16 * t, 16 * t + 16), xf, Op.add)
         for m in range(16):
             act(sub(junk, 256 * (m % 2), 256 * (m % 2) + 256), krow, Fn.Sign, bias=sub(klst, m, m + 1), scale=-1.0, acc=sub(acc, m, m + 1))
@@ -501,29 +612,31 @@ def plan(g, core, T, topo, rank, room):
         tt(sub(w, 64, 80), sub(w, 48, 64), xi, Op.add)
         ts(endo, sub(w, 64, 80), n + 0.0, Op.add)
         mark("f%d" % t)
-        a0, b1, nk, ew, hs = new("wf", 512), new("wb", 512), new("wb", 256), new("wb", n + 256), new("wb", n)
+        a0, b1, nk, ew, hs = new("wf", 512), new("wb", 512), new("wb", 256), new("wf", n + 256), new("wf", n)
         act(sub(a0, 0, 512, 2), (lutb, firstu), Fn.Copy)
         mark("f%d" % t)
-        act(sub(b1, 0, 512, 2), (lutn, firstu), Fn.Copy)
-        mark("f%d" % t)
+        b0 = new("wb", 512)
+        act(sub(b0, 0, 512, 2), sub(a0, 0, 512, 2), Fn.Identity, bias=sub(ones, 0, 1), scale=-1.0 / BIG)
         iota(nk, [[1, 64], [0, 4]], n - 256)
         act(sub(b1, 1, 512, 2), (nk, sigu), Fn.Copy, scale=1.0 / 512)
         mark("f%d" % t)
-        act(sub(ew, 0, n), sub(ones, 0, n), Fn.Copy, scale=256.0)
-        scatter(ew, endo, sub(jf, 0, 256))
+        iota(sub(ew, 0, n), [[1, n]], 512)
+        scatter(ew, endo, odds)
         scan(hs, sub(m16, 0, n), sub(ew, 0, n), Op.mult, Op.add)
-        ts(sub(endu, 0, n // 16), sub(hs, 15, n, 16), col(13), Op.mult, 1.25, Op.add)
+        ts(sub(endu, 0, n // 16), sub(hs, 15, n, 16), s16, Op.mult, 0.25, Op.add)
         mark("e%d" % t)
-        return nu, pk, sigu, s3u, d1u, endu, a0, b1
+        return nu, pk, sigu, s3u, d1u, endu, a0, b0, b1
 
-    pars = [new("wb", n) for n in NS]
+    held = [new("wb", 528 + n) for n in NS[:2]]
+    pars = [sub(held[t], 512, 512 + NS[t]) for t in range(2)] + [new("wb", NS[2])]
     ups = [[new("wb", n), new("wb", n), new("wb", n), new("wb", n)] for n in NS[:2]]
+    odds = new("wf", 256)
+    iota(odds, [[2, 256]], 1)
     nears = [near(t) for t in range(2)]
-    vs, gt, a1, b0 = new("wb", 528), new("wf", 272), new("wf", 512), new("wb", 512)
-    fill(sub(vs, 512, 528), NONE)
-    iota(gt, [[0, 272]])
-    iota(sub(a1, 1, 512, 2), [[0, 256]])
-    iota(sub(b0, 0, 512, 2), [[0, 256]])
+    a1 = new("wf", 512)
+    for t in range(2):
+        fill(sub(held[t], 512 + NS[t], 528 + NS[t]), 1.0)
+    act(sub(a1, 1, 512, 2), sub(ones, 0, 256), Fn.Copy, scale=0.0)
     base = dict(top)
     for t in range(2):
         top.update(base)
@@ -548,10 +661,11 @@ def plan(g, core, T, topo, rank, room):
                 ts(listed(i, a, b), sub(hs, a + 15, b, 16), s16y, Op.mult, 256.25, Op.add)
                 mark("u%d%d" % (t, i))
         up = ups[t]
+        above = lambda row, b: sub(row, 0, n if t else b)
         if t == 0:
             cp(sub(lists[0], 0, k), whole("pai"))
             for a, b in part(0):
-                if a:
+                if a or PAR0 == "a":
                     act(sub(par, a, b), (jc, listed(0, a, b)), Fn.Copy, scale=1.0 / 512)
                 else:
                     ts(sub(par, a, b), (jc, listed(0, a, b)), 1.0 / 512, Op.mult)
@@ -559,21 +673,21 @@ def plan(g, core, T, topo, rank, room):
             for a, b in part(0):
                 scan(sub(up[3], a, b), sub(m16, a, b), sub(par, a, b), Op.mult, Op.add)
             to_list(0, up[3])
-        for i in range(8):
+        for i in range(min(8, FULL[t])):
             lo2, hs, src, dst = low[i + 1], up[2 + i % 2], up[i % 2] if i else par, up[(i + 1) % 2]
             for a, b in part(i if t else i + 1, lo2):
-                move("a" if a > lo2 else JUMPS[t][i], sub(dst, a, b), (src, listed(i, a, b)))
+                move("a" if a > lo2 else JUMPS[t][i], sub(dst, a, b), (above(src, b), listed(i, a, b)))
                 scan(sub(hs, a, b), sub(m16, a, b), sub(dst, a, b), Op.mult, Op.add)
-            if lo2 and i < 7:
+            if lo2 and i < min(8, FULL[t]) - 1:
                 act(sub(dst, 0, lo2), sub(ones, 0, lo2), Fn.Copy, scale=-0.5)
             to_list(i + 1, hs)
         s, s2 = new("wf", n), new("wf", n)
-        for c in range(len(ch) - 1):
+        for at, c in enumerate(READY[t]):
             a, b = ch[c], ch[c + 1]
             quant(nm("qx", a, b), nm("sx", a, b), V(X, 4 * a, 4 * b))
-            mark("x%d" % t)
-            p = mm(c % 2, qr, sr, nm("qx", a, b), nm("sx", a, b))
-            p2 = mm(2 + c % 2, qr, sr, nm("qx", a, b), nm("sx", a, b)) if SCORES[t] == "v" else p
+            mark("x%d%d" % (t, c))
+            p = mm(4 + at % 2, qr, sr, nm("qx", a, b), nm("sx", a, b))
+            p2 = mm(6 + at % 2, qr, sr, nm("qx", a, b), nm("sx", a, b)) if SCORES[t] == "v" else p
             move(SCORES[t], sub(s, a, b), p)
             act(sub(s2, a, b), p2, Fn.Copy)
         sends = []
@@ -583,57 +697,66 @@ def plan(g, core, T, topo, rank, room):
             sends.append(hand(c, nm("rs", 0, b - a), nm("sx", a, b), "rp%d" % t))
         arrival(sends, [nm("lq", 0, n), nm("ls", 0, n)], "aq%d" % t, 4 * ne, LAT[0])
         for j in range(4):
-            act(V(XH, j * n, j * n + n), V(X, j * n, j * n + n), Fn.Copy, scale=0.5)
+            if HALVE[t][j] == "v":
+                ts(V(XH, j * n, j * n + n), V(X, j * n, j * n + n), 0.5, Op.mult)
+            else:
+                act(V(XH, j * n, j * n + n), V(X, j * n, j * n + n), Fn.Copy, scale=0.5)
             mark("h%d" % t)
-        twin(nm("xo", 0, 4 * n), V(XH, 0, 4 * n))
-        for c in BY_DMA[t]:
-            twin(V(XN, 4 * ch2[c], 4 * ch2[c + 1]), V(X, 4 * ch2[c], 4 * ch2[c + 1]))
         pc, other, dif = new("wf", n + 16), new("wf", n), new("wf", n)
-        cb = [other, sub(pc, 0, n)]
+        cc, full = sub(pc, 0, n), FULL[t]
+        cb = [cc, other] if full % 2 and full < 9 else [other, cc]
         tw = [new("wf", n), new("wf", n)]
         fill(sub(pc, n, n + 16), 0.0)
         for a, b in part(0):
-            tt(sub(dif, a, b), (s, listed(0, a, b)), sub(s2, a, b), Op.subtract)
-            act(sub(other, a, b), sub(dif, a, b), Fn.Abs)
+            tt(sub(dif, a, b), (above(s, b), listed(0, a, b)), sub(s2, a, b), Op.subtract)
+            act(sub(cb[0], a, b), sub(dif, a, b), Fn.Abs)
         for a, b in part(0):
             act(sub(tw[0], a, b), sub(dif, a, b), Fn.Abs)
-        for i in range(9):
+        for i in range(full):
             if low[i]:
                 act(sub(cb[(i + 1) % 2], low[i - 1], low[i]), sub(cb[i % 2], low[i - 1], low[i]), Fn.Copy)
             for a, b in part(i, low[i]):
-                tt(sub(cb[(i + 1) % 2], a, b), (cb[i % 2], listed(i, a, b)), sub(tw[i % 2], a, b), Op.max)
+                tt(sub(cb[(i + 1) % 2], a, b), (above(cb[i % 2], b), listed(i, a, b)), sub(tw[i % 2], a, b), Op.max)
                 mark("c%d%d" % (t, i))
-            if i < 8:
+            if i < full - 1:
                 for a, b in part(i, low[i]):
                     a = max(a, low[i + 1])
                     if a < b:
                         act(sub(tw[(i + 1) % 2], a, b), sub(cb[(i + 1) % 2], a, b), Fn.Copy)
                         mark("t%d" % t)
-        cc = cb[1]
+        if full < 9:
+            w = 2 ** full
+            act(sub(cc, 0, w), sub(other, 0, w), Fn.Copy)
+            for a in range(w, n, w):
+                b = min(a + w, n)
+                tt(sub(cc, a, b), (sub(cc if a > w else other, 0, a), listed(full, a, b)), sub(other, a, b), Op.max)
+                mark("c%d%d" % (t, full))
         h = n // 2
         win, msk, lst, rk = new("wf", h), new("wf", h), new("wf", h), new("wu", 16)
-        for a, b in halves(0):
+        for a, b in halves(0) if WINS[t] == 2 else ((0, 128), (128, 256), (256, n)):
             tt(sub(win, a // 2, b // 2), sub(cc, a, b, 2), sub(cc, a + 1, b, 2), Op.min)
             tt(sub(msk, a // 2, b // 2), sub(win, a // 2, b // 2), sub(diag, a // 2, b // 2), Op.mult)
             scan(sub(lst, a // 2, b // 2), sub(off16, a // 2, b // 2), sub(msk, a // 2, b // 2), Op.mult, Op.add)
         ranks(win, lst, h, SCALAR[t][0], rk)
         flag, pre, fl, cnt, acc, ou = new("wb", h), new("wb", h), new("wb", 4 * h), new("wb", 2 * h), new("wf", 2), new("wu", 8)
-        cp(flag, (lut64, sub(rk, 0, h // 16)))
+        cp(sub(flag, 0, 96), (lut64, sub(rk, 0, 6)))
+        act(sub(flag, 96, h), (lut64, sub(rk, 6, h // 16)), Fn.Copy)
         scan(pre, sub(ones, 0, h), flag, Op.mult, Op.add)
         for u in range(2):
             ts(sub(fl, u * h, u * h + h), pre, sub(kh, u, u + 1), Op.is_lt)
             scan(sub(cnt, u * h, u * h + h), sub(ones, 0, h), sub(fl, u * h, u * h + h), Op.mult, Op.add)
             act(sub(fl, (2 + u) * h, (3 + u) * h), pre, Fn.Sign, bias=sub(kh, 2 + u, 3 + u), scale=-1.0, acc=sub(acc, u, u + 1))
-        for e in range(2):
-            ts(sub(ou, 4 * e, 4 * e + 2), sub(cnt, h - 1, 2 * h, h), 2.0, Op.mult, e + 0.25, Op.add)
-            ts(sub(ou, 4 * e + 2, 4 * e + 4), acc, h + e + 0.25, Op.add)
+        ts(sub(ou, 0, 2), sub(cnt, h - 1, 2 * h, h), 2.0, Op.mult, 0.25, Op.add)
+        ts(sub(ou, 2, 4), acc, h + 0.25, Op.add)
         c2, j2, rk2, srt, hs = new("wf", 128), new("wf", 128), new("wu", 8), new("wf", 256), new("wf", 64)
-        msk, lst = new("wf", 128), new("wf", 128)
-        for e in range(2):
-            tt(sub(msk, e, 128, 2), (cc, sub(ou, 4 * e, 4 * e + 4)), sub(diag, e, 128, 2), Op.mult)
-            act(sub(c2, e, 128, 2), (cc, sub(ou, 4 * e, 4 * e + 4)), Fn.Copy)
-        for e in range(2):
-            act(sub(j2, e, 128, 2), (sub(jf, 0, n), sub(ou, 4 * e, 4 * e + 4)), Fn.Copy)
+        msk, lst, odd = new("wf", 128), new("wf", 128), new("wf", n - 1)
+        act(odd, sub(cc, 1, n), Fn.Copy)
+        mark("o%d" % t)
+        for e, row in enumerate((cc, odd)):
+            tt(sub(msk, e, 128, 2), (row, sub(ou, 0, 4)), sub(diag, e, 128, 2), Op.mult)
+            act(sub(c2, e, 128, 2), (row, sub(ou, 0, 4)), Fn.Copy)
+        act(sub(j2, 0, 128, 2), (sub(jf, 0, n), sub(ou, 0, 4)), Fn.Copy)
+        act(sub(j2, 1, 128, 2), sub(j2, 0, 128, 2), Fn.Identity, bias=sub(ones, 0, 1))
         scan(lst, sub(off16, 0, 128), msk, Op.mult, Op.add)
         ranks(c2, lst, 128, SCALAR[t][1], rk2)
         scatter(srt, rk2, j2)
@@ -641,12 +764,18 @@ def plan(g, core, T, topo, rank, room):
         ts(nm("el", 0, 16), sub(hs, 3, 64, 4), s4p, Op.mult, qto, Op.add)
         sl = hand(0, nm("rl", 0, 16), nm("el", 0, 16), "rn%d" % t)
         arrival([sl], [nm("ll", 0, 16)], "an%d" % t, ne, LAT[1])
+        twin(nm("xo", 0, 4 * n), V(XH, 0, 4 * n), nm("ll", 0, 16))
+        for c in BY_DMA[t]:
+            twin(V(XN, 4 * ch2[c], 4 * ch2[c + 1]), V(X, 4 * ch2[c], 4 * ch2[c + 1]), nm("ll", 0, 16))
         for b in range(4):
             p = mm(4 + b, V("qe", 128 * b, 128 * b + 128), V("se", 128 * b, 128 * b + 128), nm("lq", 0, n), nm("ls", 0, n))
             act(nm("dd", b, 4 * n, 4), p, Fn.Copy)
             mark("d%d" % t)
-        nu, pk, sigu, s3u, d1u, endu, a0, b1 = nears[t]
+        nu, pk, sigu, s3u, d1u, endu, a0, b0, b1 = nears[t]
         act(sub(a1, 0, 512, 2), (pc, d1u), Fn.Copy)
+        mark("s%d" % t)
+        vs = sub(held[t], 0, 512)
+        act(sub(b1, 0, 512, 2), (sub(held[t], 512, 528 + n), d1u), Fn.Copy)
         mark("s%d" % t)
         sn = new("wf", 256)
         act(sn, (s, nu), Fn.Copy)
@@ -656,42 +785,56 @@ def plan(g, core, T, topo, rank, room):
         quant(nm("qh", 0, 128), nm("sh", 0, 128), V(X, 4 * n - 256, 4 * n + 256))
         z = sub(mm(2, qr, sr, nm("qh", 0, 128), nm("sh", 0, 128)), 64, 128)
         act(V(XH, 4 * n, 4 * n2), V(X, 4 * n, 4 * n2), Fn.Copy, scale=0.5)
-        act(nm("xo", 4 * n, 4 * n2), V(X, 4 * n, 4 * n2), Fn.Copy, scale=0.5)
+        if BLEND[t][2] == "v":
+            act(nm("xo", 4 * n, 4 * n2), V(X, 4 * n, 4 * n2), Fn.Copy, scale=0.5)
         d, gap, cost, mn, gs, ga = [new("wf", 256) for i in range(6)]
-        best, pw = new("wf", 512), new("wi", 128)
+        best = new("wf", 512)
         for i in range(4):
             tt(sub(d, i, 256, 4), sub(sn, i, 256, 4), z, Op.subtract)
             act(sub(gap, i, 256, 4), sub(d, i, 256, 4), Fn.Abs)
-        tt(cost, (cc, nu), gap, Op.max)
-        scan(mn, big4, cost, Op.add, Op.min)
-        act(ga, (gap, sigu), Fn.Copy)
-        tt(sub(a0, 1, 512, 2), (mn, s3u), ga, Op.max)
-        for i in range(3):
-            tt(sub(gt, 8 + i, 264, 4), sub(mn, i, 256, 4), sub(mn, 3, 256, 4), Op.is_gt)
         for a in (0, 128):
-            scan(sub(gs, a, a + 128), sub(gt, a + 7, a + 135), sub(pk, a, a + 128), Op.max, Op.min, 1.0)
-        ts(sub(pw, 0, 64), sub(gs, 3, 256, 4), 2.0 ** 17, Op.mult)
-        ts(sub(pw, 64, 128), sub(pw, 0, 64), 511, Op.bitwise_and)
-        ts(sub(nxt, n, n2), sub(pw, 64, 128), 1.0 / 512, Op.mult, -0.5, Op.add)
+            tt(sub(cost, a, a + 128), (cc, sub(nu, a // 16, a // 16 + 8)), sub(gap, a, a + 128), Op.max)
+            scan(sub(mn, a, a + 128), sub(big4, 0, 128), sub(cost, a, a + 128), Op.add, Op.min)
+        act(ga, (gap, sigu), Fn.Copy)
+        runs = [(256 * j // SPLIT, 256 * (j + 1) // SPLIT) for j in range(SPLIT)]
+        for a, b in runs:
+            tt(sub(a0, 2 * a + 1, 2 * b, 2), (mn, sub(s3u, a // 16, b // 16)), sub(ga, a, b), Op.max)
+        for i in range(3):
+            tt(sub(gt, 3 - i, 256, 4), sub(mn, i, 256, 4), sub(mn, 3, 256, 4), Op.is_gt)
+        for a in (0, 128):
+            scan(sub(gs, a, a + 128), sub(gt, a, a + 128), sub(pk, a, a + 128), Op.mult, Op.add)
+        act(sub(nxt, n, n2), sub(gs, 3, 256, 4), Fn.Copy)
         mark("n%d" % t)
-        scan(best, a0, a1, Op.min, Op.max)
-        tt(sub(b0, 1, 512, 2), sub(best, 1, 512, 2), sub(best, 0, 512, 2), Op.is_lt)
-        scan(sub(vs, 0, 512), b0, b1, Op.add, Op.min)
+        for a, b in runs:
+            a, b = 2 * a, 2 * b
+            scan(sub(best, a, b), sub(a0, a, b), sub(a1, a, b), Op.min, Op.max, sub(best, a - 1, a) if a else 0.0)
+            tt(sub(b0, a + 1, b, 2), sub(best, a + 1, b, 2), sub(best, a, b, 2), Op.is_lt)
+            scan(sub(vs, a, b), sub(b0, a, b), sub(b1, a, b), Op.add, Op.min, sub(vs, a - 1, a) if a else 0.0)
         yo, hs = new("wu", n2 // 4), new("wb", n2)
-        for c in range(len(ch2) - 1):
+        for at, c in enumerate(ORDER[t + 1]):
             a, b = ch2[c], ch2[c + 1]
             if a < n:
-                tt(sub(nxt, a, min(b, n)), (vs, sub(endu, a // 16, min(b, n) // 16)), sub(par, a, min(b, n)), Op.max)
+                move(PARENTS[t][c], sub(nxt, a, min(b, n)), (sub(held[t], 0, 512 + n), sub(endu, a // 16, min(b, n) // 16)))
+                mark("m%d%d" % (t, c))
+        for c, (a, b) in enumerate(((0, ch2[1]), (ch2[1], n2)) if JOIN[t] else zip(ch2, ch2[1:])):
             scan(sub(hs, a, b), sub(m4, a, b), sub(nxt, a, b), Op.mult, Op.add)
             ts(sub(yo, a // 4, b // 4), sub(hs, a + 3, b, 4), s4y, Op.mult, qty, Op.add)
             mark("y%d%d" % (t, c))
-            cuts = [a + (b - a) * j // PIECES // 8 * 8 for j in range(PIECES)] + [b]
+        for at, c in enumerate(ORDER[t + 1]):
+            a, b = ch2[c], ch2[c + 1]
+            cuts = [a + (b - a) * j // PIECES[t] // 8 * 8 for j in range(PIECES[t])] + [b]
             for lo, hi in zip(cuts, cuts[1:]):
-                tt(nm("yt", 4 * lo, 4 * hi), (V(XH, 0, 4 * n2), sub(yo, lo // 4, hi // 4)), nm("xo", 4 * lo, 4 * hi), Op.add)
+                if BLEND[t][c] == "a":
+                    act(nm("xo", 4 * lo, 4 * hi), (V(XH, 0, 4 * n2), sub(yo, lo // 4, hi // 4)), Fn.Copy)
+                    mark("g%d%d" % (t, c))
+                    tt(nm("yt", 4 * lo, 4 * hi), nm("xo", 4 * lo, 4 * hi), V(XH, 4 * lo, 4 * hi), Op.add)
+                else:
+                    tt(nm("yt", 4 * lo, 4 * hi), (V(XH, 0, 4 * n2), sub(yo, lo // 4, hi // 4)), nm("xo", 4 * lo, 4 * hi), Op.add)
+                mark("b%d%d" % (t, c))
             quant(nm("qy", a, b), nm("sy", a, b), nm("yt", 4 * a, 4 * b))
             mark("q%d%d" % (t, c))
             for e in range(4):
-                p = mm(4 * (c % 2) + e, V("wq", 128 * e, 128 * e + 128), V("wsc", 128 * e, 128 * e + 128), nm("qy", a, b), nm("sy", a, b))
+                p = mm(4 * (at % 2) + e, V("wq", 128 * e, 128 * e + 128), V("wsc", 128 * e, 128 * e + 128), nm("qy", a, b), nm("sy", a, b))
                 r = nm("ru", 4 * a + e, 4 * b, 4)
                 act(r, p, Fn.Relu, scale=0.03125)
                 mark("r%d%d" % (t, c))
@@ -705,8 +848,9 @@ def plan(g, core, T, topo, rank, room):
     for c in range(len(CHUNKS[2]) - 1):
         a, b = CHUNKS[2][c], CHUNKS[2][c + 1]
         quant(V("qx2", a, b), V("sx2", a, b), V("x2", 4 * a, 4 * b))
-        p = mm(c % 2, whole("qv"), whole("sv"), V("qx2", a, b), V("sx2", a, b))
-        move("a", V("ysb", a, b), p)
+        mark("x2%d" % c)
+        p = mm(4 + c, whole("qv"), whole("sv"), V("qx2", a, b), V("sx2", a, b))
+        move(LAST[c], V("ysb", a, b), p)
         dma("s", lambda a=a, b=b: g.sync.dma_start(T.oc[:, 4 * a:4 * b], T.qx2[:, a:b].bitcast(dt.uint8)), [V("qx2", a, b)], [], 2300)
         dma("s", lambda a=a, b=b: g.sync.dma_start(T.y[:, a:b], T.ysb[:, a:b]), [V("ysb", a, b)], [], 2300)
     for j in range(4):

@@ -1,28 +1,30 @@
 import math
 import numpy as np
+from concourse.bass import DstId, RemoteDMATransfer
 from concourse.mybir import dt, AluOpType as Op, ActivationFunctionType as Fn
 
 C, A = 352, 64
 NS = (C, C + A, C + 2 * A)
-RUNS = ((0, 192, 352), (0, 208, 416))
 CHUNKS = ((0, 192, 352), (0, 160, 288, 416), (0, 160, 320, 480))
 BY_DMA = ((0,), (0,))
-BLEND = ("vvv", "vvv")
 TT2 = 2.0
-JOIN = (1, 1)
+PICKS = ("aaa", "vaa")
 PARENTS = ("aaa", "aaa")
-LAST = "aav"
-ORDER = ((0, 1), (0, 1, 2), (0, 1, 2))
+LAST = "vaa"
 READY = ((0, 1), (1, 0, 2))
+SELECT = (0, 1)
+SHARE = ((0.5, 0.75, 0.5), (0.5, 0.5, 0.5))
+FOUR = "a" * 16
 BIG = 2.0 ** 90
 HOLD = 2.0 ** 24
 KEEP = 4096.0
+BELOW, WHOLE = 4096 * 768, 1.5 * 2 ** 23
 X4 = "float8_e4m3fn_x4"
-DMAS = 40
+DMAS = 48
 
 SCRATCH = {
-    "wf": ("sbuf", [128, 16384], "float32"), "wb": ("sbuf", [128, 29696], "bfloat16"),
-    "wi": ("sbuf", [128, 1024], "int32"), "wu": ("sbuf", [128, 1024], "uint16"),
+    "wf": ("sbuf", [128, 21504], "float32"), "wb": ("sbuf", [128, 27648], "bfloat16"),
+    "wi": ("sbuf", [128, 1024], "int32"), "wu": ("sbuf", [128, 1536], "uint16"),
     "ps": ("psum", [128, 4096], "float32"),
     "pai": ("sbuf", [128, 22], "int32"), "nri": ("sbuf", [128, 32], "int32"),
     "ub": ("sbuf", [128, 512], "bfloat16"), "vb": ("sbuf", [128, 512], "bfloat16"),
@@ -31,7 +33,7 @@ SCRATCH = {
     "qv": ("sbuf", [128, 128], X4), "sv": ("sbuf", [128, 128], "uint8"),
     "wq": ("sbuf", [128, 512], X4), "wsc": ("sbuf", [128, 512], "uint8"),
     "repi": ("sbuf", [128, 8], "int32"), "repu": ("sbuf", [128, 8], "uint16"),
-    "one": ("sbuf", [128, 528], "bfloat16"), "eye": ("sbuf", [128, 528], "bfloat16"),
+    "one": ("sbuf", [128, 912], "bfloat16"), "eye": ("sbuf", [128, 528], "bfloat16"),
     "qe": ("sbuf", [128, 512], X4), "se": ("sbuf", [128, 512], "uint8"),
     "x2": ("sbuf", [128, 4 * NS[2]], "bfloat16"),
     "qx2": ("sbuf", [128, NS[2]], X4), "sx2": ("sbuf", [128, NS[2]], "uint8"),
@@ -40,36 +42,39 @@ SCRATCH = {
 for _t in range(2):
     _n, _m = NS[_t], NS[_t + 1]
     SCRATCH.update({
-        "x%d" % _t: ("sbuf", [128, 4 * _m], "bfloat16"), "xh%d" % _t: ("sbuf", [128, 4 * _m], "bfloat16"),
-        "xo%d" % _t: ("sbuf", [128, 4 * _m], "bfloat16"),
+        "x%d" % _t: ("sbuf", [128, 4 * _m], "bfloat16"),
         "yt%d" % _t: ("sbuf", [128, 4 * _m], "bfloat16"), "ru%d" % _t: ("sbuf", [128, 4 * _m], "float32"),
         "dd%d" % _t: ("sbuf", [128, 4 * _n], "bfloat16"),
         "qx%d" % _t: ("sbuf", [128, _n], X4), "sx%d" % _t: ("sbuf", [128, _n], "uint8"),
         "qh%d" % _t: ("sbuf", [128, 128], X4), "sh%d" % _t: ("sbuf", [128, 128], "uint8"),
         "qy%d" % _t: ("sbuf", [128, _m], X4), "sy%d" % _t: ("sbuf", [128, _m], "uint8"),
-        "rq%d" % _t: ("sbuf", [128, 224], X4), "rs%d" % _t: ("sbuf", [128, 224], "uint8"),
+        "rq%d" % _t: ("sbuf", [128, _n // 2], X4), "rs%d" % _t: ("sbuf", [128, _n // 2], "uint8"),
         "lq%d" % _t: ("sbuf", [128, _n], X4), "ls%d" % _t: ("sbuf", [128, _n], "uint8"),
         "el%d" % _t: ("sbuf", [128, 16], "uint16"), "rl%d" % _t: ("sbuf", [128, 16], "uint16"),
         "ll%d" % _t: ("sbuf", [128, 16], "uint16"),
     })
+    if SELECT[_t]:
+        SCRATCH.update({"sm%d" % _t: ("sbuf", [128, 4 * _n + 1024], "bfloat16"), "hh%d" % _t: ("sbuf", [128, 1024], "bfloat16")})
+    else:
+        SCRATCH.update({"xh%d" % _t: ("sbuf", [128, 4 * _m], "bfloat16"), "xo%d" % _t: ("sbuf", [128, 4 * _m], "bfloat16")})
 SEMAPHORES = (["ev", "ea", "ep", "eg", "sent"] + ["dm%d" % _i for _i in range(DMAS)]
               + ["%s%d" % (_s, _t) for _s in ("rc", "rp", "rn", "aq", "an") for _t in range(2)])
 
 CY, WAKE = 0.92, 170.0
 LAT = (12000.0, 4300.0, 1900.0)
 HOLDS = (1100.0, 1300.0, 1.25)
-PIECES = (1, 1)
 SCALAR = (((3, 2), (1, 2)), ((3, 3), (1, 2)))
-JUMPS = ("vaaaaaaa", "aaaaaaaa")
+SORT = (2, 2)
+JUMPS = ("aaaaaaaa", "aaaaaaaa")
 LOW = 5
 PAR0 = "v"
 FULL = (5, 9)
-WINS = (3, 2)
 SPLIT = 2
-SPREAD = "aaaaa"
-HALVE = ("aaaa", "aaaa")
-TRIES, SLACK, SEED, ORDERED = 40000, 30.0, 1, []
-SCORES = ("v", "a")
+SPREAD = ("cas", "4sss", "4ss", "6")
+SCORES = ("vv", "vaa")
+SPEEDS = ((1, 1, 1), (1.3, 1.48, 1.7), (0.93, 0.78, 0.62))
+WEIGH = (0.35, 0.27, 0.33)
+TRIES, SLACK, SEED, ORDERED = (2500, 90000), (15.0, 30.0), 2, []
 EARLY = {"r11": 3000, "c04": 1000, "u15": 1000, "q02": 1000, "x11": 1500, "u14": 1500, "u16": 1000, "u17": 1500, "u02": 8000, "c03": 1500,
          "c15": 600, "u03": 1000, "c00": 8000, "r00": 1000, "y01": 2000, "c11": 600, "c14": 1000, "c12": 300, "b01": 2000, "u12": 2000,
          "q00": 1500, "r01": 600, "b10": 8000, "k0": 2000, "y11": 2000, "e0": 2000, "m01": 8000, "q10": 2000, "o0": 5000, "u05": 1000,
@@ -88,10 +93,10 @@ def relay_program(g, core, T, topo, r, k):
     nin = len(topo.engines(T.cores[r], core))
     calls = 0
     for t in range(2):
-        a, b = RUNS[t][k], RUNS[t][k + 1]
-        g.wait_ge(T.sem["rc%d" % t], nin)
+        a, b = k * NS[t] // 2, (k + 1) * NS[t] // 2
+        g.wait_ge(T.sem["rc%d" % t], nin // 2)
         g.remote_dma(T["lq%d" % t][:, a:b].bitcast(dt.uint8), T["rq%d" % t][:, 0:b - a].bitcast(dt.uint8), T.sem["aq%d" % t], T.sem.sent, pid, rid, m)
-        g.wait_ge(T.sem["rp%d" % t], nin)
+        g.wait_ge(T.sem["rp%d" % t], nin // 2)
         g.remote_dma(T["ls%d" % t][:, a:b], T["rs%d" % t][:, 0:b - a], T.sem["aq%d" % t], T.sem.sent, pid, rid, m)
         calls += 2
         if k == 0:
@@ -151,31 +156,6 @@ def link(ops):
         o["deps"] = sorted(d)
 
 
-def schedule(ops):
-    n = len(ops)
-    level = [0.0] * n
-    for i in range(n - 1, -1, -1):
-        level[i] += ops[i]["cost"] + ops[i]["lat"] + EARLY.get(ops[i].get("mark"), 0.0)
-        for j in ops[i]["deps"]:
-            level[j] = max(level[j], level[i] + WAKE)
-    busy, done = {}, [0.0] * n
-    for i in sorted(range(n), key=lambda i: (-level[i], i)):
-        o = ops[i]
-        t0 = max([done[j] + WAKE for j in o["deps"]] + [0.0])
-        if o["q"] != "x":
-            line = busy.setdefault(o["q"], [])
-            k = 0
-            while k < len(line):
-                if t0 + o["cost"] <= line[k][0]:
-                    break
-                t0 = max(t0, line[k][1])
-                k += 1
-            line.insert(k, (t0, t0 + o["cost"], i))
-        o["start"] = t0
-        done[i] = t0 + o["cost"] + o["lat"]
-    return sorted(range(n), key=lambda i: (ops[i]["start"], i)), max(done)
-
-
 def thin(ops):
     above = []
     for o in ops:
@@ -184,21 +164,100 @@ def thin(ops):
             if not seen >> j & 1:
                 kept.append(j)
             seen |= above[j] | 1 << j
-        above.append(seen)
+        above.append(0 if o["kind"] in "xr" else seen)
         o["deps"] = kept
+
+
+def blocked(done, why):
+    i, pairs = done.index(max(done)), []
+    while i >= 0:
+        w = why[i]
+        if w <= -2:
+            pairs.append((-2 - w, i))
+        i = -2 - w if w <= -2 else w
+    return pairs
+
+
+def favour(ops, tries):
+    n = len(ops)
+    q, cost, deps = ["xvapgs".index(o["q"]) for o in ops], [o["cost"] for o in ops], [o["deps"] for o in ops]
+    own = [o["cost"] + o["lat"] + WAKE for o in ops]
+
+    def build(more):
+        level = [0.0] * n
+        for i in range(n - 1, -1, -1):
+            x = level[i] = level[i] + own[i] + more[i]
+            for j in deps[i]:
+                if level[j] < x:
+                    level[j] = x
+        lines = [([], [], []) for k in range(6)]
+        start, done, why = [0.0] * n, [0.0] * n, [-1] * n
+        for i in sorted(range(n), key=lambda i: -level[i]):
+            t, w = 0.0, -1
+            for j in deps[i]:
+                if done[j] > t:
+                    t, w = done[j], j
+            if q[i]:
+                c, (s, e, who) = cost[i], lines[q[i]]
+                p, m = 0, len(s)
+                hi = m
+                while p < hi:
+                    mid = (p + hi) // 2
+                    if e[mid] > t:
+                        hi = mid
+                    else:
+                        p = mid + 1
+                while p < m and t + c > s[p]:
+                    t, w = e[p], -2 - who[p]
+                    p += 1
+                s.insert(p, t)
+                e.insert(p, t + c)
+                who.insert(p, i)
+            start[i], done[i], why[i] = t, t + own[i], w
+        return max(done), start, done, why
+    draw = np.random.default_rng(SEED)
+    more = [EARLY.get(o.get("mark"), 0.0) for o in ops]
+    now = best = build(more)
+    for it in range(tries):
+        pairs = blocked(now[2], now[3])
+        a, b, c, d = draw.random(4)
+        u, v = pairs[int(a * len(pairs))]
+        step = 60.0 * math.exp(4.5 * c)
+        x = v if b < 0.55 or more[u] <= 1.0 - own[u] else u
+        old = more[x]
+        more[x] = old + step if x == v else max(old - step, 1.0 - own[x])
+        new = build(more)
+        if new[0] <= now[0] or d < math.exp((now[0] - new[0]) / (SLACK[0] * (1 - it / tries) + 1)):
+            now = new
+            if now[0] < best[0]:
+                best = now
+        else:
+            more[x] = old
+    return sorted(range(n), key=lambda i: (best[1][i], i)), best[0] - WAKE
 
 
 def exchange(ops, order, tries):
     n = len(ops)
-    q, cost = ["xvapgs".index(o["q"]) for o in ops], [o["cost"] for o in ops]
-    tail, deps, after = [o["cost"] + o["lat"] + WAKE for o in ops], [o["deps"] for o in ops], [[] for o in ops]
+    q, deps, after = ["xvapgs".index(o["q"]) for o in ops], [o["deps"] for o in ops], [[] for o in ops]
+    cases = [([o["costs"][c] for o in ops], [o["costs"][c] + o["lat"] + WAKE for o in ops]) for c in range(len(WEIGH))]
     for i in range(n):
         for j in deps[i]:
             after[j].append(i)
 
-    def times(seq):
-        free, last, start, done, why = [0.0] * 6, [-1] * 6, [0.0] * n, [0.0] * n, [-1] * n
-        for i in seq:
+    def beside(seq, k, step):
+        out, left = [-1] * 6, 5
+        while 0 <= k < n and left:
+            i = seq[k]
+            if q[i] and out[q[i]] < 0:
+                out[q[i]] = i
+                left -= 1
+            k += step
+        return out
+
+    def heads(part, last, case, start, done, why):
+        cost, tail = case
+        free, last = [start[i] + cost[i] if i >= 0 else 0.0 for i in last], last[:]
+        for i in part:
             t, w, k = 0.0, -1, q[i]
             for j in deps[i]:
                 if done[j] > t:
@@ -208,22 +267,77 @@ def exchange(ops, order, tries):
                     t, w = free[k], -2 - last[k]
                 free[k], last[k] = t + cost[i], i
             start[i], done[i], why[i] = t, t + tail[i], w
-        return start, done, why
-    draw = np.random.default_rng(SEED)
+
+    def tails(part, nxt, case, rest):
+        cost, tail = case
+        ahead = [rest[i] if i >= 0 else 0.0 for i in nxt]
+        for i in reversed(part):
+            t, k = 0.0, q[i]
+            for j in after[i]:
+                if rest[j] > t:
+                    t = rest[j]
+            t += tail[i]
+            if k:
+                if ahead[k] + cost[i] > t:
+                    t = ahead[k] + cost[i]
+                ahead[k] = t
+            rest[i] = t
+
+    def onward(seq, k, last, reach, case, start, done, why, log):
+        cost, tail = case
+        free, last, moved = [start[i] + cost[i] if i >= 0 else 0.0 for i in last], last[:], [c > 0 and c in here for c in range(6)]
+        while k < n and (k <= reach or True in moved):
+            i = seq[k]
+            t, w, c = 0.0, -1, q[i]
+            for j in deps[i]:
+                if done[j] > t:
+                    t, w = done[j], j
+            if c:
+                if free[c] > t:
+                    t, w = free[c], -2 - last[c]
+                free[c], last[c], moved[c] = t + cost[i], i, t != start[i]
+            if t != start[i] or w != why[i]:
+                log.append((i, start[i], done[i], why[i]))
+                if t != start[i]:
+                    for j in after[i]:
+                        if pos[j] > reach:
+                            reach = pos[j]
+                start[i], done[i], why[i] = t, t + tail[i], w
+            k += 1
+
+    def backward(seq, k, nxt, reach, case, rest):
+        cost, tail = case
+        ahead, moved = [rest[i] if i >= 0 else 0.0 for i in nxt], [c > 0 and c in here for c in range(6)]
+        while k >= 0 and (k >= reach or True in moved):
+            i = seq[k]
+            t, c = 0.0, q[i]
+            for j in after[i]:
+                if rest[j] > t:
+                    t = rest[j]
+            t += tail[i]
+            if c:
+                if ahead[c] + cost[i] > t:
+                    t = ahead[c] + cost[i]
+                ahead[c], moved[c] = t, t != rest[i]
+            if t != rest[i]:
+                rest[i] = t
+                for j in deps[i]:
+                    if pos[j] < reach:
+                        reach = pos[j]
+            k -= 1
+    draw = np.random.default_rng(SEED).random((tries, 5)).tolist()
     seq = list(order)
-    start, done, why = times(seq)
-    now = max(done)
-    best = (now, seq)
+    res = [[[0.0] * n, [0.0] * n, [-1] * n, [0.0] * n] for c in cases]
+    for c, r in zip(cases, res):
+        heads(seq, [-1] * 6, c, r[0], r[1], r[2])
+        tails(seq, [-1] * 6, c, r[3])
+    now = sum(w * max(r[1]) for w, r in zip(WEIGH, res))
+    best, taken = (now, list(seq)), 0
+    pairs, pos = [blocked(r[1], r[2]) for r in res], {x: k for k, x in enumerate(seq)}
     for it in range(tries):
-        i, pairs = done.index(now), []
-        while i >= 0:
-            w = why[i]
-            if w <= -2:
-                pairs.append((-2 - w, i))
-            i = -2 - w if w <= -2 else w
-        a, b, c, d, e = draw.random(5)
-        u, v = pairs[int(a * len(pairs))]
-        pos = {x: k for k, x in enumerate(seq)}
+        a, b, c, d, e = draw[it]
+        p = pairs[it % len(cases)]
+        u, v = p[int(a * len(p))]
         if b < 0.65:
             x, hi = (v, pos[u]) if b < 0.5 else (u, pos[u] - 1)
             lo = max([pos[j] for j in deps[x]] + [-1]) + 1
@@ -235,29 +349,55 @@ def exchange(ops, order, tries):
         if lo > hi:
             continue
         k = near if near is not None and c < 0.5 else lo + int(d * (hi - lo + 1))
-        new = list(seq)
-        new.pop(pos[x])
-        new.insert(k, x)
-        s2, d2, w2 = times(new)
-        t = max(d2)
-        if t <= now or e < math.exp((now - t) / (SLACK * (1 - it / tries) + 1)):
-            start, done, why, now = s2, d2, w2, t
-            pos = {x: k for k, x in enumerate(new)}
-            seq = sorted(new, key=lambda x: (start[x], pos[x]))
-            if now < best[0]:
-                best = (now, seq)
-    start = times(best[1])[0]
-    for i in range(n):
-        ops[i]["start"] = start[i]
-    return best[1], best[0] - WAKE
+        px = pos[x]
+        k0, k1, part = (k, px, [x] + seq[k:px]) if k < px else (px, k, seq[px + 1:k + 1] + [x])
+        bar = now - math.log(e + 1e-12) * (SLACK[1] * (1 - it / tries) + 1)
+        last, nxt = beside(seq, k0 - 1, -1), beside(seq, k1 + 1, 1)
+        kept, t = [[[row[i] for i in part] for row in r] for r in res], 0.0
+        for w, cs, r in zip(WEIGH, cases, res):
+            heads(part, last, cs, r[0], r[1], r[2])
+            tails(part, nxt, cs, r[3])
+            t += w * max(r[0][i] + r[3][i] for i in part)
+        logs = [[] for cs in cases]
+        if t <= bar:
+            here, reach = {q[i]: i for i in part}, max([pos[j] for i in part for j in after[i]] + [k1])
+            for cs, r, log in zip(cases, res, logs):
+                onward(seq, k1 + 1, [here.get(c, last[c]) for c in range(6)], reach, cs, r[0], r[1], r[2], log)
+            t = sum(w * max(r[1]) for w, r in zip(WEIGH, res))
+        if t > bar:
+            for r, log in zip(res, logs):
+                for i, x0, x1, x2 in log:
+                    r[0][i], r[1][i], r[2][i] = x0, x1, x2
+            for r, old in zip(res, kept):
+                for row, vals in zip(r, old):
+                    for i, y in zip(part, vals):
+                        row[i] = y
+            continue
+        seq[k0:k1 + 1] = part
+        now, taken = t, taken + 1
+        here, reach = {q[i]: i for i in reversed(part)}, min([pos[j] for i in part for j in deps[i]] + [k0])
+        for cs, r in zip(cases, res):
+            backward(seq, k0 - 1, [here.get(c, nxt[c]) for c in range(6)], reach, cs, r[3])
+        if taken % 8:
+            for k, i in enumerate(part):
+                pos[i] = k0 + k
+        else:
+            seq.sort(key=lambda x: res[0][0][x])
+            pos = {x: k for k, x in enumerate(seq)}
+        pairs = [blocked(r[1], r[2]) for r in res]
+        if now < best[0]:
+            best = (now, list(seq))
+    return best[1], best[0]
 
 
 def emit(g, T, ops):
-    link(ops)
-    thin(ops)
     if not ORDERED:
-        ORDERED.append(exchange(ops, schedule(ops)[0], TRIES)[0])
+        link(ops)
+        thin(ops)
+        ORDERED.extend([exchange(ops, favour(ops, TRIES[0])[0], TRIES[1])[0], [o["deps"] for o in ops]])
     order = ORDERED[0]
+    for o, d in zip(ops, ORDERED[1]):
+        o["deps"] = d
     queue = {"v": g.vector, "a": g.scalar, "p": g.tensor, "g": g, "s": g.sync}
     count, seen, dmas = {"v": 0, "a": 0, "p": 0, "g": 0}, {}, 0
     sent = 0
@@ -275,6 +415,8 @@ def emit(g, T, ops):
             continue
         need = {}
         for j in o["deps"]:
+            if ops[j]["kind"] == "r":
+                continue
             s, v = ops[j]["sig"]
             need[s] = max(need.get(s, 0), v)
         for s in sorted(need):
@@ -321,7 +463,10 @@ def plan(g, core, T, topo, rank, room):
         for v in r:
             if isinstance(v, tuple):
                 rr += list(v) if len(v) == 2 else [v]
-        ops.append(dict(q=q, kind=kind, fn=fn, r=rr, w=list(w), cost=cost * (HOLDS[2] if q + kind == "gc" else 1), lat=lat, after=list(after), **more))
+        cost *= HOLDS[2] if q + kind == "gc" else 1
+        way = more.pop("way", int(len(rr) > sum(isinstance(v, tuple) for v in r)))
+        costs = [cost * (1 if kind != "c" or q == "p" else s[way]) for s in SPEEDS]
+        ops.append(dict(q=q, kind=kind, fn=fn, r=rr, w=list(w), cost=cost, costs=costs, lat=lat, after=list(after), **more))
         return len(ops) - 1
 
     def price(out, ins, two=False):
@@ -347,7 +492,7 @@ def plan(g, core, T, topo, rank, room):
         add("v", "c", lambda: g.vector.tensor_copy(ap(out), ap(a)), [a], [out], price(out, [a]))
 
     def scatter(win, off, a):
-        add("v", "c", lambda: g.vector.tensor_copy(ap((win, off)), ap(a)), [a, off], [win], 50 + 3.8 * CY * size(a))
+        add("v", "c", lambda: g.vector.tensor_copy(ap((win, off)), ap(a)), [a, off], [win], 50 + 3.8 * CY * size(a), way=2)
 
     def scan(out, d0, d1, op0, op1, first=0.0):
         add("v", "c", lambda: g.vector.tensor_tensor_scan(ap(out), ap(d0), ap(d1), sc(first), op0, op1), [d0, d1, first], [out], price(out, [d0, d1]))
@@ -379,8 +524,7 @@ def plan(g, core, T, topo, rank, room):
             fn = lambda: g.iota(ap(out), pattern, base, cm, allow_small_or_imprecise_dtypes=True)
         add("g", "c", fn, [], [out], 130 + 2 * CY * size(out))
 
-    def keep(out, a, pattern=None, k=0.0):
-        pattern, base = pattern or [[0, size(out)]], 0 if pattern else 1
+    def keep(out, a, pattern, k=0.0, base=0):
         add("g", "c", lambda: g.affine_select(ap(out), ap(a), pattern, Op.not_equal, k, base, 0), [a], [out], 170 + 2 * CY * size(out))
 
     def quant(q, s, a):
@@ -397,8 +541,8 @@ def plan(g, core, T, topo, rank, room):
     def twin(out, a, gate):
         dma("s", lambda: g.sync.dma_start(ap(out), ap(a)), [a, gate], [out], 3500)
 
-    def heap(out, a, lat):
-        add("g", "d", lambda: g.dma_start(ap(out), ap(a), accum_op=Op.add), [a, out], [out], HOLDS[1], lat)
+    def heap(out, a, lat, after=()):
+        add("g", "d", lambda: g.dma_start(ap(out), ap(a), accum_op=Op.add), [a, out], [out], HOLDS[1], lat, after)
 
     def u8(v):
         return ap(v).bitcast(dt.uint8)
@@ -409,11 +553,18 @@ def plan(g, core, T, topo, rank, room):
     rl = relays_of(T, topo, rank)
     ne = len(topo.engines(rl[0], T.cores[(rank + 1) % len(T.cores)]))
 
-    def hand(k, dst, src, sem, codes=False):
-        rid, pid = topo.addr(rl[k], core)
-        f = u8 if codes else ap
-        return add("g", "r", lambda: g.remote_dma(f(dst), f(src), T.sem[sem], T.sem.sent, pid, rid, topo.mask(core, rl[k])), [src], [], HOLDS[0],
-                   inc=len(topo.engines(core, rl[k])))
+    def hand(dst, src, sem):
+        rid, pid = topo.addr(rl[0], core)
+        return add("g", "r", lambda: g.remote_dma(ap(dst), ap(src), T.sem[sem], T.sem.sent, pid, rid, topo.mask(core, rl[0])), [src], [], HOLDS[0],
+                   inc=len(topo.engines(core, rl[0])))
+
+    def both(dst, src, sem, f):
+        every, n = topo.engines(core, rl[0]), size(dst)
+        to = [topo.addr(c, core) for c in rl]
+        fn = lambda: g.remote_dma_fused([RemoteDMATransfer(dst_ids=[DstId(rid=to[k][0], pnc=to[k][1])], dma_engine_mask=sum(1 << e for e in every[k::2]),
+                                                           remote_sem=T.sem[sem], src=f(sub(src, k * n, k * n + n)), dst=f(dst)) for k in range(2)],
+                                        local_sem=T.sem.sent)
+        return add("g", "r", fn, [src], [], HOLDS[0] + 200, inc=len(every))
 
     def arrival(after, w, sem, v, lat):
         add("x", "x", None, [], w, 0.0, lat, after=after, sig=(sem, v))
@@ -429,48 +580,51 @@ def plan(g, core, T, topo, rank, room):
     dma("s", lambda: g.sync.dma_start(T.wsc[:], T.ws[:]), gate, [whole("wsc")], 2500)
     dma("s", lambda: g.sync.dma_start(T.vb[:], T.v[:]), [whole("wsc")], [whole("vb")], 3500)
 
-    pi, cols, cf = new("wi", 1), new("wi", 4), new("wf", 16)
-    col = lambda k: sub(cf, k, k + 1)
-    fill(col(14), 0.5)
-    fill(col(15), -0.5)
-    fill(col(12), 256.0)
+    pi, cols, cf = new("wi", 1), new("wi", 4), new("wf", 17)
     iota(pi, [[1, 1]], 0, 1)
     ts(sub(cols, 0, 1), pi, 15, Op.bitwise_and)
     ts(sub(cols, 1, 2), pi, 2, Op.logical_shift_right, 3, Op.bitwise_and)
     ts(sub(cols, 2, 3), pi, 3, Op.bitwise_and)
     cp(sub(cf, 0, 3), sub(cols, 0, 3))
-    q16, q4, qt, q16n, q4n, s16, s4p, s4y, qto, s16y, s4, qty = [col(k) for k in range(12)]
+    q16, q4, qt, q16n, q4n, s16, s4p, s4y, qto, s16y, s4, qty, s4z, s16k, qtz, s16r, s16h = [sub(cf, k, k + 1) for k in range(17)]
     ts(sub(cf, 3, 5), sub(cf, 0, 2), 1.0, Op.add)
     ts(s16, q16, 15.0, Op.is_equal, 1.0 / HOLD, Op.max)
     ts(s16y, s16, 512.0, Op.mult)
+    ts(s16k, s16, -512.0 * 1024.0, Op.mult)
+    ts(s16r, q16, 15.0, Op.is_lt, HOLD - 1.0, Op.mult)
+    ts(s16r, s16r, 1.0, Op.add, -1.0 / (512.0 * 1024.0), Op.mult)
+    ts(s16h, s16, 1.0 / 512, Op.mult)
     ts(s4, q4, 3.0, Op.is_equal, 1.0 / HOLD, Op.max)
     ts(s4p, s4, 4.0, Op.mult)
     ts(s4y, s4, 2048.0, Op.mult)
+    ts(s4z, s4, 1.0 / 1024, Op.mult)
+    ts(qtz, qt, BELOW / 1024 + 0.01, Op.add)
     ts(qto, qt, 0.25, Op.add)
     ts(qty, qt, 1024.25, Op.add)
-    jf, jc, rr = new("wf", 416), new("wb", 352), new("wb", 32)
+    jf, rr = new("wf", 416), new("wb", 32)
     r16, r4 = sub(rr, 0, 16), sub(rr, 16, 32)
     iota(r16, [[1, 16]])
-    iota(jc, [[1, 352]], -256)
     iota(r4, [[0, 4], [1, 4]])
     iota(jf, [[1, 416]])
-    ones = V("one", 0, 528)
-    fill(ones, 1.0)
+    ones, zeros, lut64 = V("one", 0, 528), V("one", 768, 912), V("one", 704, 912)
+    fill(V("one", 0, 768), 1.0)
+    fill(zeros, 0.0)
     qoff = new("wu", 30)
     ts(qoff, sub(ones, 0, 30), q16, Op.mult)
 
-    def spread(p, n, who="a"):
-        m, w = new(p[0], n), 16
-        if who != "g":
-            for lo in range(0, n, 192):
-                hi = min(n, lo + 192)
-                move(who, sub(m, lo, hi), (p, sub(qoff, 0, (hi - lo) // 16)))
-            return m
-        for lo in (0, 16):
-            keep(sub(m, lo, lo + 16), p)
-        while 2 * w < n:
-            w *= 2
-            keep(sub(m, w, min(2 * w, n)), sub(m, 0, min(w, n - w)))
+    def const(out, k):
+        keep(out, sub(ones, 0, size(out)), [[0, size(out)]], k)
+
+    def spread(p, n, how):
+        m, w = new(p[0], n), min(n, 16 * int(how[0], 16))
+        act(sub(m, 0, w), (p, sub(qoff, 0, w // 16)), Fn.Copy)
+        for who in how[1:]:
+            hi = min(n, 2 * w)
+            if who == "s":
+                twin(sub(m, w, hi), sub(m, 0, hi - w), sub(m, 0, 16))
+            else:
+                move(who, sub(m, w, hi), sub(m, 0, hi - w))
+            w = hi
         return m
 
     def hold(r, q, qn):
@@ -478,34 +632,25 @@ def plan(g, core, T, topo, rank, room):
         ts(a, r, q, Op.not_equal)
         ts(b, r, qn, Op.is_equal, HOLD, Op.mult)
         tt(m, a, b, Op.max)
-        return m, a
-    p16, poff = hold(r16, q16, q16n)
-    p4, _ = hold(r4, q4, q4n)
+        return m
+    p16, p4 = hold(r16, q16, q16n), hold(r4, q4, q4n)
     pdiag, w16, gt = new("wb", 16), new("wb", 16), new("wf", 256)
     ts(pdiag, r16, q16, Op.is_equal)
     ts(w16, r16, q16, Op.is_ge, -0.5, Op.add)
-    act(gt, sub(ones, 0, 256), Fn.Copy, scale=0.0)
+    act(sub(gt, 0, 256, 4), sub(zeros, 0, 64), Fn.Copy)
     most = 16 * max(sum(x) for y in SCALAR for x in y)
-    m16, m4, off16, diag, ws16 = [spread(p, n, who) for p, n, who in zip((p16, p4, poff, pdiag, w16), (416, 480, 208, 208, most), SPREAD)]
-    ns16, big4 = new("wb", most), new("wb", 128)
-    keep(ns16, sub(ones, 0, most), [[0, most // 16], [1, 16]])
-    keep(big4, sub(gt, 0, 128), [[0, 32], [1, 4]], BIG)
-    mr = {}
-    for h in (176, 208, 128):
-        mr[h] = new("wb", h + 16)
-        cp(sub(mr[h], 0, 16), poff)
-        act(sub(mr[h], 16, h), sub(ones, 16, h), Fn.Copy)
-        ts(sub(mr[h], h, h + 16), pdiag, KEEP, Op.mult, 1.0, Op.max)
-    lut64, lutb = new("wb", 416), new("wb", 16)
-    act(sub(lut64, 0, 128), sub(ones, 0, 128), Fn.Copy)
-    act(sub(lut64, 128, 416), sub(ones, 128, 416), Fn.Copy, scale=0.0)
-    ts(lutb, sub(jf, 0, 16), -BIG, Op.mult, BIG, Op.add)
+    m16, m4, diag, ws16 = [spread(p, n, how) for p, n, how in zip((p16, p4, pdiag, w16), (416, 480, 208, most), SPREAD)]
+    ns16, big4 = new("wb", 208), new("wb", 128)
+    keep(ns16, sub(ones, 0, 208), [[0, 13], [1, 16]])
+    keep(big4, sub(zeros, 0, 128), [[0, 32], [1, 4]], BIG)
+    ts(V("one", 528, 544), pdiag, KEEP, Op.mult, 1.0, Op.max)
+    ts(V("one", 544, 560), pdiag, 1.0 / KEEP - 1.0, Op.mult, 1.0, Op.add)
     m16i, xi, xf, kh = new("wi", 16), new("wi", 16), new("wf", 16), new("wf", 4)
     iota(m16i, [[16, 16]])
     ts(xf, m16i, q16, Op.add)
     cp(xi, xf)
     ts(kh, sub(xf, 0, 4), 0.5, Op.add)
-    add("g", "c", lambda: g.affine_select(T.eye[:], T.one[:], [[1, 528]], Op.is_equal, 0.0, -3, -4), [ones], [whole("eye")], 170 + 2 * CY * 528)
+    add("g", "c", lambda: g.affine_select(T.eye[:], T.one[:, 0:528], [[1, 528]], Op.is_equal, 0.0, -3, -4), [ones], [whole("eye")], 170 + 2 * CY * 528)
     for b in range(4):
         quant(V("qe", 128 * b, 128 * b + 128), V("se", 128 * b, 128 * b + 128), V("eye", 3 - b, 515 - b))
     iota(whole("repi"), [[16, 8]])
@@ -519,18 +664,16 @@ def plan(g, core, T, topo, rank, room):
     qr, sr = whole("qr"), whole("sr")
     nru, nrf = new("wu", 32), new("wf", 32)
     cp(nru, whole("nri"))
-    ts(nrf, whole("nri"), 256.0, Op.mult)
+    ts(nrf, whole("nri"), 512.0, Op.mult)
 
     def diagonals(h, lo, hi):
-        if not lo + hi:
-            return None
-        a, o = new("wf", lo + hi), new("wu", lo + hi)
-        for c0, c1, base in ((0, lo, 0), (lo, lo + hi, h - 16 * (lo + hi))):
-            if c1 > c0:
-                ts(sub(a, c0, c1), sub(jf, c0, c1), h + 16.0, Op.mult, float(base), Op.add)
+        a, o, first = new("wf", lo + hi), new("wu", lo + hi), new("wb", 16 * (lo + hi))
+        for c0, c1, m in ((0, lo, 0), (lo, lo + hi, h // 16 - hi)):
+            iota(sub(a, c0, c1), [[h + 16, c1 - c0]], c0 * h + 16 * m)
+            iota(sub(first, 16 * c0, 16 * c1), [[16, c1 - c0], [0, 16]], 16 * m)
         ts(o, a, q16, Op.add)
-        return o
-    diags = {(h, x): diagonals(h, *x) for h, x in set([(NS[t] // 2, SCALAR[t][0]) for t in range(2)] + [(128, SCALAR[t][1]) for t in range(2)])}
+        return o, first
+    diags = {(h, x): diagonals(h, *x) for h, x in sorted(set([(NS[t] // 2, SCALAR[t][0]) for t in range(2)] + [(128, SCALAR[t][1]) for t in range(2)]))}
 
     def ranks(row, lst, h, share, out):
         k, (lo, hi) = h // 16, share
@@ -540,102 +683,110 @@ def plan(g, core, T, topo, rank, room):
         for i in range(nv):
             m = lo + i
             f = sub(fl, i * w, i * w + w)
-            ts(sub(f, 0, h - 16 * m), sub(row, 16 * m, h), at(m), Op.is_lt)
-            ts(sub(f, h - 16 * m, w), sub(row, 0, 16 * m + 16), at(m), Op.is_le)
-            scan(sub(cnt, i * w, i * w + w), mr[h], f, Op.mult, Op.add)
-        ts(sub(out, lo, lo + nv), sub(cnt, w - 1, nv * w, w), 2.0 / KEEP, Op.mult, 0.25, Op.add)
-        sg, junk, acc = new("wb", max(na, 1) * h), new("wb", max(na, 1) * h), new("wf", 32)
-        ib, ibs, t1 = new("wb", 128), new("wb", 128), new("wf", 16)
-        if na:
-            ms = list(range(lo)) + list(range(k - hi, k))
-            for a, m in enumerate(ms):
-                act(sub(sg, a * h, a * h + h), row, Fn.Sign, bias=at(m), scale=-1.0)
-            tt(sub(ib, 0, 16 * na), (sg, diags[(h, share)]), sub(ws16, 0, 16 * na), Op.is_gt)
-            scan(sub(ibs, 0, 16 * na), sub(ns16, 0, 16 * na), sub(ib, 0, 16 * na), Op.mult, Op.add)
-            ts(sub(t1, 0, na), sub(ibs, 15, 16 * na, 16), 2.0, Op.mult, h - 15.75, Op.add)
-            for a, m in enumerate(ms):
-                y, sums = sub(sg, a * h, a * h + h), []
-                for c0, c1, bias in ((0, 16 * m, col(14)), (16 * m + 16, h, col(15))):
-                    if c1 > c0:
-                        sums.append(sub(acc, 16 * len(sums) + a, 16 * len(sums) + a + 1))
-                        act(sub(junk, a * h + c0, a * h + c1), sub(y, c0, c1), Fn.Sign, bias=bias, acc=sums[-1])
-                if len(sums) == 2:
-                    ts(sub(out, m, m + 1), sub(t1, a, a + 1), sums[0], Op.add, sums[1], Op.add)
-                else:
-                    ts(sub(out, m, m + 1), sub(t1, a, a + 1), sums[0], Op.add)
+            ts(sub(f, 0, 16 * m + 16), sub(row, 0, 16 * m + 16), at(m), Op.is_le)
+            ts(sub(f, 16 * m + 16, w), sub(row, 16 * m, h), at(m), Op.is_lt)
+            scan(sub(cnt, i * w, i * w + w), V("one", 528 - 16 * m, 528 - 16 * m + w), f, Op.mult, Op.add)
+        ts(sub(out, lo, lo + nv), sub(cnt, w - 1, nv * w, w), 0.25, Op.add)
+        sg, junk, acc = new("wb", na * h), new("wb", na * h), new("wf", 32)
+        ib, ibs = new("wb", 128), new("wb", 128)
+        ms = list(range(lo)) + list(range(k - hi, k))
+        for a, m in enumerate(ms):
+            act(sub(sg, a * h, a * h + h), row, Fn.Sign, bias=at(m), scale=-1.0)
+        tt(sub(ib, 0, 16 * na), (sg, diags[(h, share)][0]), sub(ws16, 0, 16 * na), Op.is_gt)
+        scan(sub(ibs, 0, 16 * na), diags[(h, share)][1], sub(ib, 0, 16 * na), Op.max, Op.add)
+        for a, m in enumerate(ms):
+            y, sums = sub(sg, a * h, a * h + h), []
+            for c0, c1, sign, op in ((16 * m + 16, h, 1.0, Op.add), (0, 16 * m, -1.0, Op.subtract)):
+                if c1 > c0:
+                    sums += [sub(acc, 8 * len(sums) + a, 8 * len(sums) + a + 1), op]
+                    act(sub(junk, a * h + c0, a * h + c1), sub(y, c0, c1), Fn.Relu, scale=sign, acc=sums[-2])
+            ts(sub(out, m, m + 1), sub(ibs, 16 * a + 15, 16 * a + 16), *((sums[0], sums[1]) + tuple(sums[2:])))
 
     def near(t):
         n = NS[t]
         nu = sub(nru, 16 * t, 16 * t + 16)
         pk, krow, klst, junk, acc = new("wf", 256), new("wf", 256), new("wf", 16), new("wb", 512), new("wf", 16)
-        act(krow, (sub(jf, 0, n), nu), Fn.Copy, scale=256.0)
-        less = new("wf", 256)
+        act(krow, (sub(jf, 0, n), nu), Fn.Copy, scale=512.0)
+        less, unit = new("wf", 256), 2.0 ** (-9 if SELECT[t] else -18)
         for i in range(4):
-            act(sub(pk, 3 - i, 256, 4), sub(krow, i, 256, 4), Fn.Copy, scale=2.0 ** -17)
+            act(sub(pk, 3 - i, 256, 4), sub(krow, i, 256, 4), Fn.Identity, bias=4096.0 if i and SELECT[t] else 0.0, scale=unit)
             if i < 3:
-                act(sub(less, 2 - i, 256, 4), sub(krow, i, 256, 4), Fn.Copy, scale=-2.0 ** -17)
-        act(sub(less, 3, 256, 4), sub(ones, 0, 64), Fn.Copy, scale=-0.5)
+                act(sub(less, 2 - i, 256, 4), sub(krow, i, 256, 4), Fn.Copy, scale=-unit)
+        if SELECT[t]:
+            act(sub(less, 3, 256, 4), sub(jf, 0, 256, 4), Fn.Identity, bias=4096.0 * n - BELOW, scale=4096.0)
+        else:
+            act(sub(less, 3, 256, 4), sub(ones, 0, 64), Fn.Copy, scale=-0.5)
         heap(pk, less, 3500)
         mark("p%d" % t)
         heap(krow, sub(jf, 0, 256), 3500)
         tt(klst, sub(nrf, 16 * t, 16 * t + 16), xf, Op.add)
-        for m in range(16):
+        nv = SORT[t]
+        fl, cnt = new("wb", 256 * nv), new("wb", 256 * nv)
+        for m in range(nv, 16):
             act(sub(junk, 256 * (m % 2), 256 * (m % 2) + 256), krow, Fn.Sign, bias=sub(klst, m, m + 1), scale=-1.0, acc=sub(acc, m, m + 1))
         ko, ks, kk, sh = new("wu", 16), new("wf", 272), new("wi", 48), new("wi", 48)
-        ts(ko, acc, 0.5, Op.mult, 127.75, Op.add)
+        for m in range(nv):
+            ts(sub(fl, 256 * m, 256 * m + 256), krow, sub(klst, m, m + 1), Op.is_lt)
+            scan(sub(cnt, 256 * m, 256 * m + 256), sub(ones, 0, 256), sub(fl, 256 * m, 256 * m + 256), Op.mult, Op.add)
+        if nv:
+            cp(sub(ko, 0, nv), sub(cnt, 255, 256 * nv, 256))
+        ts(sub(ko, nv, 16), sub(acc, nv, 16), 0.5, Op.mult, 127.75, Op.add)
         mark("k%d" % t)
-        fill(sub(ks, 0, 8), -256.0)
-        fill(sub(ks, 264, 272), 600.0 * 256)
+        const(sub(ks, 0, 8), -512.0)
+        const(sub(ks, 264, 272), 600.0 * 512)
         scatter(sub(ks, 8, 264), ko, krow)
-        for e, d in enumerate((0, -1, 1)):
+        for e, d in enumerate((-1, 0, 1)):
             hs = new("wf", 256)
             scan(hs, sub(m16, 0, 256), sub(ks, 8 + d, 264 + d), Op.mult, Op.add)
-            ts(sub(kk, 16 * e, 16 * e + 16), sub(hs, 15, 256, 16), s16, Op.mult)
-        ts(sh, kk, 8, Op.arith_shift_right)
-        plc, first, last, an = sub(sh, 0, 16), new("wi", 16), new("wi", 16), new("wi", 32)
-        tt(first, plc, sub(sh, 16, 32), Op.not_equal)
-        tt(last, plc, sub(sh, 32, 48), Op.not_equal)
-        sigu, firstu, d1u, endo, endu, s3u = new("wu", 16), new("wu", 16), new("wu", 16), new("wu", 16), new("wu", 32), new("wu", 16)
-        ts(sub(an, 0, 16), sub(kk, 0, 16), 255, Op.bitwise_and)
-        ts(sub(an, 16, 32), sub(kk, 0, 16), 252, Op.bitwise_and)
-        cp(sigu, sub(an, 0, 16))
-        ts(s3u, sub(an, 16, 32), 3.0, Op.add)
-        cp(firstu, first)
+            ts(sub(sh, 16 * e, 16 * e + 16), sub(hs, 15, 256, 16), s16h, Op.mult, 256.0002, Op.add)
+            if d == 0:
+                ts(sub(kk, 16, 32), sub(hs, 15, 256, 16), s16, Op.mult)
+        plc, ends, an, w = sub(sh, 16, 32), new("wi", 32), new("wi", 32), new("wi", 48)
+        tt(ends, sub(sh, 0, 32), sub(sh, 16, 48), Op.not_equal)
+        su, d1u, endo, endu = new("wu", 32), new("wu", 16), new("wu", 16), new("wu", 32)
+        sigu, s3u = sub(su, 0, 16), sub(su, 16, 32)
+        ts(sub(an, 0, 16), sub(kk, 16, 32), 255, Op.bitwise_and)
+        ts(sub(an, 16, 32), sub(kk, 16, 32), 252, Op.bitwise_and)
+        cp(su, an)
         mark("f%d" % t)
-        w = new("wi", 96)
-        ts(sub(w, 0, 16), plc, -n + 0.0, Op.add)
-        tt(sub(w, 16, 32), sub(w, 0, 16), first, Op.mult)
-        ts(d1u, sub(w, 16, 32), n + 0.0, Op.add)
+        tt(sub(w, 0, 16), plc, sub(ends, 0, 16), Op.mult)
+        ts(d1u, sub(w, 0, 16), -240.0, Op.add, 15.0, Op.max)
         mark("f%d" % t)
-        tt(sub(w, 32, 48), sub(w, 0, 16), xi, Op.subtract)
-        tt(sub(w, 48, 64), sub(w, 32, 48), last, Op.mult)
-        tt(sub(w, 64, 80), sub(w, 48, 64), xi, Op.add)
-        ts(endo, sub(w, 64, 80), n + 0.0, Op.add)
+        tt(sub(w, 16, 32), plc, sub(ends, 16, 32), Op.mult)
+        tt(sub(w, 32, 48), sub(w, 16, 32), xi, Op.max)
+        cp(endo, sub(w, 32, 48))
         mark("f%d" % t)
-        a0, b1, nk, ew, hs = new("wf", 512), new("wb", 512), new("wb", 256), new("wf", n + 256), new("wf", n)
-        act(sub(a0, 0, 512, 2), (lutb, firstu), Fn.Copy)
-        mark("f%d" % t)
-        b0 = new("wb", 512)
-        act(sub(b0, 0, 512, 2), sub(a0, 0, 512, 2), Fn.Identity, bias=sub(ones, 0, 1), scale=-1.0 / BIG)
-        iota(nk, [[1, 64], [0, 4]], n - 256)
-        act(sub(b1, 1, 512, 2), (nk, sigu), Fn.Copy, scale=1.0 / 512)
-        mark("f%d" % t)
-        iota(sub(ew, 0, n), [[1, n]], 512)
-        scatter(ew, endo, odds)
-        scan(hs, sub(m16, 0, n), sub(ew, 0, n), Op.mult, Op.add)
-        ts(sub(endu, 0, n // 16), sub(hs, 15, n, 16), s16, Op.mult, 0.25, Op.add)
+        a0, b0, b1, ew, hs = new("wf", 512), new("wb", 512), new("wb", 512), new("wf", n + 256), new("wf", n)
+        if not SELECT[t]:
+            act(sub(b1, 1, 512, 2), (jf, s3u), Fn.Identity, bias=(n - 256.0) / 512, scale=1.0 / 2048)
+            mark("f%d" % t)
+        twin(sub(ew, 256, 256 + n), sub(jf, 0, n), whole("vb"))
+        for a in (0, 8):
+            scatter(ew, sub(endo, a, a + 8), sub(odds, 16 * a, 16 * a + 128))
+        scan(hs, sub(m16, 0, n), sub(ew, 256, 256 + n), Op.mult, Op.add)
+        ts(sub(endu, 0, n // 16), sub(hs, 15, n, 16), s16, Op.mult, 528.25, Op.add)
         mark("e%d" % t)
-        return nu, pk, sigu, s3u, d1u, endu, a0, b0, b1
+        src = None
+        if SELECT[t]:
+            from1, froms, n4, step = new("wf", 512), new("wf", 528 + n), new("wu", 64), new("wf", 256)
+            const(sub(froms, 512, 528), 0.0)
+            iota(sub(froms, 528, 528 + n), [[4096, n]], -BELOW)
+            iota(step, [[16385, 64], [4096, 4]], 4097 * n - BELOW)
+            act(sub(from1, 1, 512, 2), (step, sigu), Fn.Copy)
+            for e in range(4):
+                ts(sub(n4, 16 * e, 16 * e + 16), V("nri", 16 * t, 16 * t + 16), 4.0, Op.mult, e + 0.25, Op.add)
+            src = (from1, froms, n4)
+        return nu, pk, sigu, s3u, d1u, endu, a0, b0, b1, src
 
     held = [new("wb", 528 + n) for n in NS[:2]]
-    pars = [sub(held[t], 512, 512 + NS[t]) for t in range(2)] + [new("wb", NS[2])]
+    pars = [sub(held[t], 528, 528 + NS[t]) for t in range(2)] + [new("wb", NS[2])]
     ups = [[new("wb", n), new("wb", n), new("wb", n), new("wb", n)] for n in NS[:2]]
     odds = new("wf", 256)
-    iota(odds, [[2, 256]], 1)
+    iota(odds, [[2, 256]], -527)
     nears = [near(t) for t in range(2)]
-    a1 = new("wf", 512)
+    a1, olds = new("wf", 512), [new("wu", n // 4) for n in NS[:2]]
     for t in range(2):
-        fill(sub(held[t], 512 + NS[t], 528 + NS[t]), 1.0)
+        const(sub(held[t], 512, 528), 1.0)
     act(sub(a1, 1, 512, 2), sub(ones, 0, 256), Fn.Copy, scale=0.0)
     base = dict(top)
     for t in range(2):
@@ -644,12 +795,12 @@ def plan(g, core, T, topo, rank, room):
         n, n2, ch, ch2 = NS[t], NS[t + 1], CHUNKS[t], CHUNKS[t + 1]
         X, XH, XN = "x%d" % t, "xh%d" % t, "x%d" % (t + 1)
         nm = lambda s, lo, hi, step=1, t=t: V("%s%d" % (s, t), lo, hi, step)
-        k = n // 16
+        k, full = n // 16, FULL[t]
         par, nxt = pars[t], pars[t + 1]
         halves = lambda lo: ((lo, (lo + n + 32) // 64 * 32), ((lo + n + 32) // 64 * 32, n))
         lists = [new("wu", 32) for i in range(9)]
         low = [0 if t or i < LOW else 2 ** i for i in range(9)]
-        cut = [halves(low[i])[0][1] if t == 0 or i == 8 else n // 2 for i in range(9)]
+        cut = [halves(low[i])[0][1] if t == 0 else n // 2 for i in range(9)]
         part = lambda i, lo=0: [(a, b) for a, b in ((lo, cut[i]), (max(lo, cut[i]), n)) if a < b]
 
         def listed(i, a, b):
@@ -666,47 +817,48 @@ def plan(g, core, T, topo, rank, room):
             cp(sub(lists[0], 0, k), whole("pai"))
             for a, b in part(0):
                 if a or PAR0 == "a":
-                    act(sub(par, a, b), (jc, listed(0, a, b)), Fn.Copy, scale=1.0 / 512)
+                    act(sub(par, a, b), (jf, listed(0, a, b)), Fn.Identity, bias=-0.5, scale=1.0 / 512)
                 else:
-                    ts(sub(par, a, b), (jc, listed(0, a, b)), 1.0 / 512, Op.mult)
+                    ts(sub(par, a, b), (jf, listed(0, a, b)), 1.0 / 512, Op.mult, -0.5, Op.add)
         else:
             for a, b in part(0):
                 scan(sub(up[3], a, b), sub(m16, a, b), sub(par, a, b), Op.mult, Op.add)
             to_list(0, up[3])
-        for i in range(min(8, FULL[t])):
+        for i in range(min(8, full)):
             lo2, hs, src, dst = low[i + 1], up[2 + i % 2], up[i % 2] if i else par, up[(i + 1) % 2]
             for a, b in part(i if t else i + 1, lo2):
                 move("a" if a > lo2 else JUMPS[t][i], sub(dst, a, b), (above(src, b), listed(i, a, b)))
                 scan(sub(hs, a, b), sub(m16, a, b), sub(dst, a, b), Op.mult, Op.add)
-            if lo2 and i < min(8, FULL[t]) - 1:
+            if lo2 and i < min(8, full) - 1:
                 act(sub(dst, 0, lo2), sub(ones, 0, lo2), Fn.Copy, scale=-0.5)
             to_list(i + 1, hs)
+        far, fa, fb, fc = new("wu", 32), new("wf", 32), new("wf", 32), new("wf", 32)
+        if full < 9:
+            a, c0 = 2 ** full, 2 ** full // 16
+            ts(sub(fa, c0, k), sub(up[2 + full % 2], a + 15, n, 16), s16y, Op.mult, 272.25 - 262144.0, Op.add)
+            ts(sub(fb, c0, k), sub(fa, c0, k), s16r, Op.mult)
+            tt(sub(fc, c0, k), sub(up[2 + (full + 1) % 2], a + 15, n, 16), sub(fb, c0, k), Op.add)
+            ts(sub(far, c0, k), sub(fc, c0, k), s16k, Op.mult)
         s, s2 = new("wf", n), new("wf", n)
         for at, c in enumerate(READY[t]):
             a, b = ch[c], ch[c + 1]
             quant(nm("qx", a, b), nm("sx", a, b), V(X, 4 * a, 4 * b))
             mark("x%d%d" % (t, c))
             p = mm(4 + at % 2, qr, sr, nm("qx", a, b), nm("sx", a, b))
-            p2 = mm(6 + at % 2, qr, sr, nm("qx", a, b), nm("sx", a, b)) if SCORES[t] == "v" else p
-            move(SCORES[t], sub(s, a, b), p)
+            p2 = mm(6 + at % 2, qr, sr, nm("qx", a, b), nm("sx", a, b)) if SCORES[t][c] == "v" else p
+            move(SCORES[t][c], sub(s, a, b), p)
             act(sub(s2, a, b), p2, Fn.Copy)
-        sends = []
-        for c in range(2):
-            a, b = RUNS[t][c], RUNS[t][c + 1]
-            sends.append(hand(c, nm("rq", 0, b - a), nm("qx", a, b), "rc%d" % t, True))
-            sends.append(hand(c, nm("rs", 0, b - a), nm("sx", a, b), "rp%d" % t))
+        sends = [both(nm("rq", 0, n // 2), nm("qx", 0, n), "rc%d" % t, u8), both(nm("rs", 0, n // 2), nm("sx", 0, n), "rp%d" % t, ap)]
         arrival(sends, [nm("lq", 0, n), nm("ls", 0, n)], "aq%d" % t, 4 * ne, LAT[0])
-        for j in range(4):
-            if HALVE[t][j] == "v":
-                ts(V(XH, j * n, j * n + n), V(X, j * n, j * n + n), 0.5, Op.mult)
-            else:
-                act(V(XH, j * n, j * n + n), V(X, j * n, j * n + n), Fn.Copy, scale=0.5)
+        for j in range(0 if SELECT[t] else 4):
+            ts(V(XH, j * n, j * n + n), V(X, j * n, j * n + n), 0.5, Op.mult)
             mark("h%d" % t)
-        pc, other, dif = new("wf", n + 16), new("wf", n), new("wf", n)
-        cc, full = sub(pc, 0, n), FULL[t]
+        behind, other, dif, shallow, capped = new("wf", n + 16), new("wf", n), new("wf", n), new("wf", C), new("wf", C)
+        cc = sub(behind, 16, n + 16)
         cb = [cc, other] if full % 2 and full < 9 else [other, cc]
         tw = [new("wf", n), new("wf", n)]
-        fill(sub(pc, n, n + 16), 0.0)
+        if t == 0:
+            const(sub(behind, 8, 16), 0.0)
         for a, b in part(0):
             tt(sub(dif, a, b), (above(s, b), listed(0, a, b)), sub(s2, a, b), Op.subtract)
             act(sub(cb[0], a, b), sub(dif, a, b), Fn.Abs)
@@ -726,57 +878,89 @@ def plan(g, core, T, topo, rank, room):
                         mark("t%d" % t)
         if full < 9:
             w = 2 ** full
+            const(sub(behind, 0, 8), BIG)
+            for a, b in part(full, w):
+                tt(sub(capped, a, b), (sub(behind, 0, b + 16), sub(far, a // 16, b // 16)), sub(tw[(full - 1) % 2], a, b), Op.max)
+            act(sub(capped, 0, w), sub(other, 0, w), Fn.Copy)
+            act(sub(shallow, 0, w), sub(other, 0, w), Fn.Copy)
+            for a, b in part(full, w):
+                tt(sub(shallow, a, b), (sub(capped, 0, b), listed(full, a, b)), sub(other, a, b), Op.max)
             act(sub(cc, 0, w), sub(other, 0, w), Fn.Copy)
             for a in range(w, n, w):
                 b = min(a + w, n)
                 tt(sub(cc, a, b), (sub(cc if a > w else other, 0, a), listed(full, a, b)), sub(other, a, b), Op.max)
                 mark("c%d%d" % (t, full))
-        h = n // 2
+        h, cs = n // 2, shallow if full < 9 else cc
         win, msk, lst, rk = new("wf", h), new("wf", h), new("wf", h), new("wu", 16)
-        for a, b in halves(0) if WINS[t] == 2 else ((0, 128), (128, 256), (256, n)):
-            tt(sub(win, a // 2, b // 2), sub(cc, a, b, 2), sub(cc, a + 1, b, 2), Op.min)
+        for a, b in halves(0):
+            tt(sub(win, a // 2, b // 2), sub(cs, a, b, 2), sub(cs, a + 1, b, 2), Op.min)
             tt(sub(msk, a // 2, b // 2), sub(win, a // 2, b // 2), sub(diag, a // 2, b // 2), Op.mult)
-            scan(sub(lst, a // 2, b // 2), sub(off16, a // 2, b // 2), sub(msk, a // 2, b // 2), Op.mult, Op.add)
+            scan(sub(lst, a // 2, b // 2), sub(ns16, a // 2, b // 2), sub(msk, a // 2, b // 2), Op.mult, Op.add)
         ranks(win, lst, h, SCALAR[t][0], rk)
         flag, pre, fl, cnt, acc, ou = new("wb", h), new("wb", h), new("wb", 4 * h), new("wb", 2 * h), new("wf", 2), new("wu", 8)
         cp(sub(flag, 0, 96), (lut64, sub(rk, 0, 6)))
         act(sub(flag, 96, h), (lut64, sub(rk, 6, h // 16)), Fn.Copy)
         scan(pre, sub(ones, 0, h), flag, Op.mult, Op.add)
+        w = h - 48
         for u in range(2):
-            ts(sub(fl, u * h, u * h + h), pre, sub(kh, u, u + 1), Op.is_lt)
-            scan(sub(cnt, u * h, u * h + h), sub(ones, 0, h), sub(fl, u * h, u * h + h), Op.mult, Op.add)
-            act(sub(fl, (2 + u) * h, (3 + u) * h), pre, Fn.Sign, bias=sub(kh, 2 + u, 3 + u), scale=-1.0, acc=sub(acc, u, u + 1))
-        ts(sub(ou, 0, 2), sub(cnt, h - 1, 2 * h, h), 2.0, Op.mult, 0.25, Op.add)
-        ts(sub(ou, 2, 4), acc, h + 0.25, Op.add)
-        c2, j2, rk2, srt, hs = new("wf", 128), new("wf", 128), new("wu", 8), new("wf", 256), new("wf", 64)
+            ts(sub(fl, u * w, u * w + w), sub(pre, 16 * u, 16 * u + w), sub(kh, u, u + 1), Op.is_lt)
+            scan(sub(cnt, u * w, u * w + w), sub(ones, 0, w), sub(fl, u * w, u * w + w), Op.mult, Op.add, 16.0 * u)
+            act(sub(fl, (2 + u) * w, (3 + u) * w), sub(pre, 32 + 16 * u, 32 + 16 * u + w), Fn.Sign, bias=sub(kh, 2 + u, 3 + u), scale=-1.0, acc=sub(acc, u, u + 1))
+        ts(sub(ou, 0, 2), sub(cnt, w - 1, 2 * w, w), 2.0, Op.mult, 0.25, Op.add)
+        for u in range(2):
+            ts(sub(ou, 2 + u, 3 + u), sub(acc, u, u + 1), w + 64.25 + 32 * u, Op.add)
+        c2, j2, rk2, srt, hs = new("wf", 128), new("wf", 128), new("wu", 8), new("wf", 128), new("wf", 64)
         msk, lst, odd = new("wf", 128), new("wf", 128), new("wf", n - 1)
-        act(odd, sub(cc, 1, n), Fn.Copy)
+        if t:
+            keep(odd, sub(cs, 1, n), [[1, n - 1]], 0.0, 1)
+        else:
+            act(odd, sub(cs, 1, n), Fn.Copy)
         mark("o%d" % t)
-        for e, row in enumerate((cc, odd)):
+        for e, row in enumerate((cs, odd)):
             tt(sub(msk, e, 128, 2), (row, sub(ou, 0, 4)), sub(diag, e, 128, 2), Op.mult)
             act(sub(c2, e, 128, 2), (row, sub(ou, 0, 4)), Fn.Copy)
         act(sub(j2, 0, 128, 2), (sub(jf, 0, n), sub(ou, 0, 4)), Fn.Copy)
         act(sub(j2, 1, 128, 2), sub(j2, 0, 128, 2), Fn.Identity, bias=sub(ones, 0, 1))
-        scan(lst, sub(off16, 0, 128), msk, Op.mult, Op.add)
+        scan(lst, sub(ns16, 0, 128), msk, Op.mult, Op.add)
         ranks(c2, lst, 128, SCALAR[t][1], rk2)
         scatter(srt, rk2, j2)
-        scan(hs, sub(m4, 0, 64), sub(srt, 0, 128, 2), Op.mult, Op.add)
+        scan(hs, sub(m4, 0, 64), sub(srt, 0, 64), Op.mult, Op.add)
         ts(nm("el", 0, 16), sub(hs, 3, 64, 4), s4p, Op.mult, qto, Op.add)
-        sl = hand(0, nm("rl", 0, 16), nm("el", 0, 16), "rn%d" % t)
+        sl = hand(nm("rl", 0, 16), nm("el", 0, 16), "rn%d" % t)
         arrival([sl], [nm("ll", 0, 16)], "an%d" % t, ne, LAT[1])
-        twin(nm("xo", 0, 4 * n), V(XH, 0, 4 * n), nm("ll", 0, 16))
+        if not SELECT[t]:
+            twin(nm("xo", 0, 4 * n), V(XH, 0, 4 * n), nm("ll", 0, 16))
         for c in BY_DMA[t]:
             twin(V(XN, 4 * ch2[c], 4 * ch2[c + 1]), V(X, 4 * ch2[c], 4 * ch2[c + 1]), nm("ll", 0, 16))
         for b in range(4):
             p = mm(4 + b, V("qe", 128 * b, 128 * b + 128), V("se", 128 * b, 128 * b + 128), nm("lq", 0, n), nm("ls", 0, n))
             act(nm("dd", b, 4 * n, 4), p, Fn.Copy)
             mark("d%d" % t)
-        nu, pk, sigu, s3u, d1u, endu, a0, b0, b1 = nears[t]
-        act(sub(a1, 0, 512, 2), (pc, d1u), Fn.Copy)
+        nu, pk, sigu, s3u, d1u, endu, a0, b0, b1, src = nears[t]
+        oh = new("wf", n)
+        if SELECT[t]:
+            from1, froms, n4 = src
+            act(oh, par, Fn.Identity, bias=256.0, scale=512.0)
+            heap(sub(froms, 528, 528 + n), oh, 2500)
+            for j in range(4):
+                act(nm("sm", j * n, j * n + n), (V(X, 0, 4 * n), sub(olds[t], j * n // 16, (j + 1) * n // 16)), Fn.Copy)
+                mark("S%d" % t)
+            heap(nm("sm", 0, 4 * n), V(X, 0, 4 * n), 2500, [sl])
+            for e in range(4):
+                act(nm("sm", 4 * n + e, 4 * n + 1024, 4), (V(X, 0, 4 * n), sub(n4, 16 * e, 16 * e + 16)), Fn.Copy)
+                mark("N%d" % t)
+        act(sub(a1, 0, 512, 2), (behind, d1u), Fn.Copy)
         mark("s%d" % t)
         vs = sub(held[t], 0, 512)
-        act(sub(b1, 0, 512, 2), (sub(held[t], 512, 528 + n), d1u), Fn.Copy)
-        mark("s%d" % t)
+        if SELECT[t]:
+            act(sub(from1, 0, 512, 2), (sub(froms, 512, 528 + n), d1u), Fn.Copy)
+            act(sub(a0, 0, 512, 2), sub(from1, 0, 512, 2), Fn.Relu, bias=BIG, scale=BIG / 2 ** 20)
+            act(sub(b0, 0, 512, 2), sub(from1, 0, 512, 2), Fn.Relu, bias=1.0, scale=2.0 ** -20)
+        else:
+            act(sub(b1, 0, 512, 2), (sub(held[t], 512, 528 + n), d1u), Fn.Copy)
+            mark("s%d" % t)
+            act(sub(a0, 0, 512, 2), sub(b1, 0, 512, 2), Fn.Relu, bias=-3 * BIG, scale=4 * BIG)
+            ts(sub(b0, 0, 512, 2), sub(b1, 0, 512, 2), 0.75, Op.is_lt)
         sn = new("wf", 256)
         act(sn, (s, nu), Fn.Copy)
         mark("s%d" % t)
@@ -784,11 +968,15 @@ def plan(g, core, T, topo, rank, room):
         act(V(X, 4 * n + 128, 4 * n + 256), (nm("dd", 0, 4 * n), nm("ll", 8, 16)), Fn.Copy)
         quant(nm("qh", 0, 128), nm("sh", 0, 128), V(X, 4 * n - 256, 4 * n + 256))
         z = sub(mm(2, qr, sr, nm("qh", 0, 128), nm("sh", 0, 128)), 64, 128)
-        act(V(XH, 4 * n, 4 * n2), V(X, 4 * n, 4 * n2), Fn.Copy, scale=0.5)
-        if BLEND[t][2] == "v":
+        if SELECT[t]:
+            for j in range(16):
+                move(FOUR[j], nm("hh", j, 1024, 16), V(X, 4 * n + j % 4, 4 * n2, 4))
+            heap(nm("sm", 4 * n, 4 * n + 1024), nm("hh", 0, 1024), LAT[2] + 300)
+        else:
+            act(V(XH, 4 * n, 4 * n2), V(X, 4 * n, 4 * n2), Fn.Copy, scale=0.5)
             act(nm("xo", 4 * n, 4 * n2), V(X, 4 * n, 4 * n2), Fn.Copy, scale=0.5)
-        d, gap, cost, mn, gs, ga = [new("wf", 256) for i in range(6)]
-        best = new("wf", 512)
+        d, gap, cost, gs, ga, mn = [new("wf", 256) for i in range(5)] + [sub(new("wf", 264), 5, 261)]
+        best, pick = new("wf", 512), new("wf", n2)
         for i in range(4):
             tt(sub(d, i, 256, 4), sub(sn, i, 256, 4), z, Op.subtract)
             act(sub(gap, i, 256, 4), sub(d, i, 256, 4), Fn.Abs)
@@ -798,43 +986,52 @@ def plan(g, core, T, topo, rank, room):
         act(ga, (gap, sigu), Fn.Copy)
         runs = [(256 * j // SPLIT, 256 * (j + 1) // SPLIT) for j in range(SPLIT)]
         for a, b in runs:
-            tt(sub(a0, 2 * a + 1, 2 * b, 2), (mn, sub(s3u, a // 16, b // 16)), sub(ga, a, b), Op.max)
+            tt(sub(a0, 2 * a + 1, 2 * b, 2), (sub(mn, 3, 256), sub(s3u, a // 16, b // 16)), sub(ga, a, b), Op.max)
         for i in range(3):
             tt(sub(gt, 3 - i, 256, 4), sub(mn, i, 256, 4), sub(mn, 3, 256, 4), Op.is_gt)
         for a in (0, 128):
             scan(sub(gs, a, a + 128), sub(gt, a, a + 128), sub(pk, a, a + 128), Op.mult, Op.add)
-        act(sub(nxt, n, n2), sub(gs, 3, 256, 4), Fn.Copy)
+        act(sub(pick if SELECT[t] else nxt, n, n2), sub(gs, 3, 256, 4), Fn.Copy)
         mark("n%d" % t)
         for a, b in runs:
             a, b = 2 * a, 2 * b
             scan(sub(best, a, b), sub(a0, a, b), sub(a1, a, b), Op.min, Op.max, sub(best, a - 1, a) if a else 0.0)
-            tt(sub(b0, a + 1, b, 2), sub(best, a + 1, b, 2), sub(best, a, b, 2), Op.is_lt)
-            scan(sub(vs, a, b), sub(b0, a, b), sub(b1, a, b), Op.add, Op.min, sub(vs, a - 1, a) if a else 0.0)
-        yo, hs = new("wu", n2 // 4), new("wb", n2)
-        for at, c in enumerate(ORDER[t + 1]):
-            a, b = ch2[c], ch2[c + 1]
-            if a < n:
-                move(PARENTS[t][c], sub(nxt, a, min(b, n)), (sub(held[t], 0, 512 + n), sub(endu, a // 16, min(b, n) // 16)))
+            tt(sub(b0, a + 1, b, 2), sub(best, a + 1, b, 2), sub(best, a, b, 2), Op.is_ge if SELECT[t] else Op.is_lt)
+            if SELECT[t]:
+                scan(sub(froms, a, b), sub(b0, a, b), sub(from1, a, b), Op.mult, Op.min, sub(froms, a - 1, a) if a else 0.0)
+            else:
+                scan(sub(vs, a, b), sub(b0, a, b), sub(b1, a, b), Op.add, Op.min, sub(vs, a - 1, a) if a else 0.0)
+        yo, hs, hf = new("wu", n2 // 4), new("wb", n2), new("wf", n2)
+        if t == 0 and SELECT[1] and not SELECT[0]:
+            yo = olds[1]
+        for c in range(3):
+            a, b = ch2[c], min(ch2[c + 1], n)
+            if SELECT[t]:
+                move(PICKS[t][c], sub(pick, a, b), (sub(froms, 0, 528 + n), sub(endu, a // 16, b // 16)))
+                scan(sub(hf, a, b), sub(m4, a, b), sub(pick, a, b), Op.mult, Op.add)
+                if b == n:
+                    scan(sub(hf, n, n2), sub(m4, n, n2), sub(gs, 3, 256, 4), Op.mult, Op.add)
+                ts(sub(yo, a // 4, ch2[c + 1] // 4), sub(hf, a + 3, ch2[c + 1], 4), s4z, Op.mult, qtz, Op.add)
+            else:
+                move(PARENTS[t][c], sub(nxt, a, b), (sub(held[t], 0, 528 + n), sub(endu, a // 16, b // 16)))
                 mark("m%d%d" % (t, c))
-        for c, (a, b) in enumerate(((0, ch2[1]), (ch2[1], n2)) if JOIN[t] else zip(ch2, ch2[1:])):
+        for c, (a, b) in enumerate(() if SELECT[t] else ((0, ch2[1]), (ch2[1], n2))):
             scan(sub(hs, a, b), sub(m4, a, b), sub(nxt, a, b), Op.mult, Op.add)
             ts(sub(yo, a // 4, b // 4), sub(hs, a + 3, b, 4), s4y, Op.mult, qty, Op.add)
             mark("y%d%d" % (t, c))
-        for at, c in enumerate(ORDER[t + 1]):
+        for c in range(3):
             a, b = ch2[c], ch2[c + 1]
-            cuts = [a + (b - a) * j // PIECES[t] // 8 * 8 for j in range(PIECES[t])] + [b]
-            for lo, hi in zip(cuts, cuts[1:]):
-                if BLEND[t][c] == "a":
-                    act(nm("xo", 4 * lo, 4 * hi), (V(XH, 0, 4 * n2), sub(yo, lo // 4, hi // 4)), Fn.Copy)
-                    mark("g%d%d" % (t, c))
-                    tt(nm("yt", 4 * lo, 4 * hi), nm("xo", 4 * lo, 4 * hi), V(XH, 4 * lo, 4 * hi), Op.add)
-                else:
-                    tt(nm("yt", 4 * lo, 4 * hi), (V(XH, 0, 4 * n2), sub(yo, lo // 4, hi // 4)), nm("xo", 4 * lo, 4 * hi), Op.add)
+            if SELECT[t]:
+                mid = a + int((b - a) * SHARE[t][c]) // 8 * 8
+                ts(nm("yt", 4 * a, 4 * mid), (nm("sm", 0, 4 * n + 1024), sub(yo, a // 4, mid // 4)), 0.5, Op.mult)
+                act(nm("yt", 4 * mid, 4 * b), (nm("sm", 0, 4 * n + 1024), sub(yo, mid // 4, b // 4)), Fn.Copy, scale=0.5)
+            else:
+                tt(nm("yt", 4 * a, 4 * b), (V(XH, 0, 4 * n2), sub(yo, a // 4, b // 4)), nm("xo", 4 * a, 4 * b), Op.add)
                 mark("b%d%d" % (t, c))
             quant(nm("qy", a, b), nm("sy", a, b), nm("yt", 4 * a, 4 * b))
             mark("q%d%d" % (t, c))
             for e in range(4):
-                p = mm(4 * (at % 2) + e, V("wq", 128 * e, 128 * e + 128), V("wsc", 128 * e, 128 * e + 128), nm("qy", a, b), nm("sy", a, b))
+                p = mm(4 * (c % 2) + e, V("wq", 128 * e, 128 * e + 128), V("wsc", 128 * e, 128 * e + 128), nm("qy", a, b), nm("sy", a, b))
                 r = nm("ru", 4 * a + e, 4 * b, 4)
                 act(r, p, Fn.Relu, scale=0.03125)
                 mark("r%d%d" % (t, c))
@@ -843,8 +1040,11 @@ def plan(g, core, T, topo, rank, room):
             if c in BY_DMA[t]:
                 heap(V(XN, 4 * a, 4 * b), nm("ru", 4 * a, 4 * b), LAT[2])
 
-    act(whole("osb"), pars[2], Fn.Identity, bias=col(12), scale=512.0)
-    dma("s", lambda: g.sync.dma_start(T.op[:], T.osb[0:128:16, :]), [whole("osb")], [], 2000)
+    col = new("wf", NS[2])
+    act(col, pick, Fn.Identity, bias=WHOLE + BELOW / 4096, scale=1.0 / 4096)
+    act(whole("osb"), col, Fn.Identity, bias=4096 * WHOLE + BELOW, scale=-4096.0)
+    dma("s", lambda: g.sync.dma_start(T.op[:], T.wf[0:128:16, pick[1]:pick[2]]), [pick], [V("op", 0, 1)], 2000)
+    add("g", "d", lambda: g.dma_start(T.op[:], T.osb[0:128:16, :], accum_op=Op.add), [whole("osb")], [V("op", 0, 1)], HOLDS[1], LAT[2] + 800)
     for c in range(len(CHUNKS[2]) - 1):
         a, b = CHUNKS[2][c], CHUNKS[2][c + 1]
         quant(V("qx2", a, b), V("sx2", a, b), V("x2", 4 * a, 4 * b))

import math
import numpy as np
from concourse.bass import DstId, RemoteDMATransfer
from concourse.mybir import dt, AluOpType as Op, ActivationFunctionType as Fn

C, A = 352, 64
NS = (C, C + A, C + 2 * A)
CHUNKS = ((0, 192, 352), (0, 160, 288, 416), (0, 160, 320, 480))
BY_DMA = ((0,), (0,))
TT2 = 2.0
PICKS = ("aaa", "vaa")
PARENTS = ("aaa", "aaa")
LAST = "vaa"
READY = ((0, 1), (1, 0, 2))
SELECT = (0, 1)
SHARE = ((0.5, 0.75, 0.5), (0.5, 0.5, 0.5))
FOUR = "a" * 16
BIG = 2.0 ** 90
HOLD = 2.0 ** 24
KEEP = 4096.0
BELOW, WHOLE = 4096 * 768, 1.5 * 2 ** 23
X4 = "float8_e4m3fn_x4"
DMAS = 48

SCRATCH = {
    "wf": ("sbuf", [128, 21504], "float32"), "wb": ("sbuf", [128, 27648], "bfloat16"),
    "wi": ("sbuf", [128, 1024], "int32"), "wu": ("sbuf", [128, 1536], "uint16"),
    "ps": ("psum", [128, 4096], "float32"),
    "pai": ("sbuf", [128, 22], "int32"), "nri": ("sbuf", [128, 32], "int32"),
    "ub": ("sbuf", [128, 512], "bfloat16"), "vb": ("sbuf", [128, 512], "bfloat16"),
    "qu": ("sbuf", [128, 128], X4), "su": ("sbuf", [128, 128], "uint8"),
    "qr": ("sbuf", [128, 128], X4), "sr": ("sbuf", [128, 128], "uint8"),
    "qv": ("sbuf", [128, 128], X4), "sv": ("sbuf", [128, 128], "uint8"),
    "wq": ("sbuf", [128, 512], X4), "wsc": ("sbuf", [128, 512], "uint8"),
    "repi": ("sbuf", [128, 8], "int32"), "repu": ("sbuf", [128, 8], "uint16"),
    "one": ("sbuf", [128, 912], "bfloat16"), "eye": ("sbuf", [128, 528], "bfloat16"),
    "qe": ("sbuf", [128, 512], X4), "se": ("sbuf", [128, 512], "uint8"),
    "x2": ("sbuf", [128, 4 * NS[2]], "bfloat16"),
    "qx2": ("sbuf", [128, NS[2]], X4), "sx2": ("sbuf", [128, NS[2]], "uint8"),
    "ysb": ("sbuf", [128, NS[2]], "float32"), "osb": ("sbuf", [128, NS[2]], "float32"),
}
for _t in range(2):
    _n, _m = NS[_t], NS[_t + 1]
    SCRATCH.update({
        "x%d" % _t: ("sbuf", [128, 4 * _m], "bfloat16"),
        "yt%d" % _t: ("sbuf", [128, 4 * _m], "bfloat16"), "ru%d" % _t: ("sbuf", [128, 4 * _m], "float32"),
        "dd%d" % _t: ("sbuf", [128, 4 * _n], "bfloat16"),
        "qx%d" % _t: ("sbuf", [128, _n], X4), "sx%d" % _t: ("sbuf", [128, _n], "uint8"),
        "qh%d" % _t: ("sbuf", [128, 128], X4), "sh%d" % _t: ("sbuf", [128, 128], "uint8"),
        "qy%d" % _t: ("sbuf", [128, _m], X4), "sy%d" % _t: ("sbuf", [128, _m], "uint8"),
        "rq%d" % _t: ("sbuf", [128, _n // 2], X4), "rs%d" % _t: ("sbuf", [128, _n // 2], "uint8"),
        "lq%d" % _t: ("sbuf", [128, _n], X4), "ls%d" % _t: ("sbuf", [128, _n], "uint8"),
        "el%d" % _t: ("sbuf", [128, 16], "uint16"), "rl%d" % _t: ("sbuf", [128, 16], "uint16"),
        "ll%d" % _t: ("sbuf", [128, 16], "uint16"),
    })
    if SELECT[_t]:
        SCRATCH.update({"sm%d" % _t: ("sbuf", [128, 4 * _n + 1024], "bfloat16"), "hh%d" % _t: ("sbuf", [128, 1024], "bfloat16")})
    else:
        SCRATCH.update({"xh%d" % _t: ("sbuf", [128, 4 * _m], "bfloat16"), "xo%d" % _t: ("sbuf", [128, 4 * _m], "bfloat16")})
SEMAPHORES = (["ev", "ea", "ep", "eg", "sent"] + ["dm%d" % _i for _i in range(DMAS)]
              + ["%s%d" % (_s, _t) for _s in ("rc", "rp", "rn", "aq", "an") for _t in range(2)])

CY, WAKE = 0.92, 170.0
LAT = (12000.0, 4300.0, 1900.0)
HOLDS = (1100.0, 1300.0, 1.25)
SCALAR = (((3, 2), (1, 2)), ((3, 3), (1, 2)))
SORT = (2, 2)
JUMPS = ("aaaaaaaa", "aaaaaaaa")
LOW = 5
PAR0 = "v"
FULL = (5, 9)
SPLIT = 2
SPREAD = ("cas", "4sss", "4ss", "6")
SCORES = ("vv", "vaa")
SPEEDS = ((1, 1, 1), (1.3, 1.48, 1.7), (0.93, 0.78, 0.62))
WEIGH = (0.35, 0.27, 0.33)
TRIES, SLACK, SEED, ORDERED = (2500, 90000), (15.0, 30.0), 2, []
EARLY = {"r11": 3000, "c04": 1000, "u15": 1000, "q02": 1000, "x11": 1500, "u14": 1500, "u16": 1000, "u17": 1500, "u02": 8000, "c03": 1500,
         "c15": 600, "u03": 1000, "c00": 8000, "r00": 1000, "y01": 2000, "c11": 600, "c14": 1000, "c12": 300, "b01": 2000, "u12": 2000,
         "q00": 1500, "r01": 600, "b10": 8000, "k0": 2000, "y11": 2000, "e0": 2000, "m01": 8000, "q10": 2000, "o0": 5000, "u05": 1000,
         "q01": 3000, "y00": 8000, "u01": 150, "x10": 5000, "x12": 1500}


def relays_of(T, topo, r):
    me, nxt = T.cores[r], T.cores[(r + 1) % len(T.cores)]
    return [c for c in topo.cores_of(me) if T.rank_of(c) is None and topo.die(c) == topo.die(me) and topo.may_write(c, nxt)][:2]


def relay_program(g, core, T, topo, r, k):
    nxt = T.cores[(r + 1) % len(T.cores)]
    rid, pid = topo.addr(nxt, core)
    m, ne = topo.mask(core, nxt), len(topo.engines(core, nxt))
    nin = len(topo.engines(T.cores[r], core))
    calls = 0
    for t in range(2):
        a, b = k * NS[t] // 2, (k + 1) * NS[t] // 2
        g.wait_ge(T.sem["rc%d" % t], nin // 2)
        g.remote_dma(T["lq%d" % t][:, a:b].bitcast(dt.uint8), T["rq%d" % t][:, 0:b - a].bitcast(dt.uint8), T.sem["aq%d" % t], T.sem.sent, pid, rid, m)
        g.wait_ge(T.sem["rp%d" % t], nin // 2)
        g.remote_dma(T["ls%d" % t][:, a:b], T["rs%d" % t][:, 0:b - a], T.sem["aq%d" % t], T.sem.sent, pid, rid, m)
        calls += 2
        if k == 0:
            g.wait_ge(T.sem["rn%d" % t], nin)
            g.remote_dma(T["ll%d" % t][:], T["rl%d" % t][:], T.sem["an%d" % t], T.sem.sent, pid, rid, m)
            calls += 1
    g.wait_ge(T.sem.sent, calls * ne)


def rank_program(g, core, T, topo):
    rank = T.rank_of(core)
    if rank is None:
        for r in range(len(T.cores)):
            rl = relays_of(T, topo, r)
            if core in rl:
                relay_program(g, core, T, topo, r, rl.index(core))
        return
    room = {}
    plan(g, core, T, topo, rank, room)
    emit(g, T, plan(g, core, T, topo, rank, room))


def V(name, lo, hi, step=1):
    return (name, lo, hi, step)


def sub(v, lo, hi, step=1):
    return (v[0], v[1] + lo, v[1] + hi, step)


def size(v):
    return (v[2] - v[1] + v[3] - 1) // v[3]


def clash(a, b):
    if a[0] != b[0]:
        return False
    if a[0] == "ps":
        return a[1] // 512 == b[1] // 512
    if a[2] <= b[1] or b[2] <= a[1]:
        return False
    if a[3] > 1 and a[3] == b[3] and (a[1] - b[1]) % a[3]:
        return False
    return True


def link(ops):
    for i, o in enumerate(ops):
        d = set(o["after"])
        for j in range(i):
            p = ops[j]
            hit = any(clash(a, b) for a in p["w"] for b in o["r"] + o["w"]) or any(clash(a, b) for a in p["r"] for b in o["w"])
            if not hit and p["q"] != o["q"]:
                hit = any(a[0] == "ps" and clash(a, b) for a in p["r"] for b in o["r"])
            if hit:
                d.add(j)
        o["deps"] = sorted(d)


def thin(ops):
    above = []
    for o in ops:
        seen, kept = 0, []
        for j in sorted(o["deps"], reverse=True):
            if not seen >> j & 1:
                kept.append(j)
            seen |= above[j] | 1 << j
        above.append(0 if o["kind"] in "xr" else seen)
        o["deps"] = kept


def blocked(done, why):
    i, pairs = done.index(max(done)), []
    while i >= 0:
        w = why[i]
        if w <= -2:
            pairs.append((-2 - w, i))
        i = -2 - w if w <= -2 else w
    return pairs


def favour(ops, tries):
    n = len(ops)
    q, cost, deps = ["xvapgs".index(o["q"]) for o in ops], [o["cost"] for o in ops], [o["deps"] for o in ops]
    own = [o["cost"] + o["lat"] + WAKE for o in ops]

    def build(more):
        level = [0.0] * n
        for i in range(n - 1, -1, -1):
            x = level[i] = level[i] + own[i] + more[i]
            for j in deps[i]:
                if level[j] < x:
                    level[j] = x
        lines = [([], [], []) for k in range(6)]
        start, done, why = [0.0] * n, [0.0] * n, [-1] * n
        for i in sorted(range(n), key=lambda i: -level[i]):
            t, w = 0.0, -1
            for j in deps[i]:
                if done[j] > t:
                    t, w = done[j], j
            if q[i]:
                c, (s, e, who) = cost[i], lines[q[i]]
                p, m = 0, len(s)
                hi = m
                while p < hi:
                    mid = (p + hi) // 2
                    if e[mid] > t:
                        hi = mid
                    else:
                        p = mid + 1
                while p < m and t + c > s[p]:
                    t, w = e[p], -2 - who[p]
                    p += 1
                s.insert(p, t)
                e.insert(p, t + c)
                who.insert(p, i)
            start[i], done[i], why[i] = t, t + own[i], w
        return max(done), start, done, why
    draw = np.random.default_rng(SEED)
    more = [EARLY.get(o.get("mark"), 0.0) for o in ops]
    now = best = build(more)
    for it in range(tries):
        pairs = blocked(now[2], now[3])
        a, b, c, d = draw.random(4)
        u, v = pairs[int(a * len(pairs))]
        step = 60.0 * math.exp(4.5 * c)
        x = v if b < 0.55 or more[u] <= 1.0 - own[u] else u
        old = more[x]
        more[x] = old + step if x == v else max(old - step, 1.0 - own[x])
        new = build(more)
        if new[0] <= now[0] or d < math.exp((now[0] - new[0]) / (SLACK[0] * (1 - it / tries) + 1)):
            now = new
            if now[0] < best[0]:
                best = now
        else:
            more[x] = old
    return sorted(range(n), key=lambda i: (best[1][i], i)), best[0] - WAKE


def exchange(ops, order, tries):
    n = len(ops)
    q, deps, after = ["xvapgs".index(o["q"]) for o in ops], [o["deps"] for o in ops], [[] for o in ops]
    cases = [([o["costs"][c] for o in ops], [o["costs"][c] + o["lat"] + WAKE for o in ops]) for c in range(len(WEIGH))]
    for i in range(n):
        for j in deps[i]:
            after[j].append(i)

    def beside(seq, k, step):
        out, left = [-1] * 6, 5
        while 0 <= k < n and left:
            i = seq[k]
            if q[i] and out[q[i]] < 0:
                out[q[i]] = i
                left -= 1
            k += step
        return out

    def heads(part, last, case, start, done, why):
        cost, tail = case
        free, last = [start[i] + cost[i] if i >= 0 else 0.0 for i in last], last[:]
        for i in part:
            t, w, k = 0.0, -1, q[i]
            for j in deps[i]:
                if done[j] > t:
                    t, w = done[j], j
            if k:
                if free[k] > t:
                    t, w = free[k], -2 - last[k]
                free[k], last[k] = t + cost[i], i
            start[i], done[i], why[i] = t, t + tail[i], w

    def tails(part, nxt, case, rest):
        cost, tail = case
        ahead = [rest[i] if i >= 0 else 0.0 for i in nxt]
        for i in reversed(part):
            t, k = 0.0, q[i]
            for j in after[i]:
                if rest[j] > t:
                    t = rest[j]
            t += tail[i]
            if k:
                if ahead[k] + cost[i] > t:
                    t = ahead[k] + cost[i]
                ahead[k] = t
            rest[i] = t

    def onward(seq, k, last, reach, case, start, done, why, log):
        cost, tail = case
        free, last, moved = [start[i] + cost[i] if i >= 0 else 0.0 for i in last], last[:], [c > 0 and c in here for c in range(6)]
        while k < n and (k <= reach or True in moved):
            i = seq[k]
            t, w, c = 0.0, -1, q[i]
            for j in deps[i]:
                if done[j] > t:
                    t, w = done[j], j
            if c:
                if free[c] > t:
                    t, w = free[c], -2 - last[c]
                free[c], last[c], moved[c] = t + cost[i], i, t != start[i]
            if t != start[i] or w != why[i]:
                log.append((i, start[i], done[i], why[i]))
                if t != start[i]:
                    for j in after[i]:
                        if pos[j] > reach:
                            reach = pos[j]
                start[i], done[i], why[i] = t, t + tail[i], w
            k += 1

    def backward(seq, k, nxt, reach, case, rest):
        cost, tail = case
        ahead, moved = [rest[i] if i >= 0 else 0.0 for i in nxt], [c > 0 and c in here for c in range(6)]
        while k >= 0 and (k >= reach or True in moved):
            i = seq[k]
            t, c = 0.0, q[i]
            for j in after[i]:
                if rest[j] > t:
                    t = rest[j]
            t += tail[i]
            if c:
                if ahead[c] + cost[i] > t:
                    t = ahead[c] + cost[i]
                ahead[c], moved[c] = t, t != rest[i]
            if t != rest[i]:
                rest[i] = t
                for j in deps[i]:
                    if pos[j] < reach:
                        reach = pos[j]
            k -= 1
    draw = np.random.default_rng(SEED).random((tries, 5)).tolist()
    seq = list(order)
    res = [[[0.0] * n, [0.0] * n, [-1] * n, [0.0] * n] for c in cases]
    for c, r in zip(cases, res):
        heads(seq, [-1] * 6, c, r[0], r[1], r[2])
        tails(seq, [-1] * 6, c, r[3])
    now = sum(w * max(r[1]) for w, r in zip(WEIGH, res))
    best, taken = (now, list(seq)), 0
    pairs, pos = [blocked(r[1], r[2]) for r in res], {x: k for k, x in enumerate(seq)}
    for it in range(tries):
        a, b, c, d, e = draw[it]
        p = pairs[it % len(cases)]
        u, v = p[int(a * len(p))]
        if b < 0.65:
            x, hi = (v, pos[u]) if b < 0.5 else (u, pos[u] - 1)
            lo = max([pos[j] for j in deps[x]] + [-1]) + 1
            near = hi if b < 0.5 else None
        else:
            x, lo = u, pos[v]
            hi = min([pos[j] for j in after[u]] + [n]) - 1
            near = lo
        if lo > hi:
            continue
        k = near if near is not None and c < 0.5 else lo + int(d * (hi - lo + 1))
        px = pos[x]
        k0, k1, part = (k, px, [x] + seq[k:px]) if k < px else (px, k, seq[px + 1:k + 1] + [x])
        bar = now - math.log(e + 1e-12) * (SLACK[1] * (1 - it / tries) + 1)
        last, nxt = beside(seq, k0 - 1, -1), beside(seq, k1 + 1, 1)
        kept, t = [[[row[i] for i in part] for row in r] for r in res], 0.0
        for w, cs, r in zip(WEIGH, cases, res):
            heads(part, last, cs, r[0], r[1], r[2])
            tails(part, nxt, cs, r[3])
            t += w * max(r[0][i] + r[3][i] for i in part)
        logs = [[] for cs in cases]
        if t <= bar:
            here, reach = {q[i]: i for i in part}, max([pos[j] for i in part for j in after[i]] + [k1])
            for cs, r, log in zip(cases, res, logs):
                onward(seq, k1 + 1, [here.get(c, last[c]) for c in range(6)], reach, cs, r[0], r[1], r[2], log)
            t = sum(w * max(r[1]) for w, r in zip(WEIGH, res))
        if t > bar:
            for r, log in zip(res, logs):
                for i, x0, x1, x2 in log:
                    r[0][i], r[1][i], r[2][i] = x0, x1, x2
            for r, old in zip(res, kept):
                for row, vals in zip(r, old):
                    for i, y in zip(part, vals):
                        row[i] = y
            continue
        seq[k0:k1 + 1] = part
        now, taken = t, taken + 1
        here, reach = {q[i]: i for i in reversed(part)}, min([pos[j] for i in part for j in deps[i]] + [k0])
        for cs, r in zip(cases, res):
            backward(seq, k0 - 1, [here.get(c, nxt[c]) for c in range(6)], reach, cs, r[3])
        if taken % 8:
            for k, i in enumerate(part):
                pos[i] = k0 + k
        else:
            seq.sort(key=lambda x: res[0][0][x])
            pos = {x: k for k, x in enumerate(seq)}
        pairs = [blocked(r[1], r[2]) for r in res]
        if now < best[0]:
            best = (now, list(seq))
    return best[1], best[0]


def emit(g, T, ops):
    if not ORDERED:
        link(ops)
        thin(ops)
        ORDERED.extend([exchange(ops, favour(ops, TRIES[0])[0], TRIES[1])[0], [o["deps"] for o in ops]])
    order = ORDERED[0]
    for o, d in zip(ops, ORDERED[1]):
        o["deps"] = d
    queue = {"v": g.vector, "a": g.scalar, "p": g.tensor, "g": g, "s": g.sync}
    count, seen, dmas = {"v": 0, "a": 0, "p": 0, "g": 0}, {}, 0
    sent = 0
    for i in order:
        o = ops[i]
        if o["kind"] == "c":
            count[o["q"]] += 1
            o["sig"] = ("e" + o["q"], count[o["q"]])
        elif o["kind"] == "d":
            o["sig"] = ("dm%d" % dmas, 16)
            dmas += 1
    for i in order:
        o = ops[i]
        if o["kind"] == "x":
            continue
        need = {}
        for j in o["deps"]:
            if ops[j]["kind"] == "r":
                continue
            s, v = ops[j]["sig"]
            need[s] = max(need.get(s, 0), v)
        for s in sorted(need):
            if seen.get((o["q"], s), 0) < need[s]:
                queue[o["q"]].wait_ge(T.sem[s], need[s])
                seen[(o["q"], s)] = need[s]
        ins = o["fn"]()
        if o["kind"] == "r":
            sent += o["inc"]
        else:
            ins.then_inc(T.sem[o["sig"][0]], 16 if o["kind"] == "d" else 1)
    g.wait_ge(T.sem.sent, sent)
    for q in count:
        g.sync.wait_ge(T.sem["e" + q], count[q])
    for k in range(dmas):
        g.sync.wait_ge(T.sem["dm%d" % k], 16)


def plan(g, core, T, topo, rank, room):
    ops, top, turn = [], {"wf": 0, "wb": 0, "wi": 0, "wu": 0}, [None]
    wide = {"float32": 4, "int32": 4, "bfloat16": 2, "uint16": 2, "uint8": 1, X4: 4}

    def new(kind, n):
        lo, w = top[kind], (n + 15) // 16 * 16
        if turn[0] is not None:
            turn[0] += 1
            w = room[(kind, turn[0])] = max(room.get((kind, turn[0]), 0), w)
        top[kind] = lo + w
        return V(kind, lo, lo + n)

    def whole(name):
        return V(name, 0, SCRATCH[name][1][1])

    def ap(v):
        if len(v) == 2:
            return ap(v[0]).indirect(ap(v[1]))
        return T[v[0]][:, v[1]:v[2]:v[3]] if v[3] > 1 else T[v[0]][:, v[1]:v[2]]

    def sc(x):
        return ap(x) if isinstance(x, tuple) else x

    def add(q, kind, fn, r, w, cost, lat=0.0, after=(), **more):
        rr = []
        for v in r:
            if isinstance(v, tuple):
                rr += list(v) if len(v) == 2 else [v]
        cost *= HOLDS[2] if q + kind == "gc" else 1
        way = more.pop("way", int(len(rr) > sum(isinstance(v, tuple) for v in r)))
        costs = [cost * (1 if kind != "c" or q == "p" else s[way]) for s in SPEEDS]
        ops.append(dict(q=q, kind=kind, fn=fn, r=rr, w=list(w), cost=cost, costs=costs, lat=lat, after=list(after), **more))
        return len(ops) - 1

    def price(out, ins, two=False):
        n = size(out)
        if any(len(v) == 2 for v in ins):
            return 50 + 1.56 * CY * n
        half = all(wide[SCRATCH[v[0]][2]] == 2 for v in [out] + ins)
        if two:
            return CY * max(64, n if any(v[0] == "ps" for v in ins) else (TT2 if half and max(v[3] for v in [out] + ins) == 1 else 2) * n)
        return CY * max(64, n / 2 if half else n)

    def tt(out, a, b, op):
        add("v", "c", lambda: g.vector.tensor_tensor(ap(out), ap(a), ap(b), op), [a, b], [out], price(out, [a, b], True))

    def ts(out, a, s1, op0, s2=None, op1=None):
        if op1 is None:
            fn = lambda: g.vector.tensor_scalar(ap(out), ap(a), sc(s1), None, op0)
        else:
            fn = lambda: g.vector.tensor_scalar(ap(out), ap(a), sc(s1), sc(s2), op0, op1)
        add("v", "c", fn, [a, s1, s2], [out], price(out, [a]))

    def cp(out, a):
        add("v", "c", lambda: g.vector.tensor_copy(ap(out), ap(a)), [a], [out], price(out, [a]))

    def scatter(win, off, a):
        add("v", "c", lambda: g.vector.tensor_copy(ap((win, off)), ap(a)), [a, off], [win], 50 + 3.8 * CY * size(a), way=2)

    def scan(out, d0, d1, op0, op1, first=0.0):
        add("v", "c", lambda: g.vector.tensor_tensor_scan(ap(out), ap(d0), ap(d1), sc(first), op0, op1), [d0, d1, first], [out], price(out, [d0, d1]))

    def fill(out, k):
        add("v", "c", lambda: g.vector.memset(ap(out), k), [], [out], price(out, []))

    def act(out, a, f, bias=None, scale=None, acc=None):
        kw = {}
        if bias is not None:
            kw["bias"] = sc(bias)
        if scale is not None:
            kw["scale"] = sc(scale)
        if acc is not None:
            kw["accum_out"] = ap(acc)
        cost = 65 + 1.56 * CY * size(out) if len(a) == 2 else CY * max(64, size(out)) + (20 if acc else 0)
        add("a", "c", lambda: g.scalar.activation(ap(out), ap(a), f, **kw), [a, bias, scale], [out] + ([acc] if acc else []), cost)

    def move(who, out, a):
        if who == "v":
            cp(out, a)
        else:
            act(out, a, Fn.Copy)

    def iota(out, pattern, base=0, cm=0):
        if SCRATCH[out[0]][2] == "int32":
            fn = lambda: g.iota(ap(out), pattern, base, cm)
        else:
            fn = lambda: g.iota(ap(out), pattern, base, cm, allow_small_or_imprecise_dtypes=True)
        add("g", "c", fn, [], [out], 130 + 2 * CY * size(out))

    def keep(out, a, pattern, k=0.0, base=0):
        add("g", "c", lambda: g.affine_select(ap(out), ap(a), pattern, Op.not_equal, k, base, 0), [a], [out], 170 + 2 * CY * size(out))

    def quant(q, s, a):
        add("v", "c", lambda: g.vector.quantize_mx(ap(q), ap(s), ap(a)), [a], [q, s], 15 + 0.27 * size(a))

    def mm(bank, lq, ls, rq, rs):
        out = V("ps", 512 * bank, 512 * bank + size(rq))
        add("p", "c", lambda: g.tensor.matmul_mx(ap(out), ap(lq), ap(ls), ap(rq), ap(rs), True, True), [lq, ls, rq, rs], [out], 0.7 * (size(rq) + 16), lat=60)
        return out

    def dma(q, fn, r, w, lat):
        add(q, "d", fn, r, w, 60, lat)

    def twin(out, a, gate):
        dma("s", lambda: g.sync.dma_start(ap(out), ap(a)), [a, gate], [out], 3500)

    def heap(out, a, lat, after=()):
        add("g", "d", lambda: g.dma_start(ap(out), ap(a), accum_op=Op.add), [a, out], [out], HOLDS[1], lat, after)

    def u8(v):
        return ap(v).bitcast(dt.uint8)

    def mark(name):
        ops[-1]["mark"] = name

    rl = relays_of(T, topo, rank)
    ne = len(topo.engines(rl[0], T.cores[(rank + 1) % len(T.cores)]))

    def hand(dst, src, sem):
        rid, pid = topo.addr(rl[0], core)
        return add("g", "r", lambda: g.remote_dma(ap(dst), ap(src), T.sem[sem], T.sem.sent, pid, rid, topo.mask(core, rl[0])), [src], [], HOLDS[0],
                   inc=len(topo.engines(core, rl[0])))

    def both(dst, src, sem, f):
        every, n = topo.engines(core, rl[0]), size(dst)
        to = [topo.addr(c, core) for c in rl]
        fn = lambda: g.remote_dma_fused([RemoteDMATransfer(dst_ids=[DstId(rid=to[k][0], pnc=to[k][1])], dma_engine_mask=sum(1 << e for e in every[k::2]),
                                                           remote_sem=T.sem[sem], src=f(sub(src, k * n, k * n + n)), dst=f(dst)) for k in range(2)],
                                        local_sem=T.sem.sent)
        return add("g", "r", fn, [src], [], HOLDS[0] + 200, inc=len(every))

    def arrival(after, w, sem, v, lat):
        add("x", "x", None, [], w, 0.0, lat, after=after, sig=(sem, v))

    dma("s", lambda: g.sync.dma_start(T.pai[:], T.pa[:]), [], [whole("pai")], 2000)
    dma("a", lambda: g.scalar.dma_start(T.ub[:], T.u[:]), [], [whole("ub")], 2200)
    x1 = 4 * CHUNKS[0][1]
    dma("s", lambda: g.sync.dma_start(T.x0[:, 0:x1], T.x[:, 0:x1]), [], [V("x0", 0, x1)], 2600)
    dma("a", lambda: g.scalar.dma_start(T.x0[:, x1:4 * C], T.x[:, x1:4 * C]), [], [V("x0", x1, 4 * C)], 2900)
    dma("s", lambda: g.sync.dma_start(T.nri[:], T.nr[:]), [], [whole("nri")], 3000)
    gate = [V("x0", x1, 4 * C)]
    dma("s", lambda: g.sync.dma_start(T.wq[:].bitcast(dt.uint8), T.wc[:]), gate, [whole("wq")], 3000)
    dma("s", lambda: g.sync.dma_start(T.wsc[:], T.ws[:]), gate, [whole("wsc")], 2500)
    dma("s", lambda: g.sync.dma_start(T.vb[:], T.v[:]), [whole("wsc")], [whole("vb")], 3500)

    pi, cols, cf = new("wi", 1), new("wi", 4), new("wf", 17)
    iota(pi, [[1, 1]], 0, 1)
    ts(sub(cols, 0, 1), pi, 15, Op.bitwise_and)
    ts(sub(cols, 1, 2), pi, 2, Op.logical_shift_right, 3, Op.bitwise_and)
    ts(sub(cols, 2, 3), pi, 3, Op.bitwise_and)
    cp(sub(cf, 0, 3), sub(cols, 0, 3))
    q16, q4, qt, q16n, q4n, s16, s4p, s4y, qto, s16y, s4, qty, s4z, s16k, qtz, s16r, s16h = [sub(cf, k, k + 1) for k in range(17)]
    ts(sub(cf, 3, 5), sub(cf, 0, 2), 1.0, Op.add)
    ts(s16, q16, 15.0, Op.is_equal, 1.0 / HOLD, Op.max)
    ts(s16y, s16, 512.0, Op.mult)
    ts(s16k, s16, -512.0 * 1024.0, Op.mult)
    ts(s16r, q16, 15.0, Op.is_lt, HOLD - 1.0, Op.mult)
    ts(s16r, s16r, 1.0, Op.add, -1.0 / (512.0 * 1024.0), Op.mult)
    ts(s16h, s16, 1.0 / 512, Op.mult)
    ts(s4, q4, 3.0, Op.is_equal, 1.0 / HOLD, Op.max)
    ts(s4p, s4, 4.0, Op.mult)
    ts(s4y, s4, 2048.0, Op.mult)
    ts(s4z, s4, 1.0 / 1024, Op.mult)
    ts(qtz, qt, BELOW / 1024 + 0.01, Op.add)
    ts(qto, qt, 0.25, Op.add)
    ts(qty, qt, 1024.25, Op.add)
    jf, rr = new("wf", 416), new("wb", 32)
    r16, r4 = sub(rr, 0, 16), sub(rr, 16, 32)
    iota(r16, [[1, 16]])
    iota(r4, [[0, 4], [1, 4]])
    iota(jf, [[1, 416]])
    ones, zeros, lut64 = V("one", 0, 528), V("one", 768, 912), V("one", 704, 912)
    fill(V("one", 0, 768), 1.0)
    fill(zeros, 0.0)
    qoff = new("wu", 30)
    ts(qoff, sub(ones, 0, 30), q16, Op.mult)

    def const(out, k):
        keep(out, sub(ones, 0, size(out)), [[0, size(out)]], k)

    def spread(p, n, how):
        m, w = new(p[0], n), min(n, 16 * int(how[0], 16))
        act(sub(m, 0, w), (p, sub(qoff, 0, w // 16)), Fn.Copy)
        for who in how[1:]:
            hi = min(n, 2 * w)
            if who == "s":
                twin(sub(m, w, hi), sub(m, 0, hi - w), sub(m, 0, 16))
            else:
                move(who, sub(m, w, hi), sub(m, 0, hi - w))
            w = hi
        return m

    def hold(r, q, qn):
        a, b, m = new("wb", 16), new("wb", 16), new("wb", 16)
        ts(a, r, q, Op.not_equal)
        ts(b, r, qn, Op.is_equal, HOLD, Op.mult)
        tt(m, a, b, Op.max)
        return m
    p16, p4 = hold(r16, q16, q16n), hold(r4, q4, q4n)
    pdiag, w16, gt = new("wb", 16), new("wb", 16), new("wf", 256)
    ts(pdiag, r16, q16, Op.is_equal)
    ts(w16, r16, q16, Op.is_ge, -0.5, Op.add)
    act(sub(gt, 0, 256, 4), sub(zeros, 0, 64), Fn.Copy)
    most = 16 * max(sum(x) for y in SCALAR for x in y)
    m16, m4, diag, ws16 = [spread(p, n, how) for p, n, how in zip((p16, p4, pdiag, w16), (416, 480, 208, most), SPREAD)]
    ns16, big4 = new("wb", 208), new("wb", 128)
    keep(ns16, sub(ones, 0, 208), [[0, 13], [1, 16]])
    keep(big4, sub(zeros, 0, 128), [[0, 32], [1, 4]], BIG)
    ts(V("one", 528, 544), pdiag, KEEP, Op.mult, 1.0, Op.max)
    ts(V("one", 544, 560), pdiag, 1.0 / KEEP - 1.0, Op.mult, 1.0, Op.add)
    m16i, xi, xf, kh = new("wi", 16), new("wi", 16), new("wf", 16), new("wf", 4)
    iota(m16i, [[16, 16]])
    ts(xf, m16i, q16, Op.add)
    cp(xi, xf)
    ts(kh, sub(xf, 0, 4), 0.5, Op.add)
    add("g", "c", lambda: g.affine_select(T.eye[:], T.one[:, 0:528], [[1, 528]], Op.is_equal, 0.0, -3, -4), [ones], [whole("eye")], 170 + 2 * CY * 528)
    for b in range(4):
        quant(V("qe", 128 * b, 128 * b + 128), V("se", 128 * b, 128 * b + 128), V("eye", 3 - b, 515 - b))
    iota(whole("repi"), [[16, 8]])
    cp(whole("repu"), whole("repi"))
    quant(whole("qu"), whole("su"), whole("ub"))
    add("v", "c", lambda: g.vector.tensor_copy(T.qr[:, 0:128].bitcast(dt.uint32), T.qu[:, 0:128].bitcast(dt.uint32).indirect(T.repu[:, 0:8])),
        [whole("qu"), whole("repu")], [whole("qr")], 260)
    add("a", "c", lambda: g.scalar.activation(T.sr[:, 0:128], T.su[:, 0:128].indirect(T.repu[:, 0:8]), Fn.Copy),
        [whole("su"), whole("repu")], [whole("sr")], 275)
    quant(whole("qv"), whole("sv"), whole("vb"))
    qr, sr = whole("qr"), whole("sr")
    nru, nrf = new("wu", 32), new("wf", 32)
    cp(nru, whole("nri"))
    ts(nrf, whole("nri"), 512.0, Op.mult)

    def diagonals(h, lo, hi):
        a, o, first = new("wf", lo + hi), new("wu", lo + hi), new("wb", 16 * (lo + hi))
        for c0, c1, m in ((0, lo, 0), (lo, lo + hi, h // 16 - hi)):
            iota(sub(a, c0, c1), [[h + 16, c1 - c0]], c0 * h + 16 * m)
            iota(sub(first, 16 * c0, 16 * c1), [[16, c1 - c0], [0, 16]], 16 * m)
        ts(o, a, q16, Op.add)
        return o, first
    diags = {(h, x): diagonals(h, *x) for h, x in sorted(set([(NS[t] // 2, SCALAR[t][0]) for t in range(2)] + [(128, SCALAR[t][1]) for t in range(2)]))}

    def ranks(row, lst, h, share, out):
        k, (lo, hi) = h // 16, share
        at = lambda m: sub(lst, 16 * m + 15, 16 * m + 16)
        nv, na, w = k - lo - hi, lo + hi, h + 16
        fl, cnt = new("wb", 9 * 224), new("wb", 9 * 224)
        for i in range(nv):
            m = lo + i
            f = sub(fl, i * w, i * w + w)
            ts(sub(f, 0, 16 * m + 16), sub(row, 0, 16 * m + 16), at(m), Op.is_le)
            ts(sub(f, 16 * m + 16, w), sub(row, 16 * m, h), at(m), Op.is_lt)
            scan(sub(cnt, i * w, i * w + w), V("one", 528 - 16 * m, 528 - 16 * m + w), f, Op.mult, Op.add)
        ts(sub(out, lo, lo + nv), sub(cnt, w - 1, nv * w, w), 0.25, Op.add)
        sg, junk, acc = new("wb", na * h), new("wb", na * h), new("wf", 32)
        ib, ibs = new("wb", 128), new("wb", 128)
        ms = list(range(lo)) + list(range(k - hi, k))
        for a, m in enumerate(ms):
            act(sub(sg, a * h, a * h + h), row, Fn.Sign, bias=at(m), scale=-1.0)
        tt(sub(ib, 0, 16 * na), (sg, diags[(h, share)][0]), sub(ws16, 0, 16 * na), Op.is_gt)
        scan(sub(ibs, 0, 16 * na), diags[(h, share)][1], sub(ib, 0, 16 * na), Op.max, Op.add)
        for a, m in enumerate(ms):
            y, sums = sub(sg, a * h, a * h + h), []
            for c0, c1, sign, op in ((16 * m + 16, h, 1.0, Op.add), (0, 16 * m, -1.0, Op.subtract)):
                if c1 > c0:
                    sums += [sub(acc, 8 * len(sums) + a, 8 * len(sums) + a + 1), op]
                    act(sub(junk, a * h + c0, a * h + c1), sub(y, c0, c1), Fn.Relu, scale=sign, acc=sums[-2])
            ts(sub(out, m, m + 1), sub(ibs, 16 * a + 15, 16 * a + 16), *((sums[0], sums[1]) + tuple(sums[2:])))

    def near(t):
        n = NS[t]
        nu = sub(nru, 16 * t, 16 * t + 16)
        pk, krow, klst, junk, acc = new("wf", 256), new("wf", 256), new("wf", 16), new("wb", 512), new("wf", 16)
        act(krow, (sub(jf, 0, n), nu), Fn.Copy, scale=512.0)
        less, unit = new("wf", 256), 2.0 ** (-9 if SELECT[t] else -18)
        for i in range(4):
            act(sub(pk, 3 - i, 256, 4), sub(krow, i, 256, 4), Fn.Identity, bias=4096.0 if i and SELECT[t] else 0.0, scale=unit)
            if i < 3:
                act(sub(less, 2 - i, 256, 4), sub(krow, i, 256, 4), Fn.Copy, scale=-unit)
        if SELECT[t]:
            act(sub(less, 3, 256, 4), sub(jf, 0, 256, 4), Fn.Identity, bias=4096.0 * n - BELOW, scale=4096.0)
        else:
            act(sub(less, 3, 256, 4), sub(ones, 0, 64), Fn.Copy, scale=-0.5)
        heap(pk, less, 3500)
        mark("p%d" % t)
        heap(krow, sub(jf, 0, 256), 3500)
        tt(klst, sub(nrf, 16 * t, 16 * t + 16), xf, Op.add)
        nv = SORT[t]
        fl, cnt = new("wb", 256 * nv), new("wb", 256 * nv)
        for m in range(nv, 16):
            act(sub(junk, 256 * (m % 2), 256 * (m % 2) + 256), krow, Fn.Sign, bias=sub(klst, m, m + 1), scale=-1.0, acc=sub(acc, m, m + 1))
        ko, ks, kk, sh = new("wu", 16), new("wf", 272), new("wi", 48), new("wi", 48)
        for m in range(nv):
            ts(sub(fl, 256 * m, 256 * m + 256), krow, sub(klst, m, m + 1), Op.is_lt)
            scan(sub(cnt, 256 * m, 256 * m + 256), sub(ones, 0, 256), sub(fl, 256 * m, 256 * m + 256), Op.mult, Op.add)
        if nv:
            cp(sub(ko, 0, nv), sub(cnt, 255, 256 * nv, 256))
        ts(sub(ko, nv, 16), sub(acc, nv, 16), 0.5, Op.mult, 127.75, Op.add)
        mark("k%d" % t)
        const(sub(ks, 0, 8), -512.0)
        const(sub(ks, 264, 272), 600.0 * 512)
        scatter(sub(ks, 8, 264), ko, krow)
        for e, d in enumerate((-1, 0, 1)):
            hs = new("wf", 256)
            scan(hs, sub(m16, 0, 256), sub(ks, 8 + d, 264 + d), Op.mult, Op.add)
            ts(sub(sh, 16 * e, 16 * e + 16), sub(hs, 15, 256, 16), s16h, Op.mult, 256.0002, Op.add)
            if d == 0:
                ts(sub(kk, 16, 32), sub(hs, 15, 256, 16), s16, Op.mult)
        plc, ends, an, w = sub(sh, 16, 32), new("wi", 32), new("wi", 32), new("wi", 48)
        tt(ends, sub(sh, 0, 32), sub(sh, 16, 48), Op.not_equal)
        su, d1u, endo, endu = new("wu", 32), new("wu", 16), new("wu", 16), new("wu", 32)
        sigu, s3u = sub(su, 0, 16), sub(su, 16, 32)
        ts(sub(an, 0, 16), sub(kk, 16, 32), 255, Op.bitwise_and)
        ts(sub(an, 16, 32), sub(kk, 16, 32), 252, Op.bitwise_and)
        cp(su, an)
        mark("f%d" % t)
        tt(sub(w, 0, 16), plc, sub(ends, 0, 16), Op.mult)
        ts(d1u, sub(w, 0, 16), -240.0, Op.add, 15.0, Op.max)
        mark("f%d" % t)
        tt(sub(w, 16, 32), plc, sub(ends, 16, 32), Op.mult)
        tt(sub(w, 32, 48), sub(w, 16, 32), xi, Op.max)
        cp(endo, sub(w, 32, 48))
        mark("f%d" % t)
        a0, b0, b1, ew, hs = new("wf", 512), new("wb", 512), new("wb", 512), new("wf", n + 256), new("wf", n)
        if not SELECT[t]:
            act(sub(b1, 1, 512, 2), (jf, s3u), Fn.Identity, bias=(n - 256.0) / 512, scale=1.0 / 2048)
            mark("f%d" % t)
        twin(sub(ew, 256, 256 + n), sub(jf, 0, n), whole("vb"))
        for a in (0, 8):
            scatter(ew, sub(endo, a, a + 8), sub(odds, 16 * a, 16 * a + 128))
        scan(hs, sub(m16, 0, n), sub(ew, 256, 256 + n), Op.mult, Op.add)
        ts(sub(endu, 0, n // 16), sub(hs, 15, n, 16), s16, Op.mult, 528.25, Op.add)
        mark("e%d" % t)
        src = None
        if SELECT[t]:
            from1, froms, n4, step = new("wf", 512), new("wf", 528 + n), new("wu", 64), new("wf", 256)
            const(sub(froms, 512, 528), 0.0)
            iota(sub(froms, 528, 528 + n), [[4096, n]], -BELOW)
            iota(step, [[16385, 64], [4096, 4]], 4097 * n - BELOW)
            act(sub(from1, 1, 512, 2), (step, sigu), Fn.Copy)
            for e in range(4):
                ts(sub(n4, 16 * e, 16 * e + 16), V("nri", 16 * t, 16 * t + 16), 4.0, Op.mult, e + 0.25, Op.add)
            src = (from1, froms, n4)
        return nu, pk, sigu, s3u, d1u, endu, a0, b0, b1, src

    held = [new("wb", 528 + n) for n in NS[:2]]
    pars = [sub(held[t], 528, 528 + NS[t]) for t in range(2)] + [new("wb", NS[2])]
    ups = [[new("wb", n), new("wb", n), new("wb", n), new("wb", n)] for n in NS[:2]]
    odds = new("wf", 256)
    iota(odds, [[2, 256]], -527)
    nears = [near(t) for t in range(2)]
    a1, olds = new("wf", 512), [new("wu", n // 4) for n in NS[:2]]
    for t in range(2):
        const(sub(held[t], 512, 528), 1.0)
    act(sub(a1, 1, 512, 2), sub(ones, 0, 256), Fn.Copy, scale=0.0)
    base = dict(top)
    for t in range(2):
        top.update(base)
        turn[0] = 0
        n, n2, ch, ch2 = NS[t], NS[t + 1], CHUNKS[t], CHUNKS[t + 1]
        X, XH, XN = "x%d" % t, "xh%d" % t, "x%d" % (t + 1)
        nm = lambda s, lo, hi, step=1, t=t: V("%s%d" % (s, t), lo, hi, step)
        k, full = n // 16, FULL[t]
        par, nxt = pars[t], pars[t + 1]
        halves = lambda lo: ((lo, (lo + n + 32) // 64 * 32), ((lo + n + 32) // 64 * 32, n))
        lists = [new("wu", 32) for i in range(9)]
        low = [0 if t or i < LOW else 2 ** i for i in range(9)]
        cut = [halves(low[i])[0][1] if t == 0 else n // 2 for i in range(9)]
        part = lambda i, lo=0: [(a, b) for a, b in ((lo, cut[i]), (max(lo, cut[i]), n)) if a < b]

        def listed(i, a, b):
            pad = cut[i] // 16 % 2 if a >= cut[i] else 0
            return sub(lists[i], a // 16 + pad, b // 16 + pad)

        def to_list(i, hs):
            for a, b in part(i, low[i]):
                ts(listed(i, a, b), sub(hs, a + 15, b, 16), s16y, Op.mult, 256.25, Op.add)
                mark("u%d%d" % (t, i))
        up = ups[t]
        above = lambda row, b: sub(row, 0, n if t else b)
        if t == 0:
            cp(sub(lists[0], 0, k), whole("pai"))
            for a, b in part(0):
                if a or PAR0 == "a":
                    act(sub(par, a, b), (jf, listed(0, a, b)), Fn.Identity, bias=-0.5, scale=1.0 / 512)
                else:
                    ts(sub(par, a, b), (jf, listed(0, a, b)), 1.0 / 512, Op.mult, -0.5, Op.add)
        else:
            for a, b in part(0):
                scan(sub(up[3], a, b), sub(m16, a, b), sub(par, a, b), Op.mult, Op.add)
            to_list(0, up[3])
        for i in range(min(8, full)):
            lo2, hs, src, dst = low[i + 1], up[2 + i % 2], up[i % 2] if i else par, up[(i + 1) % 2]
            for a, b in part(i if t else i + 1, lo2):
                move("a" if a > lo2 else JUMPS[t][i], sub(dst, a, b), (above(src, b), listed(i, a, b)))
                scan(sub(hs, a, b), sub(m16, a, b), sub(dst, a, b), Op.mult, Op.add)
            if lo2 and i < min(8, full) - 1:
                act(sub(dst, 0, lo2), sub(ones, 0, lo2), Fn.Copy, scale=-0.5)
            to_list(i + 1, hs)
        far, fa, fb, fc = new("wu", 32), new("wf", 32), new("wf", 32), new("wf", 32)
        if full < 9:
            a, c0 = 2 ** full, 2 ** full // 16
            ts(sub(fa, c0, k), sub(up[2 + full % 2], a + 15, n, 16), s16y, Op.mult, 272.25 - 262144.0, Op.add)
            ts(sub(fb, c0, k), sub(fa, c0, k), s16r, Op.mult)
            tt(sub(fc, c0, k), sub(up[2 + (full + 1) % 2], a + 15, n, 16), sub(fb, c0, k), Op.add)
            ts(sub(far, c0, k), sub(fc, c0, k), s16k, Op.mult)
        s, s2 = new("wf", n), new("wf", n)
        for at, c in enumerate(READY[t]):
            a, b = ch[c], ch[c + 1]
            quant(nm("qx", a, b), nm("sx", a, b), V(X, 4 * a, 4 * b))
            mark("x%d%d" % (t, c))
            p = mm(4 + at % 2, qr, sr, nm("qx", a, b), nm("sx", a, b))
            p2 = mm(6 + at % 2, qr, sr, nm("qx", a, b), nm("sx", a, b)) if SCORES[t][c] == "v" else p
            move(SCORES[t][c], sub(s, a, b), p)
            act(sub(s2, a, b), p2, Fn.Copy)
        sends = [both(nm("rq", 0, n // 2), nm("qx", 0, n), "rc%d" % t, u8), both(nm("rs", 0, n // 2), nm("sx", 0, n), "rp%d" % t, ap)]
        arrival(sends, [nm("lq", 0, n), nm("ls", 0, n)], "aq%d" % t, 4 * ne, LAT[0])
        for j in range(0 if SELECT[t] else 4):
            ts(V(XH, j * n, j * n + n), V(X, j * n, j * n + n), 0.5, Op.mult)
            mark("h%d" % t)
        behind, other, dif, shallow, capped = new("wf", n + 16), new("wf", n), new("wf", n), new("wf", C), new("wf", C)
        cc = sub(behind, 16, n + 16)
        cb = [cc, other] if full % 2 and full < 9 else [other, cc]
        tw = [new("wf", n), new("wf", n)]
        if t == 0:
            const(sub(behind, 8, 16), 0.0)
        for a, b in part(0):
            tt(sub(dif, a, b), (above(s, b), listed(0, a, b)), sub(s2, a, b), Op.subtract)
            act(sub(cb[0], a, b), sub(dif, a, b), Fn.Abs)
        for a, b in part(0):
            act(sub(tw[0], a, b), sub(dif, a, b), Fn.Abs)
        for i in range(full):
            if low[i]:
                act(sub(cb[(i + 1) % 2], low[i - 1], low[i]), sub(cb[i % 2], low[i - 1], low[i]), Fn.Copy)
            for a, b in part(i, low[i]):
                tt(sub(cb[(i + 1) % 2], a, b), (above(cb[i % 2], b), listed(i, a, b)), sub(tw[i % 2], a, b), Op.max)
                mark("c%d%d" % (t, i))
            if i < full - 1:
                for a, b in part(i, low[i]):
                    a = max(a, low[i + 1])
                    if a < b:
                        act(sub(tw[(i + 1) % 2], a, b), sub(cb[(i + 1) % 2], a, b), Fn.Copy)
                        mark("t%d" % t)
        if full < 9:
            w = 2 ** full
            const(sub(behind, 0, 8), BIG)
            for a, b in part(full, w):
                tt(sub(capped, a, b), (sub(behind, 0, b + 16), sub(far, a // 16, b // 16)), sub(tw[(full - 1) % 2], a, b), Op.max)
            act(sub(capped, 0, w), sub(other, 0, w), Fn.Copy)
            act(sub(shallow, 0, w), sub(other, 0, w), Fn.Copy)
            for a, b in part(full, w):
                tt(sub(shallow, a, b), (sub(capped, 0, b), listed(full, a, b)), sub(other, a, b), Op.max)
            act(sub(cc, 0, w), sub(other, 0, w), Fn.Copy)
            for a in range(w, n, w):
                b = min(a + w, n)
                tt(sub(cc, a, b), (sub(cc if a > w else other, 0, a), listed(full, a, b)), sub(other, a, b), Op.max)
                mark("c%d%d" % (t, full))
        h, cs = n // 2, shallow if full < 9 else cc
        win, msk, lst, rk = new("wf", h), new("wf", h), new("wf", h), new("wu", 16)
        for a, b in halves(0):
            tt(sub(win, a // 2, b // 2), sub(cs, a, b, 2), sub(cs, a + 1, b, 2), Op.min)
            tt(sub(msk, a // 2, b // 2), sub(win, a // 2, b // 2), sub(diag, a // 2, b // 2), Op.mult)
            scan(sub(lst, a // 2, b // 2), sub(ns16, a // 2, b // 2), sub(msk, a // 2, b // 2), Op.mult, Op.add)
        ranks(win, lst, h, SCALAR[t][0], rk)
        flag, pre, fl, cnt, acc, ou = new("wb", h), new("wb", h), new("wb", 4 * h), new("wb", 2 * h), new("wf", 2), new("wu", 8)
        cp(sub(flag, 0, 96), (lut64, sub(rk, 0, 6)))
        act(sub(flag, 96, h), (lut64, sub(rk, 6, h // 16)), Fn.Copy)
        scan(pre, sub(ones, 0, h), flag, Op.mult, Op.add)
        w = h - 48
        for u in range(2):
            ts(sub(fl, u * w, u * w + w), sub(pre, 16 * u, 16 * u + w), sub(kh, u, u + 1), Op.is_lt)
            scan(sub(cnt, u * w, u * w + w), sub(ones, 0, w), sub(fl, u * w, u * w + w), Op.mult, Op.add, 16.0 * u)
            act(sub(fl, (2 + u) * w, (3 + u) * w), sub(pre, 32 + 16 * u, 32 + 16 * u + w), Fn.Sign, bias=sub(kh, 2 + u, 3 + u), scale=-1.0, acc=sub(acc, u, u + 1))
        ts(sub(ou, 0, 2), sub(cnt, w - 1, 2 * w, w), 2.0, Op.mult, 0.25, Op.add)
        for u in range(2):
            ts(sub(ou, 2 + u, 3 + u), sub(acc, u, u + 1), w + 64.25 + 32 * u, Op.add)
        c2, j2, rk2, srt, hs = new("wf", 128), new("wf", 128), new("wu", 8), new("wf", 128), new("wf", 64)
        msk, lst, odd = new("wf", 128), new("wf", 128), new("wf", n - 1)
        if t:
            keep(odd, sub(cs, 1, n), [[1, n - 1]], 0.0, 1)
        else:
            act(odd, sub(cs, 1, n), Fn.Copy)
        mark("o%d" % t)
        for e, row in enumerate((cs, odd)):
            tt(sub(msk, e, 128, 2), (row, sub(ou, 0, 4)), sub(diag, e, 128, 2), Op.mult)
            act(sub(c2, e, 128, 2), (row, sub(ou, 0, 4)), Fn.Copy)
        act(sub(j2, 0, 128, 2), (sub(jf, 0, n), sub(ou, 0, 4)), Fn.Copy)
        act(sub(j2, 1, 128, 2), sub(j2, 0, 128, 2), Fn.Identity, bias=sub(ones, 0, 1))
        scan(lst, sub(ns16, 0, 128), msk, Op.mult, Op.add)
        ranks(c2, lst, 128, SCALAR[t][1], rk2)
        scatter(srt, rk2, j2)
        scan(hs, sub(m4, 0, 64), sub(srt, 0, 64), Op.mult, Op.add)
        ts(nm("el", 0, 16), sub(hs, 3, 64, 4), s4p, Op.mult, qto, Op.add)
        sl = hand(nm("rl", 0, 16), nm("el", 0, 16), "rn%d" % t)
        arrival([sl], [nm("ll", 0, 16)], "an%d" % t, ne, LAT[1])
        if not SELECT[t]:
            twin(nm("xo", 0, 4 * n), V(XH, 0, 4 * n), nm("ll", 0, 16))
        for c in BY_DMA[t]:
            twin(V(XN, 4 * ch2[c], 4 * ch2[c + 1]), V(X, 4 * ch2[c], 4 * ch2[c + 1]), nm("ll", 0, 16))
        for b in range(4):
            p = mm(4 + b, V("qe", 128 * b, 128 * b + 128), V("se", 128 * b, 128 * b + 128), nm("lq", 0, n), nm("ls", 0, n))
            act(nm("dd", b, 4 * n, 4), p, Fn.Copy)
            mark("d%d" % t)
        nu, pk, sigu, s3u, d1u, endu, a0, b0, b1, src = nears[t]
        oh = new("wf", n)
        if SELECT[t]:
            from1, froms, n4 = src
            act(oh, par, Fn.Identity, bias=256.0, scale=512.0)
            heap(sub(froms, 528, 528 + n), oh, 2500)
            for j in range(4):
                act(nm("sm", j * n, j * n + n), (V(X, 0, 4 * n), sub(olds[t], j * n // 16, (j + 1) * n // 16)), Fn.Copy)
                mark("S%d" % t)
            heap(nm("sm", 0, 4 * n), V(X, 0, 4 * n), 2500, [sl])
            for e in range(4):
                act(nm("sm", 4 * n + e, 4 * n + 1024, 4), (V(X, 0, 4 * n), sub(n4, 16 * e, 16 * e + 16)), Fn.Copy)
                mark("N%d" % t)
        act(sub(a1, 0, 512, 2), (behind, d1u), Fn.Copy)
        mark("s%d" % t)
        vs = sub(held[t], 0, 512)
        if SELECT[t]:
            act(sub(from1, 0, 512, 2), (sub(froms, 512, 528 + n), d1u), Fn.Copy)
            act(sub(a0, 0, 512, 2), sub(from1, 0, 512, 2), Fn.Relu, bias=BIG, scale=BIG / 2 ** 20)
            act(sub(b0, 0, 512, 2), sub(from1, 0, 512, 2), Fn.Relu, bias=1.0, scale=2.0 ** -20)
        else:
            act(sub(b1, 0, 512, 2), (sub(held[t], 512, 528 + n), d1u), Fn.Copy)
            mark("s%d" % t)
            act(sub(a0, 0, 512, 2), sub(b1, 0, 512, 2), Fn.Relu, bias=-3 * BIG, scale=4 * BIG)
            ts(sub(b0, 0, 512, 2), sub(b1, 0, 512, 2), 0.75, Op.is_lt)
        sn = new("wf", 256)
        act(sn, (s, nu), Fn.Copy)
        mark("s%d" % t)
        cp(V(X, 4 * n, 4 * n + 128), (nm("dd", 0, 4 * n), nm("ll", 0, 8)))
        act(V(X, 4 * n + 128, 4 * n + 256), (nm("dd", 0, 4 * n), nm("ll", 8, 16)), Fn.Copy)
        quant(nm("qh", 0, 128), nm("sh", 0, 128), V(X, 4 * n - 256, 4 * n + 256))
        z = sub(mm(2, qr, sr, nm("qh", 0, 128), nm("sh", 0, 128)), 64, 128)
        if SELECT[t]:
            for j in range(16):
                move(FOUR[j], nm("hh", j, 1024, 16), V(X, 4 * n + j % 4, 4 * n2, 4))
            heap(nm("sm", 4 * n, 4 * n + 1024), nm("hh", 0, 1024), LAT[2] + 300)
        else:
            act(V(XH, 4 * n, 4 * n2), V(X, 4 * n, 4 * n2), Fn.Copy, scale=0.5)
            act(nm("xo", 4 * n, 4 * n2), V(X, 4 * n, 4 * n2), Fn.Copy, scale=0.5)
        d, gap, cost, gs, ga, mn = [new("wf", 256) for i in range(5)] + [sub(new("wf", 264), 5, 261)]
        best, pick = new("wf", 512), new("wf", n2)
        for i in range(4):
            tt(sub(d, i, 256, 4), sub(sn, i, 256, 4), z, Op.subtract)
            act(sub(gap, i, 256, 4), sub(d, i, 256, 4), Fn.Abs)
        for a in (0, 128):
            tt(sub(cost, a, a + 128), (cc, sub(nu, a // 16, a // 16 + 8)), sub(gap, a, a + 128), Op.max)
            scan(sub(mn, a, a + 128), sub(big4, 0, 128), sub(cost, a, a + 128), Op.add, Op.min)
        act(ga, (gap, sigu), Fn.Copy)
        runs = [(256 * j // SPLIT, 256 * (j + 1) // SPLIT) for j in range(SPLIT)]
        for a, b in runs:
            tt(sub(a0, 2 * a + 1, 2 * b, 2), (sub(mn, 3, 256), sub(s3u, a // 16, b // 16)), sub(ga, a, b), Op.max)
        for i in range(3):
            tt(sub(gt, 3 - i, 256, 4), sub(mn, i, 256, 4), sub(mn, 3, 256, 4), Op.is_gt)
        for a in (0, 128):
            scan(sub(gs, a, a + 128), sub(gt, a, a + 128), sub(pk, a, a + 128), Op.mult, Op.add)
        act(sub(pick if SELECT[t] else nxt, n, n2), sub(gs, 3, 256, 4), Fn.Copy)
        mark("n%d" % t)
        for a, b in runs:
            a, b = 2 * a, 2 * b
            scan(sub(best, a, b), sub(a0, a, b), sub(a1, a, b), Op.min, Op.max, sub(best, a - 1, a) if a else 0.0)
            tt(sub(b0, a + 1, b, 2), sub(best, a + 1, b, 2), sub(best, a, b, 2), Op.is_ge if SELECT[t] else Op.is_lt)
            if SELECT[t]:
                scan(sub(froms, a, b), sub(b0, a, b), sub(from1, a, b), Op.mult, Op.min, sub(froms, a - 1, a) if a else 0.0)
            else:
                scan(sub(vs, a, b), sub(b0, a, b), sub(b1, a, b), Op.add, Op.min, sub(vs, a - 1, a) if a else 0.0)
        yo, hs, hf = new("wu", n2 // 4), new("wb", n2), new("wf", n2)
        if t == 0 and SELECT[1] and not SELECT[0]:
            yo = olds[1]
        for c in range(3):
            a, b = ch2[c], min(ch2[c + 1], n)
            if SELECT[t]:
                move(PICKS[t][c], sub(pick, a, b), (sub(froms, 0, 528 + n), sub(endu, a // 16, b // 16)))
                scan(sub(hf, a, b), sub(m4, a, b), sub(pick, a, b), Op.mult, Op.add)
                if b == n:
                    scan(sub(hf, n, n2), sub(m4, n, n2), sub(gs, 3, 256, 4), Op.mult, Op.add)
                ts(sub(yo, a // 4, ch2[c + 1] // 4), sub(hf, a + 3, ch2[c + 1], 4), s4z, Op.mult, qtz, Op.add)
            else:
                move(PARENTS[t][c], sub(nxt, a, b), (sub(held[t], 0, 528 + n), sub(endu, a // 16, b // 16)))
                mark("m%d%d" % (t, c))
        for c, (a, b) in enumerate(() if SELECT[t] else ((0, ch2[1]), (ch2[1], n2))):
            scan(sub(hs, a, b), sub(m4, a, b), sub(nxt, a, b), Op.mult, Op.add)
            ts(sub(yo, a // 4, b // 4), sub(hs, a + 3, b, 4), s4y, Op.mult, qty, Op.add)
            mark("y%d%d" % (t, c))
        for c in range(3):
            a, b = ch2[c], ch2[c + 1]
            if SELECT[t]:
                mid = a + int((b - a) * SHARE[t][c]) // 8 * 8
                ts(nm("yt", 4 * a, 4 * mid), (nm("sm", 0, 4 * n + 1024), sub(yo, a // 4, mid // 4)), 0.5, Op.mult)
                act(nm("yt", 4 * mid, 4 * b), (nm("sm", 0, 4 * n + 1024), sub(yo, mid // 4, b // 4)), Fn.Copy, scale=0.5)
            else:
                tt(nm("yt", 4 * a, 4 * b), (V(XH, 0, 4 * n2), sub(yo, a // 4, b // 4)), nm("xo", 4 * a, 4 * b), Op.add)
                mark("b%d%d" % (t, c))
            quant(nm("qy", a, b), nm("sy", a, b), nm("yt", 4 * a, 4 * b))
            mark("q%d%d" % (t, c))
            for e in range(4):
                p = mm(4 * (c % 2) + e, V("wq", 128 * e, 128 * e + 128), V("wsc", 128 * e, 128 * e + 128), nm("qy", a, b), nm("sy", a, b))
                r = nm("ru", 4 * a + e, 4 * b, 4)
                act(r, p, Fn.Relu, scale=0.03125)
                mark("r%d%d" % (t, c))
                if c not in BY_DMA[t]:
                    tt(V(XN, 4 * a + e, 4 * b, 4), r, V(X, 4 * a + e, 4 * b, 4), Op.add)
            if c in BY_DMA[t]:
                heap(V(XN, 4 * a, 4 * b), nm("ru", 4 * a, 4 * b), LAT[2])

    col = new("wf", NS[2])
    act(col, pick, Fn.Identity, bias=WHOLE + BELOW / 4096, scale=1.0 / 4096)
    act(whole("osb"), col, Fn.Identity, bias=4096 * WHOLE + BELOW, scale=-4096.0)
    dma("s", lambda: g.sync.dma_start(T.op[:], T.wf[0:128:16, pick[1]:pick[2]]), [pick], [V("op", 0, 1)], 2000)
    add("g", "d", lambda: g.dma_start(T.op[:], T.osb[0:128:16, :], accum_op=Op.add), [whole("osb")], [V("op", 0, 1)], HOLDS[1], LAT[2] + 800)
    for c in range(len(CHUNKS[2]) - 1):
        a, b = CHUNKS[2][c], CHUNKS[2][c + 1]
        quant(V("qx2", a, b), V("sx2", a, b), V("x2", 4 * a, 4 * b))
        mark("x2%d" % c)
        p = mm(4 + c, whole("qv"), whole("sv"), V("qx2", a, b), V("sx2", a, b))
        move(LAST[c], V("ysb", a, b), p)
        dma("s", lambda a=a, b=b: g.sync.dma_start(T.oc[:, 4 * a:4 * b], T.qx2[:, a:b].bitcast(dt.uint8)), [V("qx2", a, b)], [], 2300)
        dma("s", lambda a=a, b=b: g.sync.dma_start(T.y[:, a:b], T.ysb[:, a:b]), [V("ysb", a, b)], [], 2300)
    for j in range(4):
        dma("s", lambda j=j: g.sync.dma_start(T.osc[4 * j:4 * j + 4, :], T.sx2[32 * j:32 * j + 4, :]), [whole("sx2")], [], 2000)
    return ops
